import numpy as np
import ml_dtypes


def mxq(x, axis, fmt="e4m3"):
    dtype, down = {"e4m3": (ml_dtypes.float8_e4m3fn, 7), "e5m2": (ml_dtypes.float8_e5m2, 14)}[fmt]
    v = np.moveaxis(np.asarray(x, np.float32).astype(ml_dtypes.bfloat16).astype(np.float64), axis, -1)
    blocks = v.reshape(v.shape[:-1] + (-1, 32))
    amax = np.abs(blocks).max(-1, keepdims=True)
    byte = np.maximum(np.where(amax > 0, np.frexp(amax)[1] - 1 + 127, 0) - down, 1)
    scale = np.exp2(byte - 127.0)
    codes = (blocks / scale).astype(np.float32).astype(dtype).astype(np.float64)
    return np.moveaxis((codes * scale).reshape(v.shape), -1, axis)


WIDE = False


def mx_kscale(k):
    if not WIDE:
        return np.ones(k)
    levels = np.array([10, -10, 5, -5, 0])
    if k % 512:
        return np.exp2(np.random.permutation(np.resize(levels, k // 32))).repeat(32)
    a = np.empty((k // 512, 16))
    for p in range(k // 512):
        a[p, :8] = np.random.permutation(np.resize(levels, 8))
        for g in range(8):
            far = levels[np.abs(levels - a[p, g]) >= 10]
            a[p, g + 8] = far[np.random.randint(len(far))]
    return np.exp2(a.ravel()).repeat(32)


BF16 = ml_dtypes.bfloat16


def bf(x):
    return np.asarray(x, np.float32).astype(BF16)


def f64(x):
    return np.asarray(x).astype(np.float64)

E4M3FN = np.array([(-1.0 if i & 128 else 1.0) * ((1.0 + (i & 7) / 8.0) * 2.0 ** (((i >> 3) & 15) - 7) if i & 120 else (i & 7) * 2.0 ** -9) for i in range(256)])


def e4m3fn_bytes(y):
    return np.clip(np.asarray(y, np.float64), -448.0, 448.0).astype(np.float32).astype(ml_dtypes.float8_e4m3fn).view(np.uint8)


def e4m3fn_values(b):
    return E4M3FN[b]


T, K, D, N, G = 1536, 2048, 1024, 512, 128


def setup_inputs():
    s, t = mx_kscale(K), mx_kscale(D)
    X = np.random.standard_normal((T, K)) * s
    R = np.random.standard_normal((N, D)) / t
    X_scale = (np.abs(X).reshape(T, K // G, G).max(axis=2) / 448.0).astype(np.float32)
    R_scale = (np.abs(R).reshape(N // G, G, D // G, G).max(axis=(1, 3)) / 448.0).astype(np.float32)
    return {"X_bytes": e4m3fn_bytes(X / np.repeat(f64(X_scale), G, axis=1)),
            "X_scale": X_scale,
            "B": bf(np.random.standard_normal((K, N)) / np.sqrt(K) / s[:, None]),
            "Q": bf(np.random.standard_normal((T, D)) * t),
            "v": bf(0.3 * np.random.standard_normal(D) * t),
            "R_bytes": e4m3fn_bytes(R / np.repeat(np.repeat(f64(R_scale), G, axis=0), G, axis=1)),
            "R_scale": R_scale,
            "g": bf(1.0 + 0.1 * np.random.standard_normal(N))}


def reference(X_bytes, X_scale, B, Q, v, R_bytes, R_scale, g):
    X = e4m3fn_values(X_bytes) * np.repeat(f64(X_scale), G, axis=1)
    R = e4m3fn_values(R_bytes) * np.repeat(np.repeat(f64(R_scale), G, axis=0), G, axis=1)
    C = f64(Q) + f64(v)
    pos = mxq(C, 1, "e4m3") @ mxq(R, 1, "e4m3").T
    bias = mxq(X, 1, "e4m3") @ mxq(f64(B), 0, "e4m3")
    return (pos / np.sqrt(D) + bias) * f64(g)

@@ -1,0 +1,314 @@
+from contextlib import ExitStack
+
+import concourse.mybir as mybir
+from concourse.masks import make_identity
+
+T, K, D, N, G = 1536, 2048, 1024, 512, 128
+P = 128
+NT = T // P
+KP = K // 512
+DP = D // 512
+NB = K // G
+RB = D // G
+RT = N // P
+S_BLOCKS = 8
+TURN_BANKS = 5
+WORK_BUFS = 5
+S_ROWS = (0, 1)
+ACC_BANKS = 3
+
+FLOPS = 2 * T * N * (K + D)
+
+F32 = mybir.dt.float32
+BF16 = mybir.dt.bfloat16
+U32 = mybir.dt.uint32
+U8 = mybir.dt.uint8
+FP8 = mybir.dt.float8_e4m3fn
+FP8X4 = mybir.dt.float8_e4m3fn_x4
+MULT = mybir.AluOpType.mult
+ADD = mybir.AluOpType.add
+COPY = mybir.ActivationFunctionType.Copy
+
+
+def tile_relative_offset_scores_d9_kernel(tc, X_bytes, X_scale, B, Q, v, R_bytes, R_scale, g, out):
+    nc = tc.nc
+    with ExitStack() as ctx:
+        keep = ctx.enter_context(tc.tile_pool(name="keep", bufs=1))
+        work = ctx.enter_context(tc.tile_pool(name="work", bufs=WORK_BUFS))
+        psum = ctx.enter_context(tc.psum_pool(name="psum", bufs=TURN_BANKS))
+
+        vrow = keep.tile([P, D], BF16, align_bytes=64)
+        nc.gpsimd.memset(vrow[:], 0.0)
+        ones = keep.tile([P, P], BF16, align_bytes=64)
+        nc.vector.memset(ones[:], 1.0)
+        ident = keep.tile([P, P], F32, align_bytes=64)
+        make_identity(nc, ident[:])
+
+        xs = keep.tile([P, NT * NB], F32, align_bytes=64)
+        rs = keep.tile([P, RT * RB], F32, align_bytes=64)
+        rs32 = keep.tile([P, RT * RB], F32, align_bytes=64)
+        rb = [keep.tile([P, D], U8, name=f"rb{t}", align_bytes=64) for t in range(RT)]
+        xb = [keep.tile([P, K], U8, name=f"xb{i}", align_bytes=64) for i in range(NT)]
+        qb = [keep.tile([P, D], BF16, name=f"qb{i}", align_bytes=64) for i in range(NT)]
+        br = [keep.tile([P, 4, N], BF16, name=f"br{c}", align_bytes=64) for c in range(KP)]
+        X_v = X_bytes.rearrange("(p i) k -> p i k", i=NT)
+        Q_v = Q.rearrange("(p i) k -> p i k", i=NT)
+        B_v = B.rearrange("(c p j) n -> c p j n", p=P, j=4)
+        O_v = out.rearrange("(p i) n -> p i n", i=NT)
+
+        def load_x(i):
+            nc.sync.dma_start(out=xb[i][:], in_=X_v[:, i, :])
+
+        def load_q(i):
+            nc.sync.dma_start(out=qb[i][:], in_=Q_v[:, i, :])
+
+        def load_r(t):
+            nc.sync.dma_start(out=rb[t][:], in_=R_bytes[P * t : P * t + P, :])
+
+        def load_b(c):
+            nc.sync.dma_start(out=br[c][:], in_=B_v[c])
+
+        nc.scalar.dma_start(out=rs[:], in_=R_scale.rearrange("a b -> (a b)").partition_broadcast(P))
+        nc.scalar.dma_start(out=vrow[0:1, :], in_=v.rearrange("(o k) -> o k", o=1))
+        nc.sync.dma_start(out=xs[:], in_=X_scale.rearrange("(p i) j -> p (i j)", i=NT))
+        load_x(0)
+        load_r(0)
+        load_r(1)
+        load_r(2)
+        load_r(3)
+        load_q(0)
+        load_b(0)
+        load_x(1)
+        load_b(1)
+        load_q(1)
+        load_b(2)
+        load_x(2)
+        load_b(3)
+        load_q(2)
+        load_x(3)
+        load_q(3)
+        load_x(4)
+        gbc = keep.tile([P, N], BF16, align_bytes=64)
+        nc.sync.dma_start(out=gbc[:], in_=g.partition_broadcast(P))
+        load_q(4)
+        load_x(5)
+        load_q(5)
+        load_x(6)
+        load_q(6)
+        load_x(7)
+        load_q(7)
+        load_x(8)
+        load_q(8)
+        load_x(9)
+        load_q(9)
+        load_x(10)
+        load_q(10)
+        load_x(11)
+        load_q(11)
+        ctx.enter_context(tc.manual_schedule())
+
+        vbc = keep.tile([P, D], BF16, align_bytes=64)
+        vbc_v = vbc[:].rearrange("r (u g p e) -> r g u p e", u=2, g=DP, e=2)
+        nc.vector.tensor_scalar(out=rs32[:], in0=rs[:], scalar1=1.0 / 32.0, scalar2=None, op0=MULT)
+        st = {}
+
+        def turn_bank(key):
+            bank = psum.tile([P, 2, 2, P], F32, name="bank", tag="turn")
+            st[key] = bank
+            return bank
+
+        def bc(h):
+            bank = turn_bank(("bc", h))
+            nc.tensor.matmul(bank[:].rearrange("p c u r -> p (c u r)"), lhsT=ones[:], rhs=vrow[:, 512 * h : 512 * h + 512],
+                             start=True, stop=True)
+
+        def bev(h):
+            bank = st.pop(("bc", h))
+            nc.scalar.copy(out=vbc_v[:, h],
+                           in_=bank[:].rearrange("p c u r -> p (c u r)").rearrange("r (p u e) -> r u p e", u=2, e=2))
+
+        rw_t = keep.tile([P, RT, D], BF16, align_bytes=64)
+        rg = keep.tile([P, DP, N, 4], BF16, align_bytes=64)
+        rgw = rg[:].rearrange("p c n t -> p (c n t)").bitcast(F32).rearrange("p (c n u) -> p c n u", c=DP, u=2)
+        rc = keep.tile([P, DP, N], U32, align_bytes=64)
+        rsc = keep.tile([P, DP, N], U8, align_bytes=64)
+
+        def v_widen(out_tile, in_ap, scale, blk):
+            c, q = blk // 4, blk % 4
+            dst = out_tile.rearrange("r (c u p e) -> r c p u e", u=2, p=P, e=2)
+            nc.vector.tensor_scalar(
+                out=dst[:, c, 32 * q : 32 * q + 32],
+                in0=in_ap[:, G * blk : G * blk + G].bitcast(FP8).rearrange("r (p u e) -> r p u e", u=2, e=2),
+                scalar1=scale, scalar2=None, op0=MULT)
+
+        def s_widen(out_tile, in_ap, scale, blk):
+            nc.scalar.activation(out=out_tile[:, G * blk : G * blk + G],
+                                 in_=in_ap[:, G * blk : G * blk + G].bitcast(FP8), func=COPY, scale=scale)
+
+        def rw(t):
+            for blk in range(RB):
+                (s_widen if t in S_ROWS else v_widen)(
+                    rw_t[:, t, :], rb[t][:], rs32[:, RB * t + blk : RB * t + blk + 1], blk)
+
+        def transposes(bank, words, first, natural):
+            for c in range(2):
+                for u in range(2):
+                    w = 256 * (first + c)
+                    src = words[:, w + u : w + 256 : 2] if natural else words[:, w + P * u : w + P * u + P]
+                    nc.tensor.transpose(bank[:, c, u, :], src, ident[:])
+
+        def rt(t):
+            transposes(turn_bank(("rt", t)), rw_t[:, t, :].bitcast(F32), 0, t in S_ROWS)
+
+        def re(t):
+            bank = st.pop(("rt", t))
+            nc.scalar.copy(out=rgw[:, :, P * t : P * t + P, :], in_=bank[:].rearrange("p c u r -> p c r u"))
+
+        def rz(c):
+            nc.vector.quantize_mx(out=rc[:, c, :].bitcast(FP8X4), scales=rsc[:, c, :],
+                                  in_=rg[:, c].rearrange("p n t -> p (n t)"))
+
+        b_grp = [keep.tile([P, N, 4], BF16, name=f"bg{c}", align_bytes=64) for c in range(KP)]
+        b_code = keep.tile([P, KP, N], U32, align_bytes=64)
+        b_scale = keep.tile([P, KP, N], U8, align_bytes=64)
+
+        def bg(c):
+            nc.vector.tensor_copy(out=b_grp[c][:], in_=br[c][:].rearrange("p j n -> p n j"))
+
+        def bz(c):
+            nc.vector.quantize_mx(out=b_code[:, c, :].bitcast(FP8X4), scales=b_scale[:, c, :],
+                                  in_=b_grp[c][:].rearrange("p n t -> p (n t)"))
+
+        xw = [None] * NT
+        cw = [None] * NT
+        xg = [None] * NT
+        cg = [None] * NT
+        codes = [None] * NT
+        acc = [None] * NT
+
+        def xw_tile(i):
+            if xw[i] is None:
+                t = work.tile([P, K], BF16, name="xw", align_bytes=64)
+                xw[i] = t
+
+        def ws(i):
+            xw_tile(i)
+            for blk in range(S_BLOCKS):
+                s_widen(xw[i][:], xb[i][:], xs[:, NB * i + blk : NB * i + blk + 1], blk)
+
+        def wv(i):
+            xw_tile(i)
+            for blk in range(S_BLOCKS, NB):
+                v_widen(xw[i][:], xb[i][:], xs[:, NB * i + blk : NB * i + blk + 1], blk)
+
+        def ad(i):
+            t = work.tile([P, D], BF16, name="cw", align_bytes=64)
+            cw[i] = t
+            nc.vector.tensor_tensor(
+                out=t[:].rearrange("r (u w e) -> r u w e", u=2, e=2),
+                in0=qb[i][:].rearrange("r (w u e) -> r u w e", u=2, e=2),
+                in1=vbc[:].rearrange("r (u w e) -> r u w e", u=2, e=2), op=ADD)
+
+        def tx0(i):
+            transposes(turn_bank(("x0", i)), xw[i][:].bitcast(F32), 0, S_BLOCKS >= 8)
+
+        def tx1(i):
+            transposes(turn_bank(("x1", i)), xw[i][:].bitcast(F32), 2, False)
+
+        def xg_words(i):
+            if xg[i] is None:
+                t = work.tile([P, KP, P, 4], BF16, name="xg", align_bytes=64)
+                xg[i] = t
+            return xg[i][:].rearrange("p c r t -> p (c r t)").bitcast(F32).rearrange("p (c r u) -> p c r u", c=KP, u=2)
+
+        def ex0(i):
+            bank = st.pop(("x0", i))
+            nc.scalar.copy(out=xg_words(i)[:, 0:2], in_=bank[:].rearrange("p c u r -> p c r u"))
+
+        def ex1(i):
+            bank = st.pop(("x1", i))
+            nc.scalar.copy(out=xg_words(i)[:, 2:4], in_=bank[:].rearrange("p c u r -> p c r u"))
+
+        def tq(i):
+            bank = turn_bank(("q", i))
+            words = cw[i][:].bitcast(F32)
+            for c in range(DP):
+                for u in range(2):
+                    w = 256 * u + P * c
+                    nc.tensor.transpose(bank[:, c, u, :], words[:, w : w + P], ident[:])
+
+        def eq(i):
+            bank = st.pop(("q", i))
+            t = work.tile([P, DP, P, 4], BF16, name="cg", align_bytes=64)
+            cg[i] = t
+            words = t[:].rearrange("p c r t -> p (c r t)").bitcast(F32).rearrange("p (c r u) -> p c r u", c=DP, u=2)
+            nc.scalar.copy(out=words, in_=bank[:].rearrange("p c u r -> p c r u"))
+
+        def zx(i):
+            xc = work.tile([P, KP, P], U32, align_bytes=64)
+            xsc = work.tile([P, KP, P], U8, align_bytes=64)
+            nc.vector.quantize_mx(out=xc[:].rearrange("p c r -> p (c r)").bitcast(FP8X4),
+                                  scales=xsc[:].rearrange("p c r -> p (c r)"),
+                                  in_=xg[i][:].rearrange("p c r t -> p (c r t)"))
+            st["zx", i] = (xc, xsc)
+
+        def zq(i):
+            cc = work.tile([P, DP, P], U32, align_bytes=64)
+            csc = work.tile([P, DP, P], U8, align_bytes=64)
+            nc.vector.quantize_mx(out=cc[:].rearrange("p c r -> p (c r)").bitcast(FP8X4),
+                                  scales=csc[:].rearrange("p c r -> p (c r)"),
+                                  in_=cg[i][:].rearrange("p c r t -> p (c r t)"))
+            st["zq", i] = (cc, csc)
+
+        def mq(i):
+            cc, csc = st.pop(("zq", i))
+            t = psum.tile([P, N], F32, name="acc", tag="acc", bufs=ACC_BANKS)
+            acc[i] = t
+            for c in range(DP):
+                nc.tensor.matmul_mx(out=t[:], lhsT=cc[:, c, :].bitcast(FP8X4), lhsT_scale=csc[:, c, :],
+                                    rhs=rc[:, c, :].bitcast(FP8X4), rhs_scale=rsc[:, c, :],
+                                    start=(c == 0), stop=False)
+
+        def mxp(i, c):
+            xc, xsc = st["zx", i]
+            nc.tensor.matmul_mx(out=acc[i][:], lhsT=xc[:, c, :].bitcast(FP8X4), lhsT_scale=xsc[:, c, :],
+                                rhs=b_code[:, c, :].bitcast(FP8X4), rhs_scale=b_scale[:, c, :],
+                                start=False, stop=(c == KP - 1))
+
+        def mx(i):
+            for c in range(KP):
+                mxp(i, c)
+
+        def m0(i):
+            mxp(i, 0)
+
+        def m1(i):
+            mxp(i, 1)
+
+        def m2(i):
+            mxp(i, 2)
+
+        def m3(i):
+            mxp(i, 3)
+
+        def fin(i):
+            o = work.tile([P, N], F32, align_bytes=64)
+            nc.vector.tensor_tensor(out=o[:], in0=acc[i][:], in1=gbc[:], op=MULT)
+            nc.sync.dma_start(out=O_v[:, i, :], in_=o[:])
+
+        ws(0); wv(0); rw(3); rw(1); bc(0); rw(2); bc(1); rt(3); bev(0); bg(0); bev(1); rt(1); rw(0); wv(1); rt(2)
+        re(3); ad(0); rt(0); re(2); ad(1); ws(1); tx1(0); bg(2); tq(0); re(1); bg(1); eq(0); tx0(0); re(0); bz(0)
+        ex1(0); tx1(1); rz(1); ex0(0); tq(1); zq(0); ws(4); rz(0); tx0(1); zx(0); ex1(1); ad(4); mq(0); ex0(1)
+        bz(1); eq(1); wv(4); m0(0); ws(2); tx0(4); ad(2); tq(4); zx(1); tx1(4); ex0(4); zq(1); m1(0); eq(4); ad(6)
+        mq(1); ex1(4); wv(6); m0(1); ws(6); tq(6); tq(2); zq(4); bg(3); mq(4); eq(2); tx1(6); ws(5); tx0(6); zx(4)
+        tx0(2); bz(2); ex0(2); m0(4); bz(3); m1(4); eq(6); m1(1); wv(5); m2(0); ex0(6); m2(1); m2(4); wv(2); ex1(6)
+        tx1(5); ws(11); m3(1); ad(5); m3(0); m3(4); ad(3); tx0(5); ex1(5); ad(7); tq(5); ex0(5); tx1(2); fin(0)
+        tx0(11); eq(5); zq(6); tq(7); fin(1); tq(3); zq(2); eq(3); mq(6); zx(6); ex1(2); mq(2); fin(4); ws(9); m0(6)
+        zx(2); m1(6); m2(6); ad(9); m3(6); m0(2); ws(3); zq(5); m1(2); wv(3); m2(2); mq(5); fin(6); m3(2); ex0(11)
+        tx0(9); wv(9); eq(7); tx0(3); zq(3); tx1(9); ex0(3); zx(5); tx1(3); tq(9); ad(8); ex1(3); m0(5); ex0(9)
+        m1(5); zx(3); mq(3); ex1(9); ad(10); m2(5); eq(9); m3(5); ad(11); m0(3); ws(10); m1(3); wv(11); tq(8)
+        tq(11); fin(2); tq(10); eq(11); tx1(11); zq(9); tx0(10); fin(5); ex1(11); zq(11); mq(9); eq(10); zx(11)
+        mq(11); ws(7); zx(9); m2(3); m0(11); wv(10); m1(11); ex0(10); m0(9); m3(3); wv(8); eq(8); m1(9); m2(11)
+        ws(8); m2(9); wv(7); m3(9); m3(11); zq(10); tx1(10); fin(3); tx1(8); ex1(10); tx0(7); zx(10); tx1(7); tx0(8)
+        ex1(7); fin(9); mq(10); ex0(7); zq(7); zq(8); m0(10); ex0(8); fin(11); m1(10); ex1(8); m2(10); zx(7); m3(10)
+        mq(7); zx(8); mq(8); fin(10); m0(7); m1(7); m2(7); m3(7); m0(8); fin(7); m1(8); m2(8); m3(8); fin(8)

@@ -11,11 +11,9 @@ DP = D // 512
 NB = K // G
 RB = D // G
 RT = N // P
-S_BLOCKS = 8
-TURN_BANKS = 5
-WORK_BUFS = 5
-S_ROWS = (0, 1)
-ACC_BANKS = 3
+TURN_BANKS = 6
+ACC_BANKS = 2
+WORK_BUFS = 4
 
 FLOPS = 2 * T * N * (K + D)
 
@@ -36,9 +34,10 @@ def tile_relative_offset_scores_d9_kernel(tc, X_bytes, X_scale, B, Q, v, R_bytes
         keep = ctx.enter_context(tc.tile_pool(name="keep", bufs=1))
         work = ctx.enter_context(tc.tile_pool(name="work", bufs=WORK_BUFS))
         psum = ctx.enter_context(tc.psum_pool(name="psum", bufs=TURN_BANKS))
+        ctx.enter_context(tc.manual_schedule())
 
         vrow = keep.tile([P, D], BF16, align_bytes=64)
-        nc.gpsimd.memset(vrow[:], 0.0)
+        nc.vector.memset(vrow[:], 0.0)
         ones = keep.tile([P, P], BF16, align_bytes=64)
         nc.vector.memset(ones[:], 1.0)
         ident = keep.tile([P, P], F32, align_bytes=64)
@@ -46,7 +45,8 @@ def tile_relative_offset_scores_d9_kernel(tc, X_bytes, X_scale, B, Q, v, R_bytes
 
         xs = keep.tile([P, NT * NB], F32, align_bytes=64)
         rs = keep.tile([P, RT * RB], F32, align_bytes=64)
-        rs32 = keep.tile([P, RT * RB], F32, align_bytes=64)
+        rsk = keep.tile([P, RT * DP], F32, align_bytes=64)
+        gbc = keep.tile([P, N], BF16, align_bytes=64)
         rb = [keep.tile([P, D], U8, name=f"rb{t}", align_bytes=64) for t in range(RT)]
         xb = [keep.tile([P, K], U8, name=f"xb{i}", align_bytes=64) for i in range(NT)]
         qb = [keep.tile([P, D], BF16, name=f"qb{i}", align_bytes=64) for i in range(NT)]
@@ -68,48 +68,26 @@ def tile_relative_offset_scores_d9_kernel(tc, X_bytes, X_scale, B, Q, v, R_bytes
         def load_b(c):
             nc.sync.dma_start(out=br[c][:], in_=B_v[c])
 
-        nc.scalar.dma_start(out=rs[:], in_=R_scale.rearrange("a b -> (a b)").partition_broadcast(P))
-        nc.scalar.dma_start(out=vrow[0:1, :], in_=v.rearrange("(o k) -> o k", o=1))
-        nc.sync.dma_start(out=xs[:], in_=X_scale.rearrange("(p i) j -> p (i j)", i=NT))
-        load_x(0)
-        load_r(0)
-        load_r(1)
-        load_r(2)
-        load_r(3)
-        load_q(0)
-        load_b(0)
-        load_x(1)
-        load_b(1)
-        load_q(1)
-        load_b(2)
-        load_x(2)
-        load_b(3)
-        load_q(2)
-        load_x(3)
-        load_q(3)
-        load_x(4)
-        gbc = keep.tile([P, N], BF16, align_bytes=64)
-        nc.sync.dma_start(out=gbc[:], in_=g.partition_broadcast(P))
-        load_q(4)
-        load_x(5)
-        load_q(5)
-        load_x(6)
-        load_q(6)
-        load_x(7)
-        load_q(7)
-        load_x(8)
-        load_q(8)
-        load_x(9)
-        load_q(9)
-        load_x(10)
-        load_q(10)
-        load_x(11)
-        load_q(11)
-        ctx.enter_context(tc.manual_schedule())
+        def load_xs():
+            nc.sync.dma_start(out=xs[:], in_=X_scale.rearrange("(p i) j -> p (i j)", i=NT))
 
-        vbc = keep.tile([P, D], BF16, align_bytes=64)
-        vbc_v = vbc[:].rearrange("r (u g p e) -> r g u p e", u=2, g=DP, e=2)
-        nc.vector.tensor_scalar(out=rs32[:], in0=rs[:], scalar1=1.0 / 32.0, scalar2=None, op0=MULT)
+        def load_rs():
+            nc.sync.dma_start(out=rs[:], in_=R_scale.rearrange("a b -> (a b)").partition_broadcast(P))
+
+        def load_v():
+            nc.sync.dma_start(out=vrow[0:1, :], in_=v.rearrange("(o k) -> o k", o=1))
+
+        def load_g():
+            nc.sync.dma_start(out=gbc[:], in_=g.partition_broadcast(P))
+
+        load_r(0); load_b(0); load_r(1); load_rs(); load_v(); load_r(2); load_r(3); load_xs()
+        load_x(0); load_b(1); load_q(0); load_b(2); load_x(1); load_b(3); load_q(1)
+        for i in range(2, NT):
+            load_x(i)
+            load_q(i)
+            if i == 3:
+                load_g()
+
         st = {}
 
         def turn_bank(key):
@@ -117,21 +95,29 @@ def tile_relative_offset_scores_d9_kernel(tc, X_bytes, X_scale, B, Q, v, R_bytes
             st[key] = bank
             return bank
 
-        def bc(h):
-            bank = turn_bank(("bc", h))
-            nc.tensor.matmul(bank[:].rearrange("p c u r -> p (c u r)"), lhsT=ones[:], rhs=vrow[:, 512 * h : 512 * h + 512],
-                             start=True, stop=True)
+        vbc = keep.tile([P, D], BF16, align_bytes=64)
 
-        def bev(h):
-            bank = st.pop(("bc", h))
-            nc.scalar.copy(out=vbc_v[:, h],
-                           in_=bank[:].rearrange("p c u r -> p (c u r)").rearrange("r (p u e) -> r u p e", u=2, e=2))
+        def bc():
+            bank = turn_bank("bc")
+            wide = bank[:].rearrange("p c u r -> p (c u r)").bitcast(BF16)
+            for h in range(DP):
+                nc.tensor.matmul(wide[:, 512 * h : 512 * h + 512], lhsT=ones[:], rhs=vrow[:, 512 * h : 512 * h + 512],
+                                 start=True, stop=True)
 
-        rw_t = keep.tile([P, RT, D], BF16, align_bytes=64)
-        rg = keep.tile([P, DP, N, 4], BF16, align_bytes=64)
-        rgw = rg[:].rearrange("p c n t -> p (c n t)").bitcast(F32).rearrange("p (c n u) -> p c n u", c=DP, u=2)
+        def bev():
+            bank = st.pop("bc")
+            nc.scalar.copy(out=vbc[:].bitcast(F32).rearrange("r (u w) -> r u w", u=2),
+                           in_=bank[:].rearrange("p c u r -> p (c u r)").rearrange("r (w u) -> r u w", u=2))
+
+        rw_t = [keep.tile([P, D], BF16, name=f"rw{t}", align_bytes=64) for t in range(RT)]
+        rg = [keep.tile([P, N, 4], BF16, name=f"rg{c}", align_bytes=64) for c in range(DP)]
         rc = keep.tile([P, DP, N], U32, align_bytes=64)
         rsc = keep.tile([P, DP, N], U8, align_bytes=64)
+
+        def rscale():
+            for q in range(4):
+                nc.gpsimd.tensor_scalar(out=rsk[32 * q : 32 * q + 32, :], in0=rs[32 * q : 32 * q + 32, q : RT * RB : 4],
+                                        scalar1=1.0 / 32.0, scalar2=None, op0=MULT)
 
         def v_widen(out_tile, in_ap, scale, blk):
             c, q = blk // 4, blk % 4
@@ -146,34 +132,52 @@ def tile_relative_offset_scores_d9_kernel(tc, X_bytes, X_scale, B, Q, v, R_bytes
                                  in_=in_ap[:, G * blk : G * blk + G].bitcast(FP8), func=COPY, scale=scale)
 
         def rw(t):
-            for blk in range(RB):
-                (s_widen if t in S_ROWS else v_widen)(
-                    rw_t[:, t, :], rb[t][:], rs32[:, RB * t + blk : RB * t + blk + 1], blk)
+            nc.scalar.copy(out=rw_t[t][:], in_=rb[t][:].bitcast(FP8))
+
+        def rwv(t):
+            nc.vector.tensor_copy(out=rw_t[t][:], in_=rb[t][:].bitcast(FP8))
 
         def transposes(bank, words, first, natural):
             for c in range(2):
                 for u in range(2):
                     w = 256 * (first + c)
-                    src = words[:, w + u : w + 256 : 2] if natural else words[:, w + P * u : w + P * u + P]
+                    src = words[:, w + u : w + 256 : 2] if first + c < natural else words[:, w + P * u : w + P * u + P]
                     nc.tensor.transpose(bank[:, c, u, :], src, ident[:])
 
         def rt(t):
-            transposes(turn_bank(("rt", t)), rw_t[:, t, :].bitcast(F32), 0, t in S_ROWS)
+            transposes(turn_bank(("rt", t)), rw_t[t][:].bitcast(F32), 0, DP)
 
         def re(t):
             bank = st.pop(("rt", t))
-            nc.scalar.copy(out=rgw[:, :, P * t : P * t + P, :], in_=bank[:].rearrange("p c u r -> p c r u"))
+            for c in range(DP):
+                nc.vector.tensor_scalar(
+                    out=rg[c][:, P * t : P * t + P, :].rearrange("p r (u e) -> p r u e", u=2),
+                    in0=bank[:, c].bitcast(BF16).rearrange("p u (r e) -> p r u e", e=2),
+                    scalar1=rsk[:, DP * t + c : DP * t + c + 1], scalar2=None, op0=MULT)
+
+        def res(t):
+            bank = st.pop(("rt", t))
+            for c in range(DP):
+                nc.scalar.activation(
+                    out=rg[c][:, P * t : P * t + P, :].rearrange("p r (u e) -> p r u e", u=2),
+                    in_=bank[:, c].bitcast(BF16).rearrange("p u (r e) -> p r u e", e=2),
+                    func=COPY, scale=rsk[:, DP * t + c : DP * t + c + 1])
 
         def rz(c):
             nc.vector.quantize_mx(out=rc[:, c, :].bitcast(FP8X4), scales=rsc[:, c, :],
-                                  in_=rg[:, c].rearrange("p n t -> p (n t)"))
+                                  in_=rg[c][:].rearrange("p n t -> p (n t)"))
 
         b_grp = [keep.tile([P, N, 4], BF16, name=f"bg{c}", align_bytes=64) for c in range(KP)]
         b_code = keep.tile([P, KP, N], U32, align_bytes=64)
         b_scale = keep.tile([P, KP, N], U8, align_bytes=64)
 
         def bg(c):
-            nc.vector.tensor_copy(out=b_grp[c][:], in_=br[c][:].rearrange("p j n -> p n j"))
+            nc.vector.tensor_copy(out=b_grp[c][:].rearrange("p (m i) t -> p m t i", i=4),
+                                  in_=br[c][:].rearrange("p t (m i) -> p m t i", i=4))
+
+        def bgs(c):
+            nc.scalar.copy(out=b_grp[c][:].rearrange("p (m i) t -> p m t i", i=4),
+                           in_=br[c][:].rearrange("p t (m i) -> p m t i", i=4))
 
         def bz(c):
             nc.vector.quantize_mx(out=b_code[:, c, :].bitcast(FP8X4), scales=b_scale[:, c, :],
@@ -182,9 +186,10 @@ def tile_relative_offset_scores_d9_kernel(tc, X_bytes, X_scale, B, Q, v, R_bytes
         xw = [None] * NT
         cw = [None] * NT
         xg = [None] * NT
-        cg = [None] * NT
-        codes = [None] * NT
         acc = [None] * NT
+
+        def s_passes(i):
+            return 4 if i < 1 else 2
 
         def xw_tile(i):
             if xw[i] is None:
@@ -193,12 +198,12 @@ def tile_relative_offset_scores_d9_kernel(tc, X_bytes, X_scale, B, Q, v, R_bytes
 
         def ws(i):
             xw_tile(i)
-            for blk in range(S_BLOCKS):
+            for blk in range(4 * s_passes(i)):
                 s_widen(xw[i][:], xb[i][:], xs[:, NB * i + blk : NB * i + blk + 1], blk)
 
         def wv(i):
             xw_tile(i)
-            for blk in range(S_BLOCKS, NB):
+            for blk in range(4 * s_passes(i), NB):
                 v_widen(xw[i][:], xb[i][:], xs[:, NB * i + blk : NB * i + blk + 1], blk)
 
         def ad(i):
@@ -210,10 +215,10 @@ def tile_relative_offset_scores_d9_kernel(tc, X_bytes, X_scale, B, Q, v, R_bytes
                 in1=vbc[:].rearrange("r (u w e) -> r u w e", u=2, e=2), op=ADD)
 
         def tx0(i):
-            transposes(turn_bank(("x0", i)), xw[i][:].bitcast(F32), 0, S_BLOCKS >= 8)
+            transposes(turn_bank(("x0", i)), xw[i][:].bitcast(F32), 0, s_passes(i))
 
         def tx1(i):
-            transposes(turn_bank(("x1", i)), xw[i][:].bitcast(F32), 2, False)
+            transposes(turn_bank(("x1", i)), xw[i][:].bitcast(F32), 2, s_passes(i))
 
         def xg_words(i):
             if xg[i] is None:
@@ -240,7 +245,7 @@ def tile_relative_offset_scores_d9_kernel(tc, X_bytes, X_scale, B, Q, v, R_bytes
         def eq(i):
             bank = st.pop(("q", i))
             t = work.tile([P, DP, P, 4], BF16, name="cg", align_bytes=64)
-            cg[i] = t
+            st["cg", i] = t
             words = t[:].rearrange("p c r t -> p (c r t)").bitcast(F32).rearrange("p (c r u) -> p c r u", c=DP, u=2)
             nc.scalar.copy(out=words, in_=bank[:].rearrange("p c u r -> p c r u"))
 
@@ -257,7 +262,7 @@ def tile_relative_offset_scores_d9_kernel(tc, X_bytes, X_scale, B, Q, v, R_bytes
             csc = work.tile([P, DP, P], U8, align_bytes=64)
             nc.vector.quantize_mx(out=cc[:].rearrange("p c r -> p (c r)").bitcast(FP8X4),
                                   scales=csc[:].rearrange("p c r -> p (c r)"),
-                                  in_=cg[i][:].rearrange("p c r t -> p (c r t)"))
+                                  in_=st.pop(("cg", i))[:].rearrange("p c r t -> p (c r t)"))
             st["zq", i] = (cc, csc)
 
         def mq(i):
@@ -269,46 +274,39 @@ def tile_relative_offset_scores_d9_kernel(tc, X_bytes, X_scale, B, Q, v, R_bytes
                                     rhs=rc[:, c, :].bitcast(FP8X4), rhs_scale=rsc[:, c, :],
                                     start=(c == 0), stop=False)
 
-        def mxp(i, c):
+        def mx(i, passes=range(KP)):
             xc, xsc = st["zx", i]
-            nc.tensor.matmul_mx(out=acc[i][:], lhsT=xc[:, c, :].bitcast(FP8X4), lhsT_scale=xsc[:, c, :],
-                                rhs=b_code[:, c, :].bitcast(FP8X4), rhs_scale=b_scale[:, c, :],
-                                start=False, stop=(c == KP - 1))
-
-        def mx(i):
-            for c in range(KP):
-                mxp(i, c)
-
-        def m0(i):
-            mxp(i, 0)
-
-        def m1(i):
-            mxp(i, 1)
-
-        def m2(i):
-            mxp(i, 2)
-
-        def m3(i):
-            mxp(i, 3)
+            for c in passes:
+                nc.tensor.matmul_mx(out=acc[i][:], lhsT=xc[:, c, :].bitcast(FP8X4), lhsT_scale=xsc[:, c, :],
+                                    rhs=b_code[:, c, :].bitcast(FP8X4), rhs_scale=b_scale[:, c, :],
+                                    start=False, stop=(c == KP - 1))
 
         def fin(i):
             o = work.tile([P, N], F32, align_bytes=64)
             nc.vector.tensor_tensor(out=o[:], in0=acc[i][:], in1=gbc[:], op=MULT)
             nc.sync.dma_start(out=O_v[:, i, :], in_=o[:])
 
-        ws(0); wv(0); rw(3); rw(1); bc(0); rw(2); bc(1); rt(3); bev(0); bg(0); bev(1); rt(1); rw(0); wv(1); rt(2)
-        re(3); ad(0); rt(0); re(2); ad(1); ws(1); tx1(0); bg(2); tq(0); re(1); bg(1); eq(0); tx0(0); re(0); bz(0)
-        ex1(0); tx1(1); rz(1); ex0(0); tq(1); zq(0); ws(4); rz(0); tx0(1); zx(0); ex1(1); ad(4); mq(0); ex0(1)
-        bz(1); eq(1); wv(4); m0(0); ws(2); tx0(4); ad(2); tq(4); zx(1); tx1(4); ex0(4); zq(1); m1(0); eq(4); ad(6)
-        mq(1); ex1(4); wv(6); m0(1); ws(6); tq(6); tq(2); zq(4); bg(3); mq(4); eq(2); tx1(6); ws(5); tx0(6); zx(4)
-        tx0(2); bz(2); ex0(2); m0(4); bz(3); m1(4); eq(6); m1(1); wv(5); m2(0); ex0(6); m2(1); m2(4); wv(2); ex1(6)
-        tx1(5); ws(11); m3(1); ad(5); m3(0); m3(4); ad(3); tx0(5); ex1(5); ad(7); tq(5); ex0(5); tx1(2); fin(0)
-        tx0(11); eq(5); zq(6); tq(7); fin(1); tq(3); zq(2); eq(3); mq(6); zx(6); ex1(2); mq(2); fin(4); ws(9); m0(6)
-        zx(2); m1(6); m2(6); ad(9); m3(6); m0(2); ws(3); zq(5); m1(2); wv(3); m2(2); mq(5); fin(6); m3(2); ex0(11)
-        tx0(9); wv(9); eq(7); tx0(3); zq(3); tx1(9); ex0(3); zx(5); tx1(3); tq(9); ad(8); ex1(3); m0(5); ex0(9)
-        m1(5); zx(3); mq(3); ex1(9); ad(10); m2(5); eq(9); m3(5); ad(11); m0(3); ws(10); m1(3); wv(11); tq(8)
-        tq(11); fin(2); tq(10); eq(11); tx1(11); zq(9); tx0(10); fin(5); ex1(11); zq(11); mq(9); eq(10); zx(11)
-        mq(11); ws(7); zx(9); m2(3); m0(11); wv(10); m1(11); ex0(10); m0(9); m3(3); wv(8); eq(8); m1(9); m2(11)
-        ws(8); m2(9); wv(7); m3(9); m3(11); zq(10); tx1(10); fin(3); tx1(8); ex1(10); tx0(7); zx(10); tx1(7); tx0(8)
-        ex1(7); fin(9); mq(10); ex0(7); zq(7); zq(8); m0(10); ex0(8); fin(11); m1(10); ex1(8); m2(10); zx(7); m3(10)
-        mq(7); zx(8); mq(8); fin(10); m0(7); m1(7); m2(7); m3(7); m0(8); fin(7); m1(8); m2(8); m3(8); fin(8)
+        rscale()
+        rw(0); bg(0); rw(1); bc(); rt(0); rw(2); rt(1); rw(3); bev(); bz(0); re(0); re(1); rt(2); rt(3); ws(0); wv(0); re(2); re(3)
+        bg(1); ad(0); rz(0); rz(1); tx0(0); tx1(0); tq(0); ex0(0); ex1(0); eq(0); bz(1); bg(2); ws(1); wv(1); ad(1); zx(0); zq(0); bz(2); bgs(3)
+        tx0(1); tx1(1); tq(1); mq(0); mx(0, range(3)); ex0(1); ex1(1); eq(1); bz(3); ws(2); wv(2); ad(2); mx(0, range(3, 4))
+        for s in range(2, NT + 1+1):
+            if s + 1 < NT:
+                ws(s + 1)
+                wv(s + 1)
+            if s < NT:
+                tq(s)
+                tx1(s)
+                tx0(s)
+                eq(s)
+                ex1(s)
+                ex0(s)
+            if s - 1 < NT:
+                zq(s - 1)
+                zx(s - 1)
+            if s + 1 < NT:
+                ad(s + 1)
+            if s - 1 < NT:
+                mq(s - 1)
+                mx(s - 1)
+            fin(s - 1 - 1)

@@ -80,8 +80,8 @@ def tile_relative_offset_scores_d9_kernel(tc, X_bytes, X_scale, B, Q, v, R_bytes
         def load_g():
             nc.sync.dma_start(out=gbc[:], in_=g.partition_broadcast(P))
 
-        load_r(0); load_b(0); load_r(1); load_rs(); load_v(); load_r(2); load_r(3); load_xs()
-        load_x(0); load_b(1); load_q(0); load_b(2); load_x(1); load_b(3); load_q(1)
+        load_r(0); load_xs(); load_x(0); load_r(1); load_b(0); load_rs(); load_v(); load_r(2)
+        load_b(1); load_r(3); load_x(1); load_q(0); load_b(2); load_q(1); load_b(3)
         for i in range(2, NT):
             load_x(i)
             load_q(i)
@@ -189,7 +189,7 @@ def tile_relative_offset_scores_d9_kernel(tc, X_bytes, X_scale, B, Q, v, R_bytes
         acc = [None] * NT
 
         def s_passes(i):
-            return 4 if i < 1 else 2
+            return 2
 
         def xw_tile(i):
             if xw[i] is None:
@@ -265,21 +265,49 @@ def tile_relative_offset_scores_d9_kernel(tc, X_bytes, X_scale, B, Q, v, R_bytes
                                   in_=st.pop(("cg", i))[:].rearrange("p c r t -> p (c r t)"))
             st["zq", i] = (cc, csc)
 
+        added = [0] * NT
+
+        def group_flags(i):
+            if added[i] == 0:
+                t = psum.tile([P, N], F32, name="acc", tag="acc", bufs=ACC_BANKS)
+                acc[i] = t
+            added[i] = added[i] + 1
+            return added[i] == 1, added[i] == KP + DP
+
         def mq(i):
             cc, csc = st.pop(("zq", i))
-            t = psum.tile([P, N], F32, name="acc", tag="acc", bufs=ACC_BANKS)
-            acc[i] = t
             for c in range(DP):
-                nc.tensor.matmul_mx(out=t[:], lhsT=cc[:, c, :].bitcast(FP8X4), lhsT_scale=csc[:, c, :],
+                first, last = group_flags(i)
+                nc.tensor.matmul_mx(out=acc[i][:], lhsT=cc[:, c, :].bitcast(FP8X4), lhsT_scale=csc[:, c, :],
                                     rhs=rc[:, c, :].bitcast(FP8X4), rhs_scale=rsc[:, c, :],
-                                    start=(c == 0), stop=False)
+                                    start=first, stop=last)
 
         def mx(i, passes=range(KP)):
             xc, xsc = st["zx", i]
             for c in passes:
+                first, last = group_flags(i)
                 nc.tensor.matmul_mx(out=acc[i][:], lhsT=xc[:, c, :].bitcast(FP8X4), lhsT_scale=xsc[:, c, :],
                                     rhs=b_code[:, c, :].bitcast(FP8X4), rhs_scale=b_scale[:, c, :],
-                                    start=False, stop=(c == KP - 1))
+                                    start=first, stop=last)
+
+        def last(i):
+            cc, csc = st.pop(("zq", i))
+            xc, xsc = st["zx", i]
+            pairs = [(cc, csc, rc, rsc, c) for c in range(DP)] + [(xc, xsc, b_code, b_scale, c) for c in range(KP)]
+            for h in range(2):
+                cols = slice(256 * h, 256 * h + 256)
+                half = turn_bank(("last", h))[:].rearrange("p c u r -> p (c u r)")[:, 0:256]
+                for j, (a, a_s, b, b_s, c) in enumerate(pairs):
+                    nc.tensor.matmul_mx(out=half, lhsT=a[:, c, :].bitcast(FP8X4), lhsT_scale=a_s[:, c, :],
+                                        rhs=b[:, c, cols].bitcast(FP8X4), rhs_scale=b_s[:, c, cols],
+                                        start=(j == 0), stop=(j == len(pairs) - 1))
+            fin(i - 1)
+            for h in range(2):
+                cols = slice(256 * h, 256 * h + 256)
+                half = st.pop(("last", h))[:].rearrange("p c u r -> p (c u r)")[:, 0:256]
+                o_half = work.tile([P, 256], F32, align_bytes=64)
+                nc.vector.tensor_tensor(out=o_half[:], in0=half, in1=gbc[:, cols], op=MULT)
+                nc.sync.dma_start(out=O_v[:, i, cols], in_=o_half[:])
 
         def fin(i):
             o = work.tile([P, N], F32, align_bytes=64)
@@ -287,26 +315,42 @@ def tile_relative_offset_scores_d9_kernel(tc, X_bytes, X_scale, B, Q, v, R_bytes
             nc.sync.dma_start(out=O_v[:, i, :], in_=o[:])
 
         rscale()
-        rw(0); bg(0); rw(1); bc(); rt(0); rw(2); rt(1); rw(3); bev(); bz(0); re(0); re(1); rt(2); rt(3); ws(0); wv(0); re(2); re(3)
-        bg(1); ad(0); rz(0); rz(1); tx0(0); tx1(0); tq(0); ex0(0); ex1(0); eq(0); bz(1); bg(2); ws(1); wv(1); ad(1); zx(0); zq(0); bz(2); bgs(3)
-        tx0(1); tx1(1); tq(1); mq(0); mx(0, range(3)); ex0(1); ex1(1); eq(1); bz(3); ws(2); wv(2); ad(2); mx(0, range(3, 4))
-        for s in range(2, NT + 1+1):
-            if s + 1 < NT:
-                ws(s + 1)
-                wv(s + 1)
-            if s < NT:
-                tq(s)
-                tx1(s)
-                tx0(s)
-                eq(s)
-                ex1(s)
-                ex0(s)
-            if s - 1 < NT:
-                zq(s - 1)
-                zx(s - 1)
-            if s + 1 < NT:
-                ad(s + 1)
-            if s - 1 < NT:
-                mq(s - 1)
-                mx(s - 1)
-            fin(s - 1 - 1)
+        rw(0); ws(0); wv(0); rwv(1); rt(0); tx1(0); tx0(0); bg(0); bc(); rt(1); ex1(0); rw(2); ex0(0); bz(0); re(0); bg(1); rw(3); bev(); zx(0); re(1)
+        rt(2); rt(3); mx(0, range(1)); ws(1); bz(1); wv(1); tx1(1); tx0(1); mx(0, range(1, 2)); bgs(2); re(2); re(3); ad(0); ex1(1); ex0(1); ws(2); tq(0); rz(0); eq(0); bgs(3); rz(1); zx(1); ad(1); bz(2); zq(0)
+        mx(1, range(2)); tq(1); mx(0, range(2, 3)); mx(1, range(2, 3)); mq(0); wv(2); ad(2); eq(1); bz(3); zq(1)
+        groups = [(i,) for i in range(10)] + [(10, 11)]
+        for n in range(2, len(groups) + 1):
+            ahead = groups[n + 1] if n + 1 < len(groups) else ()
+            here = groups[n] if n < len(groups) else ()
+            behind = groups[n - 1]
+            for i in ahead:
+                ws(i)
+            for i in here:
+                tq(i)
+                tx1(i)
+                tx0(i)
+            for i in here:
+                eq(i)
+                ex1(i)
+                ex0(i)
+            if n == 2:
+                mx(0, range(3, 4))
+                mx(1, range(3, 4))
+                mq(1)
+            else:
+                for i in behind:
+                    if i > behind[0]:
+                        fin(i - 2)
+                    zq(i)
+                    zx(i)
+                for i in behind:
+                    if i < NT - 1:
+                        mq(i)
+                        mx(i)
+            for j in range(max(1, len(ahead))):
+                if j < len(ahead):
+                    wv(ahead[j])
+                    ad(ahead[j])
+                if j == 0 and n < len(groups):
+                    fin(behind[-1] - 1)
+        last(NT - 1)

@@ -14,6 +14,7 @@ RT = N // P
 TURN_BANKS = 6
 ACC_BANKS = 2
 WORK_BUFS = 4
+RUN_PASS = 2
 
 FLOPS = 2 * T * N * (K + D)
 
@@ -36,16 +37,18 @@ def tile_relative_offset_scores_d9_kernel(tc, X_bytes, X_scale, B, Q, v, R_bytes
         psum = ctx.enter_context(tc.psum_pool(name="psum", bufs=TURN_BANKS))
         ctx.enter_context(tc.manual_schedule())
 
+        ones = keep.tile([P, P], BF16, align_bytes=64)
+        one = keep.tile([P, 1], F32, align_bytes=64)
+        nc.vector.memset(one[:], 1.0)
+        nc.scalar.activation(out=ones[:], in_=one[:].to_broadcast([P, P]), func=COPY)
         vrow = keep.tile([P, D], BF16, align_bytes=64)
         nc.vector.memset(vrow[:], 0.0)
-        ones = keep.tile([P, P], BF16, align_bytes=64)
-        nc.vector.memset(ones[:], 1.0)
         ident = keep.tile([P, P], F32, align_bytes=64)
         make_identity(nc, ident[:])
 
         xs = keep.tile([P, NT * NB], F32, align_bytes=64)
         rs = keep.tile([P, RT * RB], F32, align_bytes=64)
-        rsk = keep.tile([P, RT * DP], F32, align_bytes=64)
+        rs32 = keep.tile([P, RT * RB], F32, align_bytes=64)
         gbc = keep.tile([P, N], BF16, align_bytes=64)
         rb = [keep.tile([P, D], U8, name=f"rb{t}", align_bytes=64) for t in range(RT)]
         xb = [keep.tile([P, K], U8, name=f"xb{i}", align_bytes=64) for i in range(NT)]
@@ -65,8 +68,14 @@ def tile_relative_offset_scores_d9_kernel(tc, X_bytes, X_scale, B, Q, v, R_bytes
         def load_r(t):
             nc.sync.dma_start(out=rb[t][:], in_=R_bytes[P * t : P * t + P, :])
 
+        B_w = B.rearrange("(c h u j e) n -> c j h u (e n)", h=32, u=2, j=4, e=2)
+
         def load_b(c):
-            nc.sync.dma_start(out=br[c][:], in_=B_v[c])
+            if c < RUN_PASS:
+                nc.sync.dma_start(out=br[c][:], in_=B_v[c])
+            else:
+                for j in range(4):
+                    nc.sync.dma_start(out=br[c][j:P:4].rearrange("h (u e) n -> h u (e n)", u=2), in_=B_w[c, j])
 
         def load_xs():
             nc.sync.dma_start(out=xs[:], in_=X_scale.rearrange("(p i) j -> p (i j)", i=NT))
@@ -80,7 +89,7 @@ def tile_relative_offset_scores_d9_kernel(tc, X_bytes, X_scale, B, Q, v, R_bytes
         def load_g():
             nc.sync.dma_start(out=gbc[:], in_=g.partition_broadcast(P))
 
-        load_r(0); load_xs(); load_x(0); load_r(1); load_b(0); load_rs(); load_v(); load_r(2)
+        load_xs(); load_x(0); load_rs(); load_r(0); load_b(0); load_r(1); load_v(); load_r(2)
         load_b(1); load_r(3); load_x(1); load_q(0); load_b(2); load_q(1); load_b(3)
         for i in range(2, NT):
             load_x(i)
@@ -106,36 +115,36 @@ def tile_relative_offset_scores_d9_kernel(tc, X_bytes, X_scale, B, Q, v, R_bytes
 
         def bev():
             bank = st.pop("bc")
-            nc.scalar.copy(out=vbc[:].bitcast(F32).rearrange("r (u w) -> r u w", u=2),
-                           in_=bank[:].rearrange("p c u r -> p (c u r)").rearrange("r (w u) -> r u w", u=2))
+            nc.scalar.copy(out=vbc[:].bitcast(F32), in_=bank[:].rearrange("p c u r -> p (c u r)"))
 
         rw_t = [keep.tile([P, D], BF16, name=f"rw{t}", align_bytes=64) for t in range(RT)]
-        rg = [keep.tile([P, N, 4], BF16, name=f"rg{c}", align_bytes=64) for c in range(DP)]
+        rg = keep.tile([P, DP, N, 4], BF16, align_bytes=64)
+        rgw = rg[:].rearrange("p c n t -> p (c n t)").bitcast(F32).rearrange("p (c n u) -> p c n u", c=DP, u=2)
         rc = keep.tile([P, DP, N], U32, align_bytes=64)
         rsc = keep.tile([P, DP, N], U8, align_bytes=64)
 
         def rscale():
-            for q in range(4):
-                nc.gpsimd.tensor_scalar(out=rsk[32 * q : 32 * q + 32, :], in0=rs[32 * q : 32 * q + 32, q : RT * RB : 4],
-                                        scalar1=1.0 / 32.0, scalar2=None, op0=MULT)
+            nc.gpsimd.tensor_scalar(out=rs32[:], in0=rs[:], scalar1=1.0 / 32.0, scalar2=None, op0=MULT)
 
-        def v_widen(out_tile, in_ap, scale, blk):
+        def v_widen(out_tile, in_ap, scale, blk, first_run=RUN_PASS):
             c, q = blk // 4, blk % 4
-            dst = out_tile.rearrange("r (c u p e) -> r c p u e", u=2, p=P, e=2)
-            nc.vector.tensor_scalar(
-                out=dst[:, c, 32 * q : 32 * q + 32],
-                in0=in_ap[:, G * blk : G * blk + G].bitcast(FP8).rearrange("r (p u e) -> r p u e", u=2, e=2),
-                scalar1=scale, scalar2=None, op0=MULT)
+            if c >= first_run:
+                runs = out_tile.rearrange("r (c u h m) -> r c h u m", u=2, h=32, m=8)
+                nc.vector.tensor_scalar(
+                    out=runs[:, c, 8 * q : 8 * q + 8],
+                    in0=in_ap[:, G * blk : G * blk + G].bitcast(FP8).rearrange("r (h u m) -> r h u m", u=2, m=8),
+                    scalar1=scale, scalar2=None, op0=MULT)
+                return
+            nc.vector.tensor_scalar(out=out_tile[:, G * blk : G * blk + G], in0=in_ap[:, G * blk : G * blk + G].bitcast(FP8),
+                                    scalar1=scale, scalar2=None, op0=MULT)
 
         def s_widen(out_tile, in_ap, scale, blk):
             nc.scalar.activation(out=out_tile[:, G * blk : G * blk + G],
                                  in_=in_ap[:, G * blk : G * blk + G].bitcast(FP8), func=COPY, scale=scale)
 
         def rw(t):
-            nc.scalar.copy(out=rw_t[t][:], in_=rb[t][:].bitcast(FP8))
-
-        def rwv(t):
-            nc.vector.tensor_copy(out=rw_t[t][:], in_=rb[t][:].bitcast(FP8))
+            for blk in range(RB):
+                v_widen(rw_t[t][:], rb[t][:], rs32[:, RB * t + blk : RB * t + blk + 1], blk, 0)
 
         def transposes(bank, words, first, natural):
             for c in range(2):
@@ -145,27 +154,15 @@ def tile_relative_offset_scores_d9_kernel(tc, X_bytes, X_scale, B, Q, v, R_bytes
                     nc.tensor.transpose(bank[:, c, u, :], src, ident[:])
 
         def rt(t):
-            transposes(turn_bank(("rt", t)), rw_t[t][:].bitcast(F32), 0, DP)
+            transposes(turn_bank(("rt", t)), rw_t[t][:].bitcast(F32), 0, 0)
 
         def re(t):
             bank = st.pop(("rt", t))
-            for c in range(DP):
-                nc.vector.tensor_scalar(
-                    out=rg[c][:, P * t : P * t + P, :].rearrange("p r (u e) -> p r u e", u=2),
-                    in0=bank[:, c].bitcast(BF16).rearrange("p u (r e) -> p r u e", e=2),
-                    scalar1=rsk[:, DP * t + c : DP * t + c + 1], scalar2=None, op0=MULT)
-
-        def res(t):
-            bank = st.pop(("rt", t))
-            for c in range(DP):
-                nc.scalar.activation(
-                    out=rg[c][:, P * t : P * t + P, :].rearrange("p r (u e) -> p r u e", u=2),
-                    in_=bank[:, c].bitcast(BF16).rearrange("p u (r e) -> p r u e", e=2),
-                    func=COPY, scale=rsk[:, DP * t + c : DP * t + c + 1])
+            nc.scalar.copy(out=rgw[:, :, P * t : P * t + P, :], in_=bank[:].rearrange("p c u r -> p c r u"))
 
         def rz(c):
             nc.vector.quantize_mx(out=rc[:, c, :].bitcast(FP8X4), scales=rsc[:, c, :],
-                                  in_=rg[c][:].rearrange("p n t -> p (n t)"))
+                                  in_=rg[:, c].rearrange("p n t -> p (n t)"))
 
         b_grp = [keep.tile([P, N, 4], BF16, name=f"bg{c}", align_bytes=64) for c in range(KP)]
         b_code = keep.tile([P, KP, N], U32, align_bytes=64)
@@ -188,8 +185,8 @@ def tile_relative_offset_scores_d9_kernel(tc, X_bytes, X_scale, B, Q, v, R_bytes
         xg = [None] * NT
         acc = [None] * NT
 
-        def s_passes(i):
-            return 2
+        def s_blocks(i):
+            return 4 if i == 2 else 8
 
         def xw_tile(i):
             if xw[i] is None:
@@ -198,27 +195,27 @@ def tile_relative_offset_scores_d9_kernel(tc, X_bytes, X_scale, B, Q, v, R_bytes
 
         def ws(i):
             xw_tile(i)
-            for blk in range(4 * s_passes(i)):
+            for blk in range(s_blocks(i)):
                 s_widen(xw[i][:], xb[i][:], xs[:, NB * i + blk : NB * i + blk + 1], blk)
 
         def wv(i):
             xw_tile(i)
-            for blk in range(4 * s_passes(i), NB):
+            for blk in range(s_blocks(i), NB):
                 v_widen(xw[i][:], xb[i][:], xs[:, NB * i + blk : NB * i + blk + 1], blk)
 
         def ad(i):
             t = work.tile([P, D], BF16, name="cw", align_bytes=64)
             cw[i] = t
             nc.vector.tensor_tensor(
-                out=t[:].rearrange("r (u w e) -> r u w e", u=2, e=2),
-                in0=qb[i][:].rearrange("r (w u e) -> r u w e", u=2, e=2),
-                in1=vbc[:].rearrange("r (u w e) -> r u w e", u=2, e=2), op=ADD)
+                out=t[:].rearrange("r (u h m) -> r h u m", u=2, m=8),
+                in0=qb[i][:].rearrange("r (h u m) -> r h u m", u=2, m=8),
+                in1=vbc[:].rearrange("r (h u m) -> r h u m", u=2, m=8), op=ADD)
 
         def tx0(i):
-            transposes(turn_bank(("x0", i)), xw[i][:].bitcast(F32), 0, s_passes(i))
+            transposes(turn_bank(("x0", i)), xw[i][:].bitcast(F32), 0, RUN_PASS)
 
         def tx1(i):
-            transposes(turn_bank(("x1", i)), xw[i][:].bitcast(F32), 2, s_passes(i))
+            transposes(turn_bank(("x1", i)), xw[i][:].bitcast(F32), 2, RUN_PASS)
 
         def xg_words(i):
             if xg[i] is None:
@@ -315,10 +312,10 @@ def tile_relative_offset_scores_d9_kernel(tc, X_bytes, X_scale, B, Q, v, R_bytes
             nc.sync.dma_start(out=O_v[:, i, :], in_=o[:])
 
         rscale()
-        rw(0); ws(0); wv(0); rwv(1); rt(0); tx1(0); tx0(0); bg(0); bc(); rt(1); ex1(0); rw(2); ex0(0); bz(0); re(0); bg(1); rw(3); bev(); zx(0); re(1)
-        rt(2); rt(3); mx(0, range(1)); ws(1); bz(1); wv(1); tx1(1); tx0(1); mx(0, range(1, 2)); bgs(2); re(2); re(3); ad(0); ex1(1); ex0(1); ws(2); tq(0); rz(0); eq(0); bgs(3); rz(1); zx(1); ad(1); bz(2); zq(0)
-        mx(1, range(2)); tq(1); mx(0, range(2, 3)); mx(1, range(2, 3)); mq(0); wv(2); ad(2); eq(1); bz(3); zq(1)
-        groups = [(i,) for i in range(10)] + [(10, 11)]
+        ws(0); wv(0); tx1(0); tx0(0); rw(0); bg(0); rt(0); ex1(0); ex0(0); rw(1); bz(0); bc(); rt(1); re(0); rw(2); bev(); bgs(1); zx(0); rw(3); rt(2); rt(3); mx(0, range(1))
+        wv(1); ad(0); re(1); re(2); re(3); ws(1); tq(0); tx1(1); bz(1); bg(2); rz(0); rz(1); eq(0); tx0(1); mx(0, range(1, 2)); ad(1); bz(2); ex1(1); ex0(1); bgs(3); zq(0); tq(1); mq(0); mx(0, range(2, 3))
+        wv(2); zx(1); ad(2); mx(1, range(3)); eq(1); ws(2); bz(3); zq(1)
+        groups = [(i,) for i in range(NT)]
         for n in range(2, len(groups) + 1):
             ahead = groups[n + 1] if n + 1 < len(groups) else ()
             here = groups[n] if n < len(groups) else ()

@@ -14,6 +14,8 @@ RT = N // P
 TURN_BANKS = 6
 ACC_BANKS = 2
 WORK_BUFS = 4
+LOT_BUFS = 3
+LOTS = [(i, 1) for i in range(NT)]
 RUN_PASS = 2
 
 FLOPS = 2 * T * N * (K + D)
@@ -46,13 +48,25 @@ def tile_relative_offset_scores_d9_kernel(tc, X_bytes, X_scale, B, Q, v, R_bytes
         ident = keep.tile([P, P], F32, align_bytes=64)
         make_identity(nc, ident[:])
 
-        xs = keep.tile([P, NT * NB], F32, align_bytes=64)
+        xs = keep.tile([P, (NT - 1) * NB], F32, align_bytes=64)
         rs = keep.tile([P, RT * RB], F32, align_bytes=64)
         rs32 = keep.tile([P, RT * RB], F32, align_bytes=64)
         gbc = keep.tile([P, N], BF16, align_bytes=64)
         rb = [keep.tile([P, D], U8, name=f"rb{t}", align_bytes=64) for t in range(RT)]
-        xb = [keep.tile([P, K], U8, name=f"xb{i}", align_bytes=64) for i in range(NT)]
-        qb = [keep.tile([P, D], BF16, name=f"qb{i}", align_bytes=64) for i in range(NT)]
+        x_loads = [(1, 1), (2, 2), (4, 2), (6, 2), (8, 2), (10, 2)]
+        q_loads = [(0, 1), (1, 1), (2, 2), (4, 4), (8, 4)]
+        xb = {}
+        qb = {}
+        x_tile = {}
+        q_tile = {}
+        for lo, n in x_loads:
+            x_tile[lo] = keep.tile([P, n, K], U8, name=f"xb{lo}", align_bytes=64)
+            for i in range(n):
+                xb[lo + i] = x_tile[lo][:, i, :]
+        for lo, n in q_loads:
+            q_tile[lo] = keep.tile([P, n, D], BF16, name=f"qb{lo}", align_bytes=64)
+            for i in range(n):
+                qb[lo + i] = q_tile[lo][:, i, :]
         br = [keep.tile([P, 4, N], BF16, name=f"br{c}", align_bytes=64) for c in range(KP)]
         X_v = X_bytes.rearrange("(p i) k -> p i k", i=NT)
         Q_v = Q.rearrange("(p i) k -> p i k", i=NT)
@@ -60,10 +74,12 @@ def tile_relative_offset_scores_d9_kernel(tc, X_bytes, X_scale, B, Q, v, R_bytes
         O_v = out.rearrange("(p i) n -> p i n", i=NT)
 
         def load_x(i):
-            nc.sync.dma_start(out=xb[i][:], in_=X_v[:, i, :])
+            if i in x_tile:
+                nc.sync.dma_start(out=x_tile[i][:], in_=X_v[:, i : i + dict(x_loads)[i], :])
 
         def load_q(i):
-            nc.sync.dma_start(out=qb[i][:], in_=Q_v[:, i, :])
+            if i in q_tile:
+                nc.sync.dma_start(out=q_tile[i][:], in_=Q_v[:, i : i + dict(q_loads)[i], :])
 
         def load_r(t):
             nc.sync.dma_start(out=rb[t][:], in_=R_bytes[P * t : P * t + P, :])
@@ -77,8 +93,23 @@ def tile_relative_offset_scores_d9_kernel(tc, X_bytes, X_scale, B, Q, v, R_bytes
                 for j in range(4):
                     nc.sync.dma_start(out=br[c][j:P:4].rearrange("h (u e) n -> h u (e n)", u=2), in_=B_w[c, j])
 
+        xs_v = X_scale.rearrange("(p i) j -> p (i j)", i=NT)
+        xs_first = keep.tile([P, NB], F32, align_bytes=64)
+        x_first = [keep.tile([P, K // 2], U8, name=f"x_first{h}", align_bytes=64) for h in range(2)]
+
         def load_xs():
-            nc.sync.dma_start(out=xs[:], in_=X_scale.rearrange("(p i) j -> p (i j)", i=NT))
+            nc.sync.dma_start(out=xs[:], in_=xs_v[:, NB:])
+
+        def load_first():
+            nc.sync.dma_start(out=xs_first[:], in_=xs_v[:, 0:NB])
+            for h in (1, 0):
+                nc.sync.dma_start(out=x_first[h][:], in_=X_v[:, 0, K // 2 * h : K // 2 * h + K // 2])
+
+        def x_block(i, blk):
+            if i == 0:
+                half = NB // 2
+                return x_first[blk // half][:, G * (blk % half) : G * (blk % half) + G], xs_first[:, blk : blk + 1]
+            return xb[i][:, G * blk : G * blk + G], xs[:, NB * (i - 1) + blk : NB * (i - 1) + blk + 1]
 
         def load_rs():
             nc.sync.dma_start(out=rs[:], in_=R_scale.rearrange("a b -> (a b)").partition_broadcast(P))
@@ -89,8 +120,8 @@ def tile_relative_offset_scores_d9_kernel(tc, X_bytes, X_scale, B, Q, v, R_bytes
         def load_g():
             nc.sync.dma_start(out=gbc[:], in_=g.partition_broadcast(P))
 
-        load_xs(); load_x(0); load_rs(); load_r(0); load_b(0); load_r(1); load_v(); load_r(2)
-        load_b(1); load_r(3); load_x(1); load_q(0); load_b(2); load_q(1); load_b(3)
+        load_first(); load_rs(); load_r(0); load_b(0); load_r(1); load_v(); load_r(2)
+        load_b(1); load_r(3); load_xs(); load_x(1); load_q(0); load_b(2); load_q(1); load_b(3)
         for i in range(2, NT):
             load_x(i)
             load_q(i)
@@ -132,19 +163,19 @@ def tile_relative_offset_scores_d9_kernel(tc, X_bytes, X_scale, B, Q, v, R_bytes
                 runs = out_tile.rearrange("r (c u h m) -> r c h u m", u=2, h=32, m=8)
                 nc.vector.tensor_scalar(
                     out=runs[:, c, 8 * q : 8 * q + 8],
-                    in0=in_ap[:, G * blk : G * blk + G].bitcast(FP8).rearrange("r (h u m) -> r h u m", u=2, m=8),
+                    in0=in_ap.bitcast(FP8).rearrange("r (h u m) -> r h u m", u=2, m=8),
                     scalar1=scale, scalar2=None, op0=MULT)
                 return
-            nc.vector.tensor_scalar(out=out_tile[:, G * blk : G * blk + G], in0=in_ap[:, G * blk : G * blk + G].bitcast(FP8),
+            nc.vector.tensor_scalar(out=out_tile[:, G * blk : G * blk + G], in0=in_ap.bitcast(FP8),
                                     scalar1=scale, scalar2=None, op0=MULT)
 
         def s_widen(out_tile, in_ap, scale, blk):
             nc.scalar.activation(out=out_tile[:, G * blk : G * blk + G],
-                                 in_=in_ap[:, G * blk : G * blk + G].bitcast(FP8), func=COPY, scale=scale)
+                                 in_=in_ap.bitcast(FP8), func=COPY, scale=scale)
 
         def rw(t):
             for blk in range(RB):
-                v_widen(rw_t[t][:], rb[t][:], rs32[:, RB * t + blk : RB * t + blk + 1], blk, 0)
+                v_widen(rw_t[t][:], rb[t][:, G * blk : G * blk + G], rs32[:, RB * t + blk : RB * t + blk + 1], blk, 0)
 
         def transposes(bank, words, first, natural):
             for c in range(2):
@@ -182,7 +213,10 @@ def tile_relative_offset_scores_d9_kernel(tc, X_bytes, X_scale, B, Q, v, R_bytes
 
         xw = [None] * NT
         cw = [None] * NT
-        xg = [None] * NT
+        lot = {}
+        for lo, n in LOTS:
+            for i in range(lo, lo + n):
+                lot[i] = (lo, n)
         acc = [None] * NT
 
         def s_blocks(i):
@@ -196,19 +230,19 @@ def tile_relative_offset_scores_d9_kernel(tc, X_bytes, X_scale, B, Q, v, R_bytes
         def ws(i):
             xw_tile(i)
             for blk in range(s_blocks(i)):
-                s_widen(xw[i][:], xb[i][:], xs[:, NB * i + blk : NB * i + blk + 1], blk)
+                s_widen(xw[i][:], *x_block(i, blk), blk)
 
         def wv(i):
             xw_tile(i)
             for blk in range(s_blocks(i), NB):
-                v_widen(xw[i][:], xb[i][:], xs[:, NB * i + blk : NB * i + blk + 1], blk)
+                v_widen(xw[i][:], *x_block(i, blk), blk)
 
         def ad(i):
             t = work.tile([P, D], BF16, name="cw", align_bytes=64)
             cw[i] = t
             nc.vector.tensor_tensor(
                 out=t[:].rearrange("r (u h m) -> r h u m", u=2, m=8),
-                in0=qb[i][:].rearrange("r (h u m) -> r h u m", u=2, m=8),
+                in0=qb[i].rearrange("r (h u m) -> r h u m", u=2, m=8),
                 in1=vbc[:].rearrange("r (h u m) -> r h u m", u=2, m=8), op=ADD)
 
         def tx0(i):
@@ -218,14 +252,17 @@ def tile_relative_offset_scores_d9_kernel(tc, X_bytes, X_scale, B, Q, v, R_bytes
             transposes(turn_bank(("x1", i)), xw[i][:].bitcast(F32), 2, RUN_PASS)
 
         def xg_words(i):
-            if xg[i] is None:
-                t = work.tile([P, KP, P, 4], BF16, name="xg", align_bytes=64)
-                xg[i] = t
-            return xg[i][:].rearrange("p c r t -> p (c r t)").bitcast(F32).rearrange("p (c r u) -> p c r u", c=KP, u=2)
+            lo, n = lot[i]
+            if ("xg", lo) not in st:
+                st["xg", lo] = work.tile([P, n, KP, P, 4], BF16, name="xg", bufs=LOT_BUFS, align_bytes=64)
+            return st["xg", lo][:, i - lo].rearrange("p c r t -> p (c r t)").bitcast(F32).rearrange("p (c r u) -> p c r u", c=KP, u=2)
 
         def ex0(i):
             bank = st.pop(("x0", i))
-            nc.scalar.copy(out=xg_words(i)[:, 0:2], in_=bank[:].rearrange("p c u r -> p c r u"))
+            if i == NT - 1:
+                nc.vector.tensor_copy(out=xg_words(i)[:, 0:2], in_=bank[:].rearrange("p c u r -> p c r u"))
+            else:
+                nc.scalar.copy(out=xg_words(i)[:, 0:2], in_=bank[:].rearrange("p c u r -> p c r u"))
 
         def ex1(i):
             bank = st.pop(("x1", i))
@@ -241,26 +278,31 @@ def tile_relative_offset_scores_d9_kernel(tc, X_bytes, X_scale, B, Q, v, R_bytes
 
         def eq(i):
             bank = st.pop(("q", i))
-            t = work.tile([P, DP, P, 4], BF16, name="cg", align_bytes=64)
-            st["cg", i] = t
-            words = t[:].rearrange("p c r t -> p (c r t)").bitcast(F32).rearrange("p (c r u) -> p c r u", c=DP, u=2)
+            lo, n = lot[i]
+            if ("cg", lo) not in st:
+                st["cg", lo] = work.tile([P, n, DP, P, 4], BF16, name="cg", bufs=LOT_BUFS, align_bytes=64)
+            words = st["cg", lo][:, i - lo].rearrange("p c r t -> p (c r t)").bitcast(F32).rearrange("p (c r u) -> p c r u", c=DP, u=2)
             nc.scalar.copy(out=words, in_=bank[:].rearrange("p c u r -> p c r u"))
 
         def zx(i):
-            xc = work.tile([P, KP, P], U32, align_bytes=64)
-            xsc = work.tile([P, KP, P], U8, align_bytes=64)
-            nc.vector.quantize_mx(out=xc[:].rearrange("p c r -> p (c r)").bitcast(FP8X4),
-                                  scales=xsc[:].rearrange("p c r -> p (c r)"),
-                                  in_=xg[i][:].rearrange("p c r t -> p (c r t)"))
-            st["zx", i] = (xc, xsc)
+            lo, n = lot[i]
+            xc = work.tile([P, n, KP, P], U32, bufs=LOT_BUFS, align_bytes=64)
+            xsc = work.tile([P, n, KP, P], U8, bufs=LOT_BUFS, align_bytes=64)
+            nc.vector.quantize_mx(out=xc[:].rearrange("p n c r -> p (n c r)").bitcast(FP8X4),
+                                  scales=xsc[:].rearrange("p n c r -> p (n c r)"),
+                                  in_=st.pop(("xg", lo))[:].rearrange("p n c r t -> p (n c r t)"))
+            for j in range(n):
+                st["zx", lo + j] = (xc[:, j], xsc[:, j])
 
         def zq(i):
-            cc = work.tile([P, DP, P], U32, align_bytes=64)
-            csc = work.tile([P, DP, P], U8, align_bytes=64)
-            nc.vector.quantize_mx(out=cc[:].rearrange("p c r -> p (c r)").bitcast(FP8X4),
-                                  scales=csc[:].rearrange("p c r -> p (c r)"),
-                                  in_=st.pop(("cg", i))[:].rearrange("p c r t -> p (c r t)"))
-            st["zq", i] = (cc, csc)
+            lo, n = lot[i]
+            cc = work.tile([P, n, DP, P], U32, bufs=LOT_BUFS, align_bytes=64)
+            csc = work.tile([P, n, DP, P], U8, bufs=LOT_BUFS, align_bytes=64)
+            nc.vector.quantize_mx(out=cc[:].rearrange("p n c r -> p (n c r)").bitcast(FP8X4),
+                                  scales=csc[:].rearrange("p n c r -> p (n c r)"),
+                                  in_=st.pop(("cg", lo))[:].rearrange("p n c r t -> p (n c r t)"))
+            for j in range(n):
+                st["zq", lo + j] = (cc[:, j], csc[:, j])
 
         added = [0] * NT
 
@@ -307,7 +349,7 @@ def tile_relative_offset_scores_d9_kernel(tc, X_bytes, X_scale, B, Q, v, R_bytes
                 nc.sync.dma_start(out=O_v[:, i, cols], in_=o_half[:])
 
         def fin(i):
-            o = work.tile([P, N], F32, align_bytes=64)
+            o = work.tile([P, N], F32, bufs=NT, align_bytes=64)
             nc.vector.tensor_tensor(out=o[:], in0=acc[i][:], in1=gbc[:], op=MULT)
             nc.sync.dma_start(out=O_v[:, i, :], in_=o[:])
 
@@ -315,39 +357,32 @@ def tile_relative_offset_scores_d9_kernel(tc, X_bytes, X_scale, B, Q, v, R_bytes
         ws(0); wv(0); tx1(0); tx0(0); rw(0); bg(0); rt(0); ex1(0); ex0(0); rw(1); bz(0); bc(); rt(1); re(0); rw(2); bev(); bgs(1); zx(0); rw(3); rt(2); rt(3); mx(0, range(1))
         wv(1); ad(0); re(1); re(2); re(3); ws(1); tq(0); tx1(1); bz(1); bg(2); rz(0); rz(1); eq(0); tx0(1); mx(0, range(1, 2)); ad(1); bz(2); ex1(1); ex0(1); bgs(3); zq(0); tq(1); mq(0); mx(0, range(2, 3))
         wv(2); zx(1); ad(2); mx(1, range(3)); eq(1); ws(2); bz(3); zq(1)
-        groups = [(i,) for i in range(NT)]
-        for n in range(2, len(groups) + 1):
-            ahead = groups[n + 1] if n + 1 < len(groups) else ()
-            here = groups[n] if n < len(groups) else ()
-            behind = groups[n - 1]
-            for i in ahead:
-                ws(i)
-            for i in here:
-                tq(i)
-                tx1(i)
-                tx0(i)
-            for i in here:
-                eq(i)
-                ex1(i)
-                ex0(i)
-            if n == 2:
+        for s in range(2, NT + 1):
+            if s + 1 < NT:
+                ws(s + 1)
+            if s < NT:
+                tq(s)
+                tx1(s)
+                tx0(s)
+                ex1(s)
+                eq(s)
+                if s < NT - 1:
+                    ex0(s)
+            if s == 2:
                 mx(0, range(3, 4))
                 mx(1, range(3, 4))
                 mq(1)
             else:
-                for i in behind:
-                    if i > behind[0]:
-                        fin(i - 2)
-                    zq(i)
-                    zx(i)
-                for i in behind:
-                    if i < NT - 1:
-                        mq(i)
-                        mx(i)
-            for j in range(max(1, len(ahead))):
-                if j < len(ahead):
-                    wv(ahead[j])
-                    ad(ahead[j])
-                if j == 0 and n < len(groups):
-                    fin(behind[-1] - 1)
+                zq(s - 1)
+                zx(s - 1)
+                if s < NT:
+                    mq(s - 1)
+                    mx(s - 1)
+            if s + 1 < NT:
+                wv(s + 1)
+                ad(s + 1)
+            if s == NT - 1:
+                ex0(s)
+            if s < NT:
+                fin(s - 2)
         last(NT - 1)

@@ -157,13 +157,20 @@ def tile_relative_offset_scores_d9_kernel(tc, X_bytes, X_scale, B, Q, v, R_bytes
         def rscale():
             nc.gpsimd.tensor_scalar(out=rs32[:], in0=rs[:], scalar1=1.0 / 32.0, scalar2=None, op0=MULT)
 
-        def v_widen(out_tile, in_ap, scale, blk, first_run=RUN_PASS):
+        def v_widen(out_tile, in_ap, scale, blk, first_run=RUN_PASS, natural=RUN_PASS):
             c, q = blk // 4, blk % 4
             if c >= first_run:
                 runs = out_tile.rearrange("r (c u h m) -> r c h u m", u=2, h=32, m=8)
                 nc.vector.tensor_scalar(
                     out=runs[:, c, 8 * q : 8 * q + 8],
                     in0=in_ap.bitcast(FP8).rearrange("r (h u m) -> r h u m", u=2, m=8),
+                    scalar1=scale, scalar2=None, op0=MULT)
+                return
+            if c >= natural:
+                dst = out_tile.rearrange("r (c u p e) -> r c p u e", u=2, p=P, e=2)
+                nc.vector.tensor_scalar(
+                    out=dst[:, c, 32 * q : 32 * q + 32],
+                    in0=in_ap.bitcast(FP8).rearrange("r (p u e) -> r p u e", u=2, e=2),
                     scalar1=scale, scalar2=None, op0=MULT)
                 return
             nc.vector.tensor_scalar(out=out_tile[:, G * blk : G * blk + G], in0=in_ap.bitcast(FP8),
@@ -220,7 +227,7 @@ def tile_relative_offset_scores_d9_kernel(tc, X_bytes, X_scale, B, Q, v, R_bytes
         acc = [None] * NT
 
         def s_blocks(i):
-            return 4 if i == 2 else 8
+            return 4 if i % 3 == 2 else 8
 
         def xw_tile(i):
             if xw[i] is None:
@@ -235,7 +242,7 @@ def tile_relative_offset_scores_d9_kernel(tc, X_bytes, X_scale, B, Q, v, R_bytes
         def wv(i):
             xw_tile(i)
             for blk in range(s_blocks(i), NB):
-                v_widen(xw[i][:], *x_block(i, blk), blk)
+                v_widen(xw[i][:], *x_block(i, blk), blk, RUN_PASS, (s_blocks(i) + 3) // 4)
 
         def ad(i):
             t = work.tile([P, D], BF16, name="cw", align_bytes=64)
@@ -246,7 +253,7 @@ def tile_relative_offset_scores_d9_kernel(tc, X_bytes, X_scale, B, Q, v, R_bytes
                 in1=vbc[:].rearrange("r (h u m) -> r h u m", u=2, m=8), op=ADD)
 
         def tx0(i):
-            transposes(turn_bank(("x0", i)), xw[i][:].bitcast(F32), 0, RUN_PASS)
+            transposes(turn_bank(("x0", i)), xw[i][:].bitcast(F32), 0, (s_blocks(i) + 3) // 4)
 
         def tx1(i):
             transposes(turn_bank(("x1", i)), xw[i][:].bitcast(F32), 2, RUN_PASS)
@@ -259,10 +266,7 @@ def tile_relative_offset_scores_d9_kernel(tc, X_bytes, X_scale, B, Q, v, R_bytes
 
         def ex0(i):
             bank = st.pop(("x0", i))
-            if i == NT - 1:
-                nc.vector.tensor_copy(out=xg_words(i)[:, 0:2], in_=bank[:].rearrange("p c u r -> p c r u"))
-            else:
-                nc.scalar.copy(out=xg_words(i)[:, 0:2], in_=bank[:].rearrange("p c u r -> p c r u"))
+            nc.scalar.copy(out=xg_words(i)[:, 0:2], in_=bank[:].rearrange("p c u r -> p c r u"))
 
         def ex1(i):
             bank = st.pop(("x1", i))
@@ -366,23 +370,23 @@ def tile_relative_offset_scores_d9_kernel(tc, X_bytes, X_scale, B, Q, v, R_bytes
                 tx0(s)
                 ex1(s)
                 eq(s)
-                if s < NT - 1:
-                    ex0(s)
+                ex0(s)
             if s == 2:
                 mx(0, range(3, 4))
                 mx(1, range(3, 4))
+            elif s == 3:
                 mq(1)
             else:
-                zq(s - 1)
-                zx(s - 1)
-                if s < NT:
-                    mq(s - 1)
-                    mx(s - 1)
+                mq(s - 2)
+                mx(s - 2)
             if s + 1 < NT:
                 wv(s + 1)
+            if s + 1 < NT:
                 ad(s + 1)
-            if s == NT - 1:
-                ex0(s)
-            if s < NT:
-                fin(s - 2)
+            if 2 < s <= NT:
+                zq(s - 1)
+            if 2 < s <= NT:
+                zx(s - 1)
+            if 2 < s <= NT:
+                fin(s - 3)
         last(NT - 1)

@@ -5,18 +5,22 @@ from concourse.masks import make_identity
 
 T, K, D, N, G = 1536, 2048, 1024, 512, 128
 P = 128
+PASS = 512
 NT = T // P
-KP = K // 512
-DP = D // 512
+KP = K // PASS
+DP = D // PASS
 NB = K // G
 RB = D // G
 RT = N // P
+PASS_BLOCKS = PASS // G
+PLAIN_PASSES = 2
+ROOT_D = 32.0
 TURN_BANKS = 6
-ACC_BANKS = 2
-WORK_BUFS = 4
-LOT_BUFS = 3
-LOTS = [(i, 1) for i in range(NT)]
-RUN_PASS = 2
+SUM_BANKS = 2
+WIDE_BUFS = 4
+TURNED_BUFS = 3
+X_LOADS = [(1, 1)] + [(i, 2) for i in range(2, NT, 2)]
+Q_LOADS = [(0, 1), (1, 1), (2, 2)] + [(i, 4) for i in range(4, NT, 4)]
 
 FLOPS = 2 * T * N * (K + D)
 
@@ -31,11 +35,15 @@ ADD = mybir.AluOpType.add
 COPY = mybir.ActivationFunctionType.Copy
 
 
+def scalar_passes(i):
+    return 1 if i % 3 == 2 else 2
+
+
 def tile_relative_offset_scores_d9_kernel(tc, X_bytes, X_scale, B, Q, v, R_bytes, R_scale, g, out):
     nc = tc.nc
     with ExitStack() as ctx:
         keep = ctx.enter_context(tc.tile_pool(name="keep", bufs=1))
-        work = ctx.enter_context(tc.tile_pool(name="work", bufs=WORK_BUFS))
+        work = ctx.enter_context(tc.tile_pool(name="work", bufs=WIDE_BUFS))
         psum = ctx.enter_context(tc.psum_pool(name="psum", bufs=TURN_BANKS))
         ctx.enter_context(tc.manual_schedule())
 
@@ -43,350 +51,335 @@ def tile_relative_offset_scores_d9_kernel(tc, X_bytes, X_scale, B, Q, v, R_bytes
         one = keep.tile([P, 1], F32, align_bytes=64)
         nc.vector.memset(one[:], 1.0)
         nc.scalar.activation(out=ones[:], in_=one[:].to_broadcast([P, P]), func=COPY)
-        vrow = keep.tile([P, D], BF16, align_bytes=64)
-        nc.vector.memset(vrow[:], 0.0)
+        v_row = keep.tile([P, D], BF16, align_bytes=64)
+        nc.vector.memset(v_row[:], 0.0)
         ident = keep.tile([P, P], F32, align_bytes=64)
         make_identity(nc, ident[:])
 
-        xs = keep.tile([P, (NT - 1) * NB], F32, align_bytes=64)
-        rs = keep.tile([P, RT * RB], F32, align_bytes=64)
-        rs32 = keep.tile([P, RT * RB], F32, align_bytes=64)
-        gbc = keep.tile([P, N], BF16, align_bytes=64)
-        rb = [keep.tile([P, D], U8, name=f"rb{t}", align_bytes=64) for t in range(RT)]
-        x_loads = [(1, 1), (2, 2), (4, 2), (6, 2), (8, 2), (10, 2)]
-        q_loads = [(0, 1), (1, 1), (2, 2), (4, 4), (8, 4)]
-        xb = {}
-        qb = {}
-        x_tile = {}
-        q_tile = {}
-        for lo, n in x_loads:
-            x_tile[lo] = keep.tile([P, n, K], U8, name=f"xb{lo}", align_bytes=64)
-            for i in range(n):
-                xb[lo + i] = x_tile[lo][:, i, :]
-        for lo, n in q_loads:
-            q_tile[lo] = keep.tile([P, n, D], BF16, name=f"qb{lo}", align_bytes=64)
-            for i in range(n):
-                qb[lo + i] = q_tile[lo][:, i, :]
-        br = [keep.tile([P, 4, N], BF16, name=f"br{c}", align_bytes=64) for c in range(KP)]
-        X_v = X_bytes.rearrange("(p i) k -> p i k", i=NT)
-        Q_v = Q.rearrange("(p i) k -> p i k", i=NT)
-        B_v = B.rearrange("(c p j) n -> c p j n", p=P, j=4)
-        O_v = out.rearrange("(p i) n -> p i n", i=NT)
+        x_scales = keep.tile([P, (NT - 1) * NB], F32, align_bytes=64)
+        r_scales = keep.tile([P, RT * RB], F32, align_bytes=64)
+        g_all = keep.tile([P, N], BF16, align_bytes=64)
+        r_raw = [keep.tile([P, D], U8, name=f"r_raw{t}", align_bytes=64) for t in range(RT)]
+        x_lot = {lo: keep.tile([P, n, K], U8, name=f"x_raw{lo}", align_bytes=64) for lo, n in X_LOADS}
+        q_lot = {lo: keep.tile([P, n, D], BF16, name=f"q_raw{lo}", align_bytes=64) for lo, n in Q_LOADS}
+        x_raw = {lo + j: x_lot[lo][:, j, :] for lo, n in X_LOADS for j in range(n)}
+        q_raw = {lo + j: q_lot[lo][:, j, :] for lo, n in Q_LOADS for j in range(n)}
+        b_raw = [keep.tile([P, 4, N], BF16, name=f"b_raw{c}", align_bytes=64) for c in range(KP)]
+        x0_scales = keep.tile([P, NB], F32, align_bytes=64)
+        x0_raw = [keep.tile([P, K // 2], U8, name=f"x0_raw{h}", align_bytes=64) for h in range(2)]
+        X_tiles = X_bytes.rearrange("(p i) k -> p i k", i=NT)
+        Q_tiles = Q.rearrange("(p i) k -> p i k", i=NT)
+        out_tiles = out.rearrange("(p i) n -> p i n", i=NT)
+        X_scale_rows = X_scale.rearrange("(p i) j -> p (i j)", i=NT)
+        B_plain = B.rearrange("(c p t) n -> c p t n", p=P, t=4)
+        B_runs = B.rearrange("(c h u j e) n -> c j h u (e n)", h=32, u=2, j=4, e=2)
 
         def load_x(i):
-            if i in x_tile:
-                nc.sync.dma_start(out=x_tile[i][:], in_=X_v[:, i : i + dict(x_loads)[i], :])
+            nc.sync.dma_start(out=x_lot[i][:], in_=X_tiles[:, i : i + dict(X_LOADS)[i], :])
 
         def load_q(i):
-            if i in q_tile:
-                nc.sync.dma_start(out=q_tile[i][:], in_=Q_v[:, i : i + dict(q_loads)[i], :])
+            nc.sync.dma_start(out=q_lot[i][:], in_=Q_tiles[:, i : i + dict(Q_LOADS)[i], :])
 
         def load_r(t):
-            nc.sync.dma_start(out=rb[t][:], in_=R_bytes[P * t : P * t + P, :])
-
-        B_w = B.rearrange("(c h u j e) n -> c j h u (e n)", h=32, u=2, j=4, e=2)
+            nc.sync.dma_start(out=r_raw[t][:], in_=R_bytes[P * t : P * t + P, :])
 
         def load_b(c):
-            if c < RUN_PASS:
-                nc.sync.dma_start(out=br[c][:], in_=B_v[c])
+            if c < PLAIN_PASSES:
+                nc.sync.dma_start(out=b_raw[c][:], in_=B_plain[c])
             else:
                 for j in range(4):
-                    nc.sync.dma_start(out=br[c][j:P:4].rearrange("h (u e) n -> h u (e n)", u=2), in_=B_w[c, j])
+                    nc.sync.dma_start(out=b_raw[c][j:P:4].rearrange("h (u e) n -> h u (e n)", u=2), in_=B_runs[c, j])
 
-        xs_v = X_scale.rearrange("(p i) j -> p (i j)", i=NT)
-        xs_first = keep.tile([P, NB], F32, align_bytes=64)
-        x_first = [keep.tile([P, K // 2], U8, name=f"x_first{h}", align_bytes=64) for h in range(2)]
+        nc.sync.dma_start(out=x0_scales[:], in_=X_scale_rows[:, 0:NB])
+        for h in (1, 0):
+            nc.sync.dma_start(out=x0_raw[h][:], in_=X_tiles[:, 0, K // 2 * h : K // 2 * h + K // 2])
+        nc.sync.dma_start(out=r_scales[:], in_=R_scale.rearrange("a b -> (a b)").partition_broadcast(P))
+        load_r(0)
+        load_r(1)
+        load_b(0)
+        nc.sync.dma_start(out=v_row[0:1, :], in_=v.rearrange("(o k) -> o k", o=1))
+        load_r(2)
+        load_b(1)
+        load_r(3)
+        nc.sync.dma_start(out=x_scales[:], in_=X_scale_rows[:, NB:])
+        load_x(1)
+        load_q(0)
+        load_b(2)
+        load_q(1)
+        load_b(3)
+        load_x(2)
+        load_q(2)
+        nc.sync.dma_start(out=g_all[:], in_=g.partition_broadcast(P))
+        for i in range(4, NT, 2):
+            load_x(i)
+            if i in q_lot:
+                load_q(i)
 
-        def load_xs():
-            nc.sync.dma_start(out=xs[:], in_=xs_v[:, NB:])
+        held = {}
 
-        def load_first():
-            nc.sync.dma_start(out=xs_first[:], in_=xs_v[:, 0:NB])
-            for h in (1, 0):
-                nc.sync.dma_start(out=x_first[h][:], in_=X_v[:, 0, K // 2 * h : K // 2 * h + K // 2])
+        def new_bank(key):
+            bank = psum.tile([P, 2, 2, P], F32, name="bank", tag="turn")
+            held[key] = bank
+            return bank
+
+        def flat(bank):
+            return bank[:].rearrange("p c u r -> p (c u r)")
+
+        def turn(bank, words, first, stepped):
+            for c in range(2):
+                for u in range(2):
+                    w = 2 * P * (first + c)
+                    src = words[:, w + u : w + 2 * P : 2] if first + c < stepped else words[:, w + P * u : w + P * u + P]
+                    nc.tensor.transpose(bank[:, c, u, :], src, ident[:])
+
+        def empty(key, words):
+            nc.scalar.copy(out=words, in_=held.pop(key)[:].rearrange("p c u r -> p c r u"))
+
+        def as_words(grouped):
+            return grouped.rearrange("p c r t -> p (c r t)").bitcast(F32).rearrange("p (c r u) -> p c r u", c=grouped.shape[1], u=2)
+
+        def widen_runs(wide, raw, scale, blk):
+            c, q = divmod(blk, PASS_BLOCKS)
+            runs = wide.rearrange("r (c u h m) -> r c h u m", u=2, h=32, m=8)
+            nc.vector.tensor_scalar(out=runs[:, c, 8 * q : 8 * q + 8],
+                                    in0=raw.bitcast(FP8).rearrange("r (h u m) -> r h u m", u=2, m=8),
+                                    scalar1=scale, scalar2=None, op0=MULT)
+
+        def widen_words(wide, raw, scale, blk):
+            c, q = divmod(blk, PASS_BLOCKS)
+            words = wide.rearrange("r (c u p e) -> r c p u e", u=2, p=P, e=2)
+            nc.vector.tensor_scalar(out=words[:, c, 32 * q : 32 * q + 32],
+                                    in0=raw.bitcast(FP8).rearrange("r (p u e) -> r p u e", u=2, e=2),
+                                    scalar1=scale, scalar2=None, op0=MULT)
+
+        v_all = keep.tile([P, D], BF16, align_bytes=64)
+
+        def spread_v():
+            wide = flat(new_bank("v")).bitcast(BF16)
+            for h in range(D // N):
+                nc.tensor.matmul(wide[:, N * h : N * h + N], lhsT=ones[:], rhs=v_row[:, N * h : N * h + N], start=True, stop=True)
+
+        def empty_v():
+            nc.scalar.copy(out=v_all[:].bitcast(F32), in_=flat(held.pop("v")))
+
+        r_wide = [keep.tile([P, D], BF16, name=f"r_wide{t}", align_bytes=64) for t in range(RT)]
+        r_grouped = keep.tile([P, DP, N, 4], BF16, align_bytes=64)
+        r_codes = keep.tile([P, DP, N], U32, align_bytes=64)
+        r_exps = keep.tile([P, DP, N], U8, align_bytes=64)
+
+        def widen_r(t):
+            for blk in range(RB):
+                widen_runs(r_wide[t][:], r_raw[t][:, G * blk : G * blk + G], r_scales[:, RB * t + blk : RB * t + blk + 1], blk)
+
+        def turn_r(t):
+            turn(new_bank(("r", t)), r_wide[t][:].bitcast(F32), 0, 0)
+
+        def empty_r(t):
+            empty(("r", t), as_words(r_grouped[:])[:, :, P * t : P * t + P, :])
+
+        def quantise_r(c):
+            nc.vector.quantize_mx(out=r_codes[:, c, :].bitcast(FP8X4), scales=r_exps[:, c, :],
+                                  in_=r_grouped[:, c].rearrange("p n t -> p (n t)"))
+
+        b_grouped = [keep.tile([P, N, 4], BF16, name=f"b_grouped{c}", align_bytes=64) for c in range(KP)]
+        b_codes = keep.tile([P, KP, N], U32, align_bytes=64)
+        b_exps = keep.tile([P, KP, N], U8, align_bytes=64)
+
+        def group_b(c):
+            dst = b_grouped[c][:].rearrange("p (m i) t -> p m t i", i=4)
+            src = b_raw[c][:].rearrange("p t (m i) -> p m t i", i=4)
+            if c % 2 == 0:
+                nc.vector.tensor_scalar(out=dst, in0=src, scalar1=ROOT_D, scalar2=None, op0=MULT)
+            else:
+                nc.scalar.activation(out=dst, in_=src, func=COPY, scale=ROOT_D)
+
+        def quantise_b(c):
+            nc.vector.quantize_mx(out=b_codes[:, c, :].bitcast(FP8X4), scales=b_exps[:, c, :],
+                                  in_=b_grouped[c][:].rearrange("p n t -> p (n t)"))
 
         def x_block(i, blk):
             if i == 0:
-                half = NB // 2
-                return x_first[blk // half][:, G * (blk % half) : G * (blk % half) + G], xs_first[:, blk : blk + 1]
-            return xb[i][:, G * blk : G * blk + G], xs[:, NB * (i - 1) + blk : NB * (i - 1) + blk + 1]
+                h, b = divmod(blk, NB // 2)
+                return x0_raw[h][:, G * b : G * b + G], x0_scales[:, blk : blk + 1]
+            col = NB * (i - 1) + blk
+            return x_raw[i][:, G * blk : G * blk + G], x_scales[:, col : col + 1]
 
-        def load_rs():
-            nc.sync.dma_start(out=rs[:], in_=R_scale.rearrange("a b -> (a b)").partition_broadcast(P))
+        def x_wide(i):
+            if ("x_wide", i) not in held:
+                held["x_wide", i] = work.tile([P, K], BF16, name="x_wide", align_bytes=64)
+            return held["x_wide", i][:]
 
-        def load_v():
-            nc.sync.dma_start(out=vrow[0:1, :], in_=v.rearrange("(o k) -> o k", o=1))
+        def widen_x_scalar(i):
+            for blk in range(PASS_BLOCKS * scalar_passes(i)):
+                raw, scale = x_block(i, blk)
+                nc.scalar.activation(out=x_wide(i)[:, G * blk : G * blk + G], in_=raw.bitcast(FP8), func=COPY, scale=scale)
 
-        def load_g():
-            nc.sync.dma_start(out=gbc[:], in_=g.partition_broadcast(P))
+        def widen_x_vector(i):
+            for blk in range(PASS_BLOCKS * scalar_passes(i), NB):
+                widen = widen_words if blk < PASS_BLOCKS * PLAIN_PASSES else widen_runs
+                widen(x_wide(i), *x_block(i, blk), blk)
 
-        load_first(); load_rs(); load_r(0); load_b(0); load_r(1); load_v(); load_r(2)
-        load_b(1); load_r(3); load_xs(); load_x(1); load_q(0); load_b(2); load_q(1); load_b(3)
-        for i in range(2, NT):
-            load_x(i)
-            load_q(i)
-            if i == 3:
-                load_g()
+        def add_v(i):
+            c_wide = work.tile([P, D], BF16, align_bytes=64)
+            held["c_wide", i] = c_wide
+            nc.vector.tensor_tensor(out=c_wide[:].rearrange("r (u h m) -> r h u m", u=2, m=8),
+                                    in0=q_raw[i].rearrange("r (h u m) -> r h u m", u=2, m=8),
+                                    in1=v_all[:].rearrange("r (h u m) -> r h u m", u=2, m=8), op=ADD)
 
-        st = {}
+        def turn_x(i, half):
+            turn(new_bank(("x", i, half)), x_wide(i).bitcast(F32), 2 * half, scalar_passes(i))
 
-        def turn_bank(key):
-            bank = psum.tile([P, 2, 2, P], F32, name="bank", tag="turn")
-            st[key] = bank
-            return bank
-
-        vbc = keep.tile([P, D], BF16, align_bytes=64)
-
-        def bc():
-            bank = turn_bank("bc")
-            wide = bank[:].rearrange("p c u r -> p (c u r)").bitcast(BF16)
-            for h in range(DP):
-                nc.tensor.matmul(wide[:, 512 * h : 512 * h + 512], lhsT=ones[:], rhs=vrow[:, 512 * h : 512 * h + 512],
-                                 start=True, stop=True)
-
-        def bev():
-            bank = st.pop("bc")
-            nc.scalar.copy(out=vbc[:].bitcast(F32), in_=bank[:].rearrange("p c u r -> p (c u r)"))
-
-        rw_t = [keep.tile([P, D], BF16, name=f"rw{t}", align_bytes=64) for t in range(RT)]
-        rg = keep.tile([P, DP, N, 4], BF16, align_bytes=64)
-        rgw = rg[:].rearrange("p c n t -> p (c n t)").bitcast(F32).rearrange("p (c n u) -> p c n u", c=DP, u=2)
-        rc = keep.tile([P, DP, N], U32, align_bytes=64)
-        rsc = keep.tile([P, DP, N], U8, align_bytes=64)
-
-        def rscale():
-            nc.gpsimd.tensor_scalar(out=rs32[:], in0=rs[:], scalar1=1.0 / 32.0, scalar2=None, op0=MULT)
-
-        def v_widen(out_tile, in_ap, scale, blk, first_run=RUN_PASS, natural=RUN_PASS):
-            c, q = blk // 4, blk % 4
-            if c >= first_run:
-                runs = out_tile.rearrange("r (c u h m) -> r c h u m", u=2, h=32, m=8)
-                nc.vector.tensor_scalar(
-                    out=runs[:, c, 8 * q : 8 * q + 8],
-                    in0=in_ap.bitcast(FP8).rearrange("r (h u m) -> r h u m", u=2, m=8),
-                    scalar1=scale, scalar2=None, op0=MULT)
-                return
-            if c >= natural:
-                dst = out_tile.rearrange("r (c u p e) -> r c p u e", u=2, p=P, e=2)
-                nc.vector.tensor_scalar(
-                    out=dst[:, c, 32 * q : 32 * q + 32],
-                    in0=in_ap.bitcast(FP8).rearrange("r (p u e) -> r p u e", u=2, e=2),
-                    scalar1=scale, scalar2=None, op0=MULT)
-                return
-            nc.vector.tensor_scalar(out=out_tile[:, G * blk : G * blk + G], in0=in_ap.bitcast(FP8),
-                                    scalar1=scale, scalar2=None, op0=MULT)
-
-        def s_widen(out_tile, in_ap, scale, blk):
-            nc.scalar.activation(out=out_tile[:, G * blk : G * blk + G],
-                                 in_=in_ap.bitcast(FP8), func=COPY, scale=scale)
-
-        def rw(t):
-            for blk in range(RB):
-                v_widen(rw_t[t][:], rb[t][:, G * blk : G * blk + G], rs32[:, RB * t + blk : RB * t + blk + 1], blk, 0)
-
-        def transposes(bank, words, first, natural):
-            for c in range(2):
-                for u in range(2):
-                    w = 256 * (first + c)
-                    src = words[:, w + u : w + 256 : 2] if first + c < natural else words[:, w + P * u : w + P * u + P]
-                    nc.tensor.transpose(bank[:, c, u, :], src, ident[:])
-
-        def rt(t):
-            transposes(turn_bank(("rt", t)), rw_t[t][:].bitcast(F32), 0, 0)
-
-        def re(t):
-            bank = st.pop(("rt", t))
-            nc.scalar.copy(out=rgw[:, :, P * t : P * t + P, :], in_=bank[:].rearrange("p c u r -> p c r u"))
-
-        def rz(c):
-            nc.vector.quantize_mx(out=rc[:, c, :].bitcast(FP8X4), scales=rsc[:, c, :],
-                                  in_=rg[:, c].rearrange("p n t -> p (n t)"))
-
-        b_grp = [keep.tile([P, N, 4], BF16, name=f"bg{c}", align_bytes=64) for c in range(KP)]
-        b_code = keep.tile([P, KP, N], U32, align_bytes=64)
-        b_scale = keep.tile([P, KP, N], U8, align_bytes=64)
-
-        def bg(c):
-            nc.vector.tensor_copy(out=b_grp[c][:].rearrange("p (m i) t -> p m t i", i=4),
-                                  in_=br[c][:].rearrange("p t (m i) -> p m t i", i=4))
-
-        def bgs(c):
-            nc.scalar.copy(out=b_grp[c][:].rearrange("p (m i) t -> p m t i", i=4),
-                           in_=br[c][:].rearrange("p t (m i) -> p m t i", i=4))
-
-        def bz(c):
-            nc.vector.quantize_mx(out=b_code[:, c, :].bitcast(FP8X4), scales=b_scale[:, c, :],
-                                  in_=b_grp[c][:].rearrange("p n t -> p (n t)"))
-
-        xw = [None] * NT
-        cw = [None] * NT
-        lot = {}
-        for lo, n in LOTS:
-            for i in range(lo, lo + n):
-                lot[i] = (lo, n)
-        acc = [None] * NT
-
-        def s_blocks(i):
-            return 4 if i % 3 == 2 else 8
-
-        def xw_tile(i):
-            if xw[i] is None:
-                t = work.tile([P, K], BF16, name="xw", align_bytes=64)
-                xw[i] = t
-
-        def ws(i):
-            xw_tile(i)
-            for blk in range(s_blocks(i)):
-                s_widen(xw[i][:], *x_block(i, blk), blk)
-
-        def wv(i):
-            xw_tile(i)
-            for blk in range(s_blocks(i), NB):
-                v_widen(xw[i][:], *x_block(i, blk), blk, RUN_PASS, (s_blocks(i) + 3) // 4)
-
-        def ad(i):
-            t = work.tile([P, D], BF16, name="cw", align_bytes=64)
-            cw[i] = t
-            nc.vector.tensor_tensor(
-                out=t[:].rearrange("r (u h m) -> r h u m", u=2, m=8),
-                in0=qb[i].rearrange("r (h u m) -> r h u m", u=2, m=8),
-                in1=vbc[:].rearrange("r (h u m) -> r h u m", u=2, m=8), op=ADD)
-
-        def tx0(i):
-            transposes(turn_bank(("x0", i)), xw[i][:].bitcast(F32), 0, (s_blocks(i) + 3) // 4)
-
-        def tx1(i):
-            transposes(turn_bank(("x1", i)), xw[i][:].bitcast(F32), 2, RUN_PASS)
-
-        def xg_words(i):
-            lo, n = lot[i]
-            if ("xg", lo) not in st:
-                st["xg", lo] = work.tile([P, n, KP, P, 4], BF16, name="xg", bufs=LOT_BUFS, align_bytes=64)
-            return st["xg", lo][:, i - lo].rearrange("p c r t -> p (c r t)").bitcast(F32).rearrange("p (c r u) -> p c r u", c=KP, u=2)
-
-        def ex0(i):
-            bank = st.pop(("x0", i))
-            nc.scalar.copy(out=xg_words(i)[:, 0:2], in_=bank[:].rearrange("p c u r -> p c r u"))
-
-        def ex1(i):
-            bank = st.pop(("x1", i))
-            nc.scalar.copy(out=xg_words(i)[:, 2:4], in_=bank[:].rearrange("p c u r -> p c r u"))
-
-        def tq(i):
-            bank = turn_bank(("q", i))
-            words = cw[i][:].bitcast(F32)
+        def turn_c(i):
+            bank = new_bank(("c", i))
+            words = held.pop(("c_wide", i))[:].bitcast(F32)
             for c in range(DP):
                 for u in range(2):
-                    w = 256 * u + P * c
+                    w = P * (DP * u + c)
                     nc.tensor.transpose(bank[:, c, u, :], words[:, w : w + P], ident[:])
 
-        def eq(i):
-            bank = st.pop(("q", i))
-            lo, n = lot[i]
-            if ("cg", lo) not in st:
-                st["cg", lo] = work.tile([P, n, DP, P, 4], BF16, name="cg", bufs=LOT_BUFS, align_bytes=64)
-            words = st["cg", lo][:, i - lo].rearrange("p c r t -> p (c r t)").bitcast(F32).rearrange("p (c r u) -> p c r u", c=DP, u=2)
-            nc.scalar.copy(out=words, in_=bank[:].rearrange("p c u r -> p c r u"))
+        def empty_x(i, half):
+            if ("x_grouped", i) not in held:
+                held["x_grouped", i] = work.tile([P, KP, P, 4], BF16, name="x_grouped", bufs=TURNED_BUFS, align_bytes=64)
+            empty(("x", i, half), as_words(held["x_grouped", i][:])[:, 2 * half : 2 * half + 2])
 
-        def zx(i):
-            lo, n = lot[i]
-            xc = work.tile([P, n, KP, P], U32, bufs=LOT_BUFS, align_bytes=64)
-            xsc = work.tile([P, n, KP, P], U8, bufs=LOT_BUFS, align_bytes=64)
-            nc.vector.quantize_mx(out=xc[:].rearrange("p n c r -> p (n c r)").bitcast(FP8X4),
-                                  scales=xsc[:].rearrange("p n c r -> p (n c r)"),
-                                  in_=st.pop(("xg", lo))[:].rearrange("p n c r t -> p (n c r t)"))
-            for j in range(n):
-                st["zx", lo + j] = (xc[:, j], xsc[:, j])
+        def empty_c(i):
+            c_grouped = work.tile([P, DP, P, 4], BF16, bufs=TURNED_BUFS, align_bytes=64)
+            held["c_grouped", i] = c_grouped
+            empty(("c", i), as_words(c_grouped[:]))
 
-        def zq(i):
-            lo, n = lot[i]
-            cc = work.tile([P, n, DP, P], U32, bufs=LOT_BUFS, align_bytes=64)
-            csc = work.tile([P, n, DP, P], U8, bufs=LOT_BUFS, align_bytes=64)
-            nc.vector.quantize_mx(out=cc[:].rearrange("p n c r -> p (n c r)").bitcast(FP8X4),
-                                  scales=csc[:].rearrange("p n c r -> p (n c r)"),
-                                  in_=st.pop(("cg", lo))[:].rearrange("p n c r t -> p (n c r t)"))
-            for j in range(n):
-                st["zq", lo + j] = (cc[:, j], csc[:, j])
+        def quantise_x(i):
+            x_codes = work.tile([P, KP, P], U32, bufs=TURNED_BUFS, align_bytes=64)
+            x_exps = work.tile([P, KP, P], U8, bufs=TURNED_BUFS, align_bytes=64)
+            nc.vector.quantize_mx(out=x_codes[:].rearrange("p c r -> p (c r)").bitcast(FP8X4),
+                                  scales=x_exps[:].rearrange("p c r -> p (c r)"),
+                                  in_=held.pop(("x_grouped", i))[:].rearrange("p c r t -> p (c r t)"))
+            held["x_mx", i] = (x_codes, x_exps, b_codes, b_exps)
+
+        def quantise_c(i):
+            c_codes = work.tile([P, DP, P], U32, bufs=TURNED_BUFS, align_bytes=64)
+            c_exps = work.tile([P, DP, P], U8, bufs=TURNED_BUFS, align_bytes=64)
+            nc.vector.quantize_mx(out=c_codes[:].rearrange("p c r -> p (c r)").bitcast(FP8X4),
+                                  scales=c_exps[:].rearrange("p c r -> p (c r)"),
+                                  in_=held.pop(("c_grouped", i))[:].rearrange("p c r t -> p (c r t)"))
+            held["c_mx", i] = (c_codes, c_exps, r_codes, r_exps)
+
+        def one_pass(total, operands, c, cols, number):
+            codes, exps, other_codes, other_exps = operands
+            nc.tensor.matmul_mx(out=total, lhsT=codes[:, c, :].bitcast(FP8X4), lhsT_scale=exps[:, c, :],
+                                rhs=other_codes[:, c, cols].bitcast(FP8X4), rhs_scale=other_exps[:, c, cols],
+                                start=(number == 0), stop=(number == KP + DP - 1))
 
         added = [0] * NT
 
-        def group_flags(i):
-            if added[i] == 0:
-                t = psum.tile([P, N], F32, name="acc", tag="acc", bufs=ACC_BANKS)
-                acc[i] = t
-            added[i] = added[i] + 1
-            return added[i] == 1, added[i] == KP + DP
-
-        def mq(i):
-            cc, csc = st.pop(("zq", i))
-            for c in range(DP):
-                first, last = group_flags(i)
-                nc.tensor.matmul_mx(out=acc[i][:], lhsT=cc[:, c, :].bitcast(FP8X4), lhsT_scale=csc[:, c, :],
-                                    rhs=rc[:, c, :].bitcast(FP8X4), rhs_scale=rsc[:, c, :],
-                                    start=first, stop=last)
-
-        def mx(i, passes=range(KP)):
-            xc, xsc = st["zx", i]
+        def multiply(i, product, passes):
             for c in passes:
-                first, last = group_flags(i)
-                nc.tensor.matmul_mx(out=acc[i][:], lhsT=xc[:, c, :].bitcast(FP8X4), lhsT_scale=xsc[:, c, :],
-                                    rhs=b_code[:, c, :].bitcast(FP8X4), rhs_scale=b_scale[:, c, :],
-                                    start=first, stop=last)
+                if added[i] == 0:
+                    held["sum", i] = psum.tile([P, N], F32, name="total", tag="sum", bufs=SUM_BANKS)
+                one_pass(held["sum", i][:], held[product, i], c, slice(0, N), added[i])
+                added[i] = added[i] + 1
 
-        def last(i):
-            cc, csc = st.pop(("zq", i))
-            xc, xsc = st["zx", i]
-            pairs = [(cc, csc, rc, rsc, c) for c in range(DP)] + [(xc, xsc, b_code, b_scale, c) for c in range(KP)]
-            for h in range(2):
-                cols = slice(256 * h, 256 * h + 256)
-                half = turn_bank(("last", h))[:].rearrange("p c u r -> p (c u r)")[:, 0:256]
-                for j, (a, a_s, b, b_s, c) in enumerate(pairs):
-                    nc.tensor.matmul_mx(out=half, lhsT=a[:, c, :].bitcast(FP8X4), lhsT_scale=a_s[:, c, :],
-                                        rhs=b[:, c, cols].bitcast(FP8X4), rhs_scale=b_s[:, c, cols],
-                                        start=(j == 0), stop=(j == len(pairs) - 1))
-            fin(i - 1)
-            for h in range(2):
-                cols = slice(256 * h, 256 * h + 256)
-                half = st.pop(("last", h))[:].rearrange("p c u r -> p (c u r)")[:, 0:256]
-                o_half = work.tile([P, 256], F32, align_bytes=64)
-                nc.vector.tensor_tensor(out=o_half[:], in0=half, in1=gbc[:, cols], op=MULT)
-                nc.sync.dma_start(out=O_v[:, i, cols], in_=o_half[:])
+        def multiply_c(i):
+            multiply(i, "c_mx", range(DP))
 
-        def fin(i):
-            o = work.tile([P, N], F32, bufs=NT, align_bytes=64)
-            nc.vector.tensor_tensor(out=o[:], in0=acc[i][:], in1=gbc[:], op=MULT)
-            nc.sync.dma_start(out=O_v[:, i, :], in_=o[:])
+        def multiply_x(i, first, end):
+            multiply(i, "x_mx", range(first, end))
 
-        rscale()
-        ws(0); wv(0); tx1(0); tx0(0); rw(0); bg(0); rt(0); ex1(0); ex0(0); rw(1); bz(0); bc(); rt(1); re(0); rw(2); bev(); bgs(1); zx(0); rw(3); rt(2); rt(3); mx(0, range(1))
-        wv(1); ad(0); re(1); re(2); re(3); ws(1); tq(0); tx1(1); bz(1); bg(2); rz(0); rz(1); eq(0); tx0(1); mx(0, range(1, 2)); ad(1); bz(2); ex1(1); ex0(1); bgs(3); zq(0); tq(1); mq(0); mx(0, range(2, 3))
-        wv(2); zx(1); ad(2); mx(1, range(3)); eq(1); ws(2); bz(3); zq(1)
+        def scale_and_store(result, total, i, cols):
+            nc.vector.scalar_tensor_tensor(out=result[:], in0=total, scalar=1.0 / ROOT_D, in1=g_all[:, cols], op0=MULT, op1=MULT)
+            nc.sync.dma_start(out=out_tiles[:, i, cols], in_=result[:])
+
+        def finish(i):
+            result = work.tile([P, N], F32, bufs=NT, align_bytes=64)
+            scale_and_store(result, held.pop(("sum", i))[:], i, slice(0, N))
+
+        widen_x_scalar(0)
+        widen_x_vector(0)
+        turn_x(0, 1)
+        turn_x(0, 0)
+        widen_r(0)
+        widen_r(1)
+        group_b(0)
+        turn_r(0)
+        empty_x(0, 1)
+        empty_x(0, 0)
+        widen_r(2)
+        quantise_b(0)
+        spread_v()
+        turn_r(1)
+        empty_r(0)
+        group_b(1)
+        empty_v()
+        quantise_x(0)
+        widen_r(3)
+        turn_r(2)
+        turn_r(3)
+        multiply_x(0, 0, 1)
+        widen_x_vector(1)
+        add_v(0)
+        for t in range(1, RT):
+            empty_r(t)
+        widen_x_scalar(1)
+        turn_c(0)
+        turn_x(1, 1)
+        quantise_b(1)
+        group_b(2)
+        for c in range(DP):
+            quantise_r(c)
+        empty_c(0)
+        turn_x(1, 0)
+        multiply_x(0, 1, 2)
+        add_v(1)
+        quantise_b(2)
+        empty_x(1, 1)
+        empty_x(1, 0)
+        group_b(3)
+        quantise_c(0)
+        turn_c(1)
+        multiply_c(0)
+        multiply_x(0, 2, 3)
+        widen_x_vector(2)
+        quantise_x(1)
+        add_v(2)
+        multiply_x(1, 0, 3)
+        empty_c(1)
+        widen_x_scalar(2)
+        quantise_b(3)
+        quantise_c(1)
+
         for s in range(2, NT + 1):
             if s + 1 < NT:
-                ws(s + 1)
+                widen_x_scalar(s + 1)
             if s < NT:
-                tq(s)
-                tx1(s)
-                tx0(s)
-                ex1(s)
-                eq(s)
-                ex0(s)
+                turn_c(s)
+                turn_x(s, 1)
+                turn_x(s, 0)
+                empty_x(s, 1)
+                empty_c(s)
+                empty_x(s, 0)
             if s == 2:
-                mx(0, range(3, 4))
-                mx(1, range(3, 4))
+                multiply_x(0, KP - 1, KP)
+                multiply_x(1, KP - 1, KP)
             elif s == 3:
-                mq(1)
+                multiply_c(1)
             else:
-                mq(s - 2)
-                mx(s - 2)
+                multiply_c(s - 2)
+                multiply_x(s - 2, 0, KP)
             if s + 1 < NT:
-                wv(s + 1)
-            if s + 1 < NT:
-                ad(s + 1)
-            if 2 < s <= NT:
-                zq(s - 1)
-            if 2 < s <= NT:
-                zx(s - 1)
-            if 2 < s <= NT:
-                fin(s - 3)
-        last(NT - 1)
+                widen_x_vector(s + 1)
+                add_v(s + 1)
+            if s > 2:
+                quantise_c(s - 1)
+                quantise_x(s - 1)
+                finish(s - 3)
+
+        last = NT - 1
+        passes = [("c_mx", c) for c in range(DP)] + [("x_mx", c) for c in range(KP)]
+        halves = [slice(N // 2 * h, N // 2 * h + N // 2) for h in range(2)]
+        for h, cols in enumerate(halves):
+            total = flat(new_bank(("last", h)))[:, 0 : N // 2]
+            for number, (product, c) in enumerate(passes):
+                one_pass(total, held[product, last], c, cols, number)
+        finish(last - 1)
+        for h, cols in enumerate(halves):
+            half_result = work.tile([P, N // 2], F32, align_bytes=64)
+            scale_and_store(half_result, flat(held.pop(("last", h)))[:, 0 : N // 2], last, cols)

@@ -19,8 +19,10 @@ TURN_BANKS = 6
 SUM_BANKS = 2
 WIDE_BUFS = 4
 TURNED_BUFS = 3
+MX_ALIGN = 256
 X_LOADS = [(1, 1)] + [(i, 2) for i in range(2, NT, 2)]
 Q_LOADS = [(0, 1), (1, 1), (2, 2)] + [(i, 4) for i in range(4, NT, 4)]
+LAST_PIECES = [(0, N // 2), (N // 2, 3 * N // 4), (3 * N // 4, N)]
 
 FLOPS = 2 * T * N * (K + D)
 
@@ -164,8 +166,8 @@ def tile_relative_offset_scores_d9_kernel(tc, X_bytes, X_scale, B, Q, v, R_bytes
 
         r_wide = [keep.tile([P, D], BF16, name=f"r_wide{t}", align_bytes=64) for t in range(RT)]
         r_grouped = keep.tile([P, DP, N, 4], BF16, align_bytes=64)
-        r_codes = keep.tile([P, DP, N], U32, align_bytes=64)
-        r_exps = keep.tile([P, DP, N], U8, align_bytes=64)
+        r_codes = keep.tile([P, DP, N], U32, align_bytes=MX_ALIGN)
+        r_exps = keep.tile([P, DP, N], U8, align_bytes=MX_ALIGN)
 
         def widen_r(t):
             for blk in range(RB):
@@ -182,8 +184,8 @@ def tile_relative_offset_scores_d9_kernel(tc, X_bytes, X_scale, B, Q, v, R_bytes
                                   in_=r_grouped[:, c].rearrange("p n t -> p (n t)"))
 
         b_grouped = [keep.tile([P, N, 4], BF16, name=f"b_grouped{c}", align_bytes=64) for c in range(KP)]
-        b_codes = keep.tile([P, KP, N], U32, align_bytes=64)
-        b_exps = keep.tile([P, KP, N], U8, align_bytes=64)
+        b_codes = keep.tile([P, KP, N], U32, align_bytes=MX_ALIGN)
+        b_exps = keep.tile([P, KP, N], U8, align_bytes=MX_ALIGN)
 
         def group_b(c):
             dst = b_grouped[c][:].rearrange("p (m i) t -> p m t i", i=4)
@@ -248,16 +250,16 @@ def tile_relative_offset_scores_d9_kernel(tc, X_bytes, X_scale, B, Q, v, R_bytes
             empty(("c", i), as_words(c_grouped[:]))
 
         def quantise_x(i):
-            x_codes = work.tile([P, KP, P], U32, bufs=TURNED_BUFS, align_bytes=64)
-            x_exps = work.tile([P, KP, P], U8, bufs=TURNED_BUFS, align_bytes=64)
+            x_codes = work.tile([P, KP, P], U32, bufs=TURNED_BUFS, align_bytes=MX_ALIGN)
+            x_exps = work.tile([P, KP, P], U8, bufs=TURNED_BUFS, align_bytes=MX_ALIGN)
             nc.vector.quantize_mx(out=x_codes[:].rearrange("p c r -> p (c r)").bitcast(FP8X4),
                                   scales=x_exps[:].rearrange("p c r -> p (c r)"),
                                   in_=held.pop(("x_grouped", i))[:].rearrange("p c r t -> p (c r t)"))
             held["x_mx", i] = (x_codes, x_exps, b_codes, b_exps)
 
         def quantise_c(i):
-            c_codes = work.tile([P, DP, P], U32, bufs=TURNED_BUFS, align_bytes=64)
-            c_exps = work.tile([P, DP, P], U8, bufs=TURNED_BUFS, align_bytes=64)
+            c_codes = work.tile([P, DP, P], U32, bufs=TURNED_BUFS, align_bytes=MX_ALIGN)
+            c_exps = work.tile([P, DP, P], U8, bufs=TURNED_BUFS, align_bytes=MX_ALIGN)
             nc.vector.quantize_mx(out=c_codes[:].rearrange("p c r -> p (c r)").bitcast(FP8X4),
                                   scales=c_exps[:].rearrange("p c r -> p (c r)"),
                                   in_=held.pop(("c_grouped", i))[:].rearrange("p c r t -> p (c r t)"))
@@ -374,12 +376,13 @@ def tile_relative_offset_scores_d9_kernel(tc, X_bytes, X_scale, B, Q, v, R_bytes
 
         last = NT - 1
         passes = [("c_mx", c) for c in range(DP)] + [("x_mx", c) for c in range(KP)]
-        halves = [slice(N // 2 * h, N // 2 * h + N // 2) for h in range(2)]
-        for h, cols in enumerate(halves):
-            total = flat(new_bank(("last", h)))[:, 0 : N // 2]
+        totals = []
+        for lo, hi in LAST_PIECES:
+            total = flat(psum.tile([P, 2, 2, P], F32, name="bank", tag="turn"))[:, 0 : hi - lo]
+            totals.append(total)
             for number, (product, c) in enumerate(passes):
-                one_pass(total, held[product, last], c, cols, number)
+                one_pass(total, held[product, last], c, slice(lo, hi), number)
         finish(last - 1)
-        for h, cols in enumerate(halves):
-            half_result = work.tile([P, N // 2], F32, align_bytes=64)
-            scale_and_store(half_result, flat(held.pop(("last", h)))[:, 0 : N // 2], last, cols)
+        for (lo, hi), total in zip(LAST_PIECES, totals):
+            piece = work.tile([P, hi - lo], F32, align_bytes=64)
+            scale_and_store(piece, total, last, slice(lo, hi))

@@ -18,7 +18,7 @@ ROOT_D = 32.0
 TURN_BANKS = 6
 SUM_BANKS = 2
 WIDE_BUFS = 4
-TURNED_BUFS = 3
+TURNED_BUFS = 4
 MX_ALIGN = 256
 X_LOADS = [(1, 1)] + [(i, 2) for i in range(2, NT, 2)]
 Q_LOADS = [(0, 1), (1, 1), (2, 2)] + [(i, 4) for i in range(4, NT, 4)]
@@ -38,7 +38,7 @@ COPY = mybir.ActivationFunctionType.Copy
 
 
 def scalar_passes(i):
-    return 1 if i % 3 == 2 else 2
+    return [2,2,2,2,1,2,1,2,1,2,1,1][i]
 
 
 def tile_relative_offset_scores_d9_kernel(tc, X_bytes, X_scale, B, Q, v, R_bytes, R_scale, g, out):
@@ -57,6 +57,8 @@ def tile_relative_offset_scores_d9_kernel(tc, X_bytes, X_scale, B, Q, v, R_bytes
         nc.vector.memset(v_row[:], 0.0)
         ident = keep.tile([P, P], F32, align_bytes=64)
         make_identity(nc, ident[:])
+        ident32 = keep.tile([P, P], BF16, align_bytes=64)
+        nc.vector.tensor_scalar(out=ident32[:], in0=ident[:], scalar1=ROOT_D, scalar2=None, op0=MULT)
 
         x_scales = keep.tile([P, (NT - 1) * NB], F32, align_bytes=64)
         r_scales = keep.tile([P, RT * RB], F32, align_bytes=64)
@@ -93,29 +95,31 @@ def tile_relative_offset_scores_d9_kernel(tc, X_bytes, X_scale, B, Q, v, R_bytes
                     nc.sync.dma_start(out=b_raw[c][j:P:4].rearrange("h (u e) n -> h u (e n)", u=2), in_=B_runs[c, j])
 
         nc.sync.dma_start(out=x0_scales[:], in_=X_scale_rows[:, 0:NB])
-        for h in (1, 0):
-            nc.sync.dma_start(out=x0_raw[h][:], in_=X_tiles[:, 0, K // 2 * h : K // 2 * h + K // 2])
+        nc.sync.dma_start(out=x0_raw[1][:], in_=X_tiles[:, 0, K // 2 :])
+        nc.sync.dma_start(out=v_row[0:1, 0:D], in_=v.rearrange("(o k) -> o k", o=1))
+        nc.sync.dma_start(out=x0_raw[0][:], in_=X_tiles[:, 0, 0 : K // 2])
         nc.sync.dma_start(out=r_scales[:], in_=R_scale.rearrange("a b -> (a b)").partition_broadcast(P))
         load_r(0)
         load_r(1)
         load_b(0)
-        nc.sync.dma_start(out=v_row[0:1, :], in_=v.rearrange("(o k) -> o k", o=1))
         load_r(2)
-        load_b(1)
-        load_r(3)
         nc.sync.dma_start(out=x_scales[:], in_=X_scale_rows[:, NB:])
         load_x(1)
+        load_r(3)
+        load_b(1)
         load_q(0)
         load_b(2)
         load_q(1)
-        load_b(3)
         load_x(2)
+        load_b(3)
         load_q(2)
+        load_x(4)
         nc.sync.dma_start(out=g_all[:], in_=g.partition_broadcast(P))
-        for i in range(4, NT, 2):
-            load_x(i)
-            if i in q_lot:
-                load_q(i)
+        load_q(4)
+        load_x(6)
+        load_x(8)
+        load_q(8)
+        load_x(10)
 
         held = {}
 
@@ -194,6 +198,19 @@ def tile_relative_offset_scores_d9_kernel(tc, X_bytes, X_scale, B, Q, v, R_bytes
                 nc.vector.tensor_scalar(out=dst, in0=src, scalar1=ROOT_D, scalar2=None, op0=MULT)
             else:
                 nc.scalar.activation(out=dst, in_=src, func=COPY, scale=ROOT_D)
+
+        def weave_b(c, half):
+            slots = flat(new_bank(("b", c, half))).bitcast(BF16).rearrange("p (n u e) -> p u e n", u=2, e=2)
+            cols = slice(N // 2 * half, N // 2 * half + N // 2)
+            for u in range(2):
+                nc.tensor.matmul(slots[:, u], lhsT=ident32[:], rhs=b_raw[c][:, 2 * u : 2 * u + 2, cols], start=True, stop=True)
+
+        def empty_b(c, half, vector=False):
+            words = b_grouped[c][:].rearrange("p n t -> p (n t)").bitcast(F32)[:, N * half : N * half + N]
+            if vector:
+                nc.vector.tensor_copy(out=words, in_=flat(held.pop(("b", c, half))))
+            else:
+                nc.scalar.copy(out=words, in_=flat(held.pop(("b", c, half))))
 
         def quantise_b(c):
             nc.vector.quantize_mx(out=b_codes[:, c, :].bitcast(FP8X4), scales=b_exps[:, c, :],
@@ -294,6 +311,30 @@ def tile_relative_offset_scores_d9_kernel(tc, X_bytes, X_scale, B, Q, v, R_bytes
             result = work.tile([P, N], F32, bufs=NT, align_bytes=64)
             scale_and_store(result, held.pop(("sum", i))[:], i, slice(0, N))
 
+
+        def turn_tile(i):
+            turn_c(i)
+            turn_x(i, 1)
+            turn_x(i, 0)
+
+        def empty_tile(i):
+            empty_x(i, 1)
+            empty_c(i)
+            empty_x(i, 0)
+
+        def widen_vector(i):
+            widen_x_vector(i)
+            add_v(i)
+
+        def quantise_tile(i):
+            quantise_x(i)
+            quantise_c(i)
+
+        def multiply_tile(i):
+            multiply_c(i)
+            multiply_x(i, 0, KP)
+
+        spread_v()
         widen_x_scalar(0)
         widen_x_vector(0)
         turn_x(0, 1)
@@ -301,78 +342,86 @@ def tile_relative_offset_scores_d9_kernel(tc, X_bytes, X_scale, B, Q, v, R_bytes
         widen_r(0)
         widen_r(1)
         group_b(0)
-        turn_r(0)
+        empty_v()
         empty_x(0, 1)
         empty_x(0, 0)
-        widen_r(2)
-        quantise_b(0)
-        spread_v()
+        turn_r(0)
         turn_r(1)
-        empty_r(0)
-        group_b(1)
-        empty_v()
-        quantise_x(0)
-        widen_r(3)
-        turn_r(2)
-        turn_r(3)
-        multiply_x(0, 0, 1)
+        widen_r(2)
         widen_x_vector(1)
-        add_v(0)
-        for t in range(1, RT):
-            empty_r(t)
+        widen_r(3)
+        quantise_b(0)
         widen_x_scalar(1)
-        turn_c(0)
+        turn_r(2)
         turn_x(1, 1)
-        quantise_b(1)
-        group_b(2)
-        for c in range(DP):
-            quantise_r(c)
-        empty_c(0)
+        weave_b(1, 0)
+        weave_b(1, 1)
+        empty_r(0)
+        empty_r(1)
+        empty_r(2)
+        turn_r(3)
         turn_x(1, 0)
-        multiply_x(0, 1, 2)
+        add_v(0)
+        quantise_x(0)
         add_v(1)
-        quantise_b(2)
-        empty_x(1, 1)
-        empty_x(1, 0)
-        group_b(3)
-        quantise_c(0)
+        empty_b(1, 0)
+        empty_b(1, 1)
+        turn_c(0)
         turn_c(1)
-        multiply_c(0)
-        multiply_x(0, 2, 3)
+        empty_r(3)
+        group_b(2)
         widen_x_vector(2)
-        quantise_x(1)
+        quantise_b(1)
+        weave_b(3, 0)
+        empty_x(1, 1)
+        weave_b(3, 1)
+        empty_x(1, 0)
+        empty_c(0)
+        quantise_r(0)
+        quantise_r(1)
         add_v(2)
-        multiply_x(1, 0, 3)
-        empty_c(1)
         widen_x_scalar(2)
+        multiply_x(0, 0, 2)
+        empty_b(3, 0)
+        empty_b(3, 1)
+        quantise_b(2)
+        turn_tile(2)
+        empty_c(1)
+        quantise_c(0)
+        widen_vector(3)
         quantise_b(3)
-        quantise_c(1)
-
-        for s in range(2, NT + 1):
-            if s + 1 < NT:
-                widen_x_scalar(s + 1)
-            if s < NT:
-                turn_c(s)
-                turn_x(s, 1)
-                turn_x(s, 0)
-                empty_x(s, 1)
-                empty_c(s)
-                empty_x(s, 0)
-            if s == 2:
-                multiply_x(0, KP - 1, KP)
-                multiply_x(1, KP - 1, KP)
-            elif s == 3:
-                multiply_c(1)
-            else:
-                multiply_c(s - 2)
-                multiply_x(s - 2, 0, KP)
-            if s + 1 < NT:
-                widen_x_vector(s + 1)
-                add_v(s + 1)
-            if s > 2:
-                quantise_c(s - 1)
-                quantise_x(s - 1)
-                finish(s - 3)
+        widen_x_scalar(3)
+        widen_x_scalar(4)
+        multiply_c(0)
+        multiply_x(0, 2, 4)
+        widen_vector(4)
+        empty_tile(2)
+        quantise_tile(1)
+        for a in range(3, NT - 1, 2):
+            b = a + 1
+            turn_tile(a)
+            turn_tile(b)
+            empty_tile(a)
+            quantise_tile(a - 1)
+            finish(a - 3)
+            multiply_tile(a - 2)
+            multiply_tile(a - 1)
+            widen_vector(a + 2)
+            empty_tile(b)
+            widen_x_scalar(a + 2)
+            if b + 2 < NT:
+                widen_x_scalar(b + 2)
+                widen_vector(b + 2)
+            finish(a - 2)
+            quantise_tile(a)
+        turn_tile(11)
+        empty_tile(11)
+        quantise_tile(10)
+        finish(8)
+        multiply_tile(9)
+        multiply_tile(10)
+        quantise_tile(11)
+        finish(9)
 
         last = NT - 1
         passes = [("c_mx", c) for c in range(DP)] + [("x_mx", c) for c in range(KP)]

@@ -391,37 +391,21 @@ def tile_relative_offset_scores_d9_kernel(tc, X_bytes, X_scale, B, Q, v, R_bytes
         widen_vector(3)
         quantise_b(3)
         widen_x_scalar(3)
-        widen_x_scalar(4)
         multiply_c(0)
         multiply_x(0, 2, 4)
-        widen_vector(4)
-        empty_tile(2)
         quantise_tile(1)
-        for a in range(3, NT - 1, 2):
-            b = a + 1
-            turn_tile(a)
-            turn_tile(b)
-            empty_tile(a)
-            quantise_tile(a - 1)
-            finish(a - 3)
-            multiply_tile(a - 2)
-            multiply_tile(a - 1)
-            widen_vector(a + 2)
-            empty_tile(b)
-            widen_x_scalar(a + 2)
-            if b + 2 < NT:
-                widen_x_scalar(b + 2)
-                widen_vector(b + 2)
-            finish(a - 2)
-            quantise_tile(a)
-        turn_tile(11)
-        empty_tile(11)
-        quantise_tile(10)
-        finish(8)
-        multiply_tile(9)
-        multiply_tile(10)
-        quantise_tile(11)
-        finish(9)
+        empty_tile(2)
+        for s in range(3, NT + 1):
+            if s + 1 < NT:
+                widen_x_scalar(s + 1)
+            if s < NT:
+                turn_tile(s)
+                empty_tile(s)
+            multiply_tile(s - 2)
+            if s + 1 < NT:
+                widen_vector(s + 1)
+            quantise_tile(s - 1)
+            finish(s - 3)
 
         last = NT - 1
         passes = [("c_mx", c) for c in range(DP)] + [("x_mx", c) for c in range(KP)]

@@ -15,6 +15,7 @@ RT = N // P
 PASS_BLOCKS = PASS // G
 PLAIN_PASSES = 2
 ROOT_D = 32.0
+BANKS = 8
 TURN_BANKS = 6
 SUM_BANKS = 2
 WIDE_BUFS = 4
@@ -46,11 +47,13 @@ def tile_relative_offset_scores_d9_kernel(tc, X_bytes, X_scale, B, Q, v, R_bytes
     with ExitStack() as ctx:
         keep = ctx.enter_context(tc.tile_pool(name="keep", bufs=1))
         work = ctx.enter_context(tc.tile_pool(name="work", bufs=WIDE_BUFS))
-        psum = ctx.enter_context(tc.psum_pool(name="psum", bufs=TURN_BANKS))
+        psum = ctx.enter_context(tc.psum_pool(name="psum", bufs=1))
         ctx.enter_context(tc.manual_schedule())
 
         ones = keep.tile([P, P], BF16, align_bytes=64)
         one = keep.tile([P, 1], F32, align_bytes=64)
+        r_column = keep.tile([P, 1], F32, align_bytes=64)
+        nc.vector.memset(r_column[:], 0.0)
         nc.vector.memset(one[:], 1.0)
         nc.scalar.activation(out=ones[:], in_=one[:].to_broadcast([P, P]), func=COPY)
         v_row = keep.tile([P, D], BF16, align_bytes=64)
@@ -96,16 +99,16 @@ def tile_relative_offset_scores_d9_kernel(tc, X_bytes, X_scale, B, Q, v, R_bytes
 
         nc.sync.dma_start(out=x0_scales[:], in_=X_scale_rows[:, 0:NB])
         nc.sync.dma_start(out=x0_raw[1][:], in_=X_tiles[:, 0, K // 2 :])
-        nc.sync.dma_start(out=v_row[0:1, 0:D], in_=v.rearrange("(o k) -> o k", o=1))
-        nc.sync.dma_start(out=x0_raw[0][:], in_=X_tiles[:, 0, 0 : K // 2])
-        nc.sync.dma_start(out=r_scales[:], in_=R_scale.rearrange("a b -> (a b)").partition_broadcast(P))
+        nc.sync.dma_start(out=r_column[0 : RT * RB, :], in_=R_scale.rearrange("a (b o) -> (a b) o", o=1))
         load_r(0)
+        nc.sync.dma_start(out=x0_raw[0][:], in_=X_tiles[:, 0, 0 : K // 2])
         load_r(1)
-        load_b(0)
+        nc.sync.dma_start(out=v_row[0:1, 0:D], in_=v.rearrange("(o k) -> o k", o=1))
         load_r(2)
+        load_b(0)
+        load_r(3)
         nc.sync.dma_start(out=x_scales[:], in_=X_scale_rows[:, NB:])
         load_x(1)
-        load_r(3)
         load_b(1)
         load_q(0)
         load_b(2)
@@ -123,9 +126,17 @@ def tile_relative_offset_scores_d9_kernel(tc, X_bytes, X_scale, B, Q, v, R_bytes
 
         held = {}
 
+        free_banks = list(range(BANKS))
+
         def new_bank(key):
-            bank = psum.tile([P, 2, 2, P], F32, name="bank", tag="turn")
-            held[key] = bank
+            number = free_banks.pop(0)
+            bank = psum.tile([P, 2, 2, P], F32, name=f"bank{number}")
+            held[key] = (bank, number)
+            return bank
+
+        def full_bank(key):
+            bank, number = held.pop(key)
+            free_banks.append(number)
             return bank
 
         def flat(bank):
@@ -138,8 +149,8 @@ def tile_relative_offset_scores_d9_kernel(tc, X_bytes, X_scale, B, Q, v, R_bytes
                     src = words[:, w + u : w + 2 * P : 2] if first + c < stepped else words[:, w + P * u : w + P * u + P]
                     nc.tensor.transpose(bank[:, c, u, :], src, ident[:])
 
-        def empty(key, words):
-            nc.scalar.copy(out=words, in_=held.pop(key)[:].rearrange("p c u r -> p c r u"))
+        def empty(key, words, copy=nc.scalar.copy):
+            copy(out=words, in_=full_bank(key)[:].rearrange("p c u r -> p c r u"))
 
         def as_words(grouped):
             return grouped.rearrange("p c r t -> p (c r t)").bitcast(F32).rearrange("p (c r u) -> p c r u", c=grouped.shape[1], u=2)
@@ -166,7 +177,11 @@ def tile_relative_offset_scores_d9_kernel(tc, X_bytes, X_scale, B, Q, v, R_bytes
                 nc.tensor.matmul(wide[:, N * h : N * h + N], lhsT=ones[:], rhs=v_row[:, N * h : N * h + N], start=True, stop=True)
 
         def empty_v():
-            nc.scalar.copy(out=v_all[:].bitcast(F32), in_=flat(held.pop("v")))
+            nc.scalar.copy(out=v_all[:].bitcast(F32), in_=flat(full_bank("v")))
+
+        def spread_r_scales():
+            nc.tensor.transpose(new_bank("r_scales")[:, 0, 0, :], r_column[:].to_broadcast([P, P]), ident[:])
+            nc.scalar.copy(out=r_scales[:], in_=full_bank("r_scales")[:, 0, 0, 0 : RT * RB])
 
         r_wide = [keep.tile([P, D], BF16, name=f"r_wide{t}", align_bytes=64) for t in range(RT)]
         r_grouped = keep.tile([P, DP, N, 4], BF16, align_bytes=64)
@@ -180,8 +195,8 @@ def tile_relative_offset_scores_d9_kernel(tc, X_bytes, X_scale, B, Q, v, R_bytes
         def turn_r(t):
             turn(new_bank(("r", t)), r_wide[t][:].bitcast(F32), 0, 0)
 
-        def empty_r(t):
-            empty(("r", t), as_words(r_grouped[:])[:, :, P * t : P * t + P, :])
+        def empty_r(t, copy=nc.scalar.copy):
+            empty(("r", t), as_words(r_grouped[:])[:, :, P * t : P * t + P, :], copy)
 
         def quantise_r(c):
             nc.vector.quantize_mx(out=r_codes[:, c, :].bitcast(FP8X4), scales=r_exps[:, c, :],
@@ -208,9 +223,9 @@ def tile_relative_offset_scores_d9_kernel(tc, X_bytes, X_scale, B, Q, v, R_bytes
         def empty_b(c, half, vector=False):
             words = b_grouped[c][:].rearrange("p n t -> p (n t)").bitcast(F32)[:, N * half : N * half + N]
             if vector:
-                nc.vector.tensor_copy(out=words, in_=flat(held.pop(("b", c, half))))
+                nc.vector.tensor_copy(out=words, in_=flat(full_bank(("b", c, half))))
             else:
-                nc.scalar.copy(out=words, in_=flat(held.pop(("b", c, half))))
+                nc.scalar.copy(out=words, in_=flat(full_bank(("b", c, half))))
 
         def quantise_b(c):
             nc.vector.quantize_mx(out=b_codes[:, c, :].bitcast(FP8X4), scales=b_exps[:, c, :],
@@ -256,15 +271,15 @@ def tile_relative_offset_scores_d9_kernel(tc, X_bytes, X_scale, B, Q, v, R_bytes
                     w = P * (DP * u + c)
                     nc.tensor.transpose(bank[:, c, u, :], words[:, w : w + P], ident[:])
 
-        def empty_x(i, half):
+        def empty_x(i, half, copy=nc.scalar.copy):
             if ("x_grouped", i) not in held:
                 held["x_grouped", i] = work.tile([P, KP, P, 4], BF16, name="x_grouped", bufs=TURNED_BUFS, align_bytes=64)
-            empty(("x", i, half), as_words(held["x_grouped", i][:])[:, 2 * half : 2 * half + 2])
+            empty(("x", i, half), as_words(held["x_grouped", i][:])[:, 2 * half : 2 * half + 2], copy)
 
-        def empty_c(i):
+        def empty_c(i, copy=nc.scalar.copy):
             c_grouped = work.tile([P, DP, P, 4], BF16, bufs=TURNED_BUFS, align_bytes=64)
             held["c_grouped", i] = c_grouped
-            empty(("c", i), as_words(c_grouped[:]))
+            empty(("c", i), as_words(c_grouped[:]), copy)
 
         def quantise_x(i):
             x_codes = work.tile([P, KP, P], U32, bufs=TURNED_BUFS, align_bytes=MX_ALIGN)
@@ -273,6 +288,17 @@ def tile_relative_offset_scores_d9_kernel(tc, X_bytes, X_scale, B, Q, v, R_bytes
                                   scales=x_exps[:].rearrange("p c r -> p (c r)"),
                                   in_=held.pop(("x_grouped", i))[:].rearrange("p c r t -> p (c r t)"))
             held["x_mx", i] = (x_codes, x_exps, b_codes, b_exps)
+
+        def quantise_x_half(i, half):
+            if ("x_mx", i) not in held:
+                x_codes = work.tile([P, KP, P], U32, bufs=TURNED_BUFS, align_bytes=MX_ALIGN)
+                x_exps = work.tile([P, KP, P], U8, bufs=TURNED_BUFS, align_bytes=MX_ALIGN)
+                held["x_mx", i] = (x_codes, x_exps, b_codes, b_exps)
+            x_codes, x_exps = held["x_mx", i][0:2]
+            two = slice(2 * half, 2 * half + 2)
+            nc.vector.quantize_mx(out=x_codes[:, two].rearrange("p c r -> p (c r)").bitcast(FP8X4),
+                                  scales=x_exps[:, two].rearrange("p c r -> p (c r)"),
+                                  in_=held["x_grouped", i][:, two].rearrange("p c r t -> p (c r t)"))
 
         def quantise_c(i):
             c_codes = work.tile([P, DP, P], U32, bufs=TURNED_BUFS, align_bytes=MX_ALIGN)
@@ -293,8 +319,8 @@ def tile_relative_offset_scores_d9_kernel(tc, X_bytes, X_scale, B, Q, v, R_bytes
         def multiply(i, product, passes):
             for c in passes:
                 if added[i] == 0:
-                    held["sum", i] = psum.tile([P, N], F32, name="total", tag="sum", bufs=SUM_BANKS)
-                one_pass(held["sum", i][:], held[product, i], c, slice(0, N), added[i])
+                    new_bank(("sum", i))
+                one_pass(flat(held["sum", i][0]), held[product, i], c, slice(0, N), added[i])
                 added[i] = added[i] + 1
 
         def multiply_c(i):
@@ -309,7 +335,7 @@ def tile_relative_offset_scores_d9_kernel(tc, X_bytes, X_scale, B, Q, v, R_bytes
 
         def finish(i):
             result = work.tile([P, N], F32, bufs=NT, align_bytes=64)
-            scale_and_store(result, held.pop(("sum", i))[:], i, slice(0, N))
+            scale_and_store(result, flat(full_bank(("sum", i))), i, slice(0, N))
 
 
         def turn_tile(i):
@@ -334,32 +360,34 @@ def tile_relative_offset_scores_d9_kernel(tc, X_bytes, X_scale, B, Q, v, R_bytes
             multiply_c(i)
             multiply_x(i, 0, KP)
 
-        spread_v()
-        widen_x_scalar(0)
+        spread_r_scales()
         widen_x_vector(0)
+        widen_x_scalar(0)
         turn_x(0, 1)
+        spread_v()
         turn_x(0, 0)
         widen_r(0)
         widen_r(1)
+        widen_r(2)
         group_b(0)
-        empty_v()
         empty_x(0, 1)
+        empty_v()
         empty_x(0, 0)
         turn_r(0)
         turn_r(1)
-        widen_r(2)
-        widen_x_vector(1)
-        widen_r(3)
-        quantise_b(0)
-        widen_x_scalar(1)
         turn_r(2)
+        widen_r(3)
+        widen_x_vector(1)
+        quantise_b(0)
+        empty_r(0)
+        widen_x_scalar(1)
+        turn_r(3)
         turn_x(1, 1)
         weave_b(1, 0)
         weave_b(1, 1)
-        empty_r(0)
         empty_r(1)
         empty_r(2)
-        turn_r(3)
+        empty_r(3)
         turn_x(1, 0)
         add_v(0)
         quantise_x(0)
@@ -368,8 +396,9 @@ def tile_relative_offset_scores_d9_kernel(tc, X_bytes, X_scale, B, Q, v, R_bytes
         empty_b(1, 1)
         turn_c(0)
         turn_c(1)
-        empty_r(3)
         group_b(2)
+        quantise_r(0)
+        quantise_r(1)
         widen_x_vector(2)
         quantise_b(1)
         weave_b(3, 0)
@@ -377,8 +406,6 @@ def tile_relative_offset_scores_d9_kernel(tc, X_bytes, X_scale, B, Q, v, R_bytes
         weave_b(3, 1)
         empty_x(1, 0)
         empty_c(0)
-        quantise_r(0)
-        quantise_r(1)
         add_v(2)
         widen_x_scalar(2)
         multiply_x(0, 0, 2)
@@ -388,8 +415,8 @@ def tile_relative_offset_scores_d9_kernel(tc, X_bytes, X_scale, B, Q, v, R_bytes
         turn_tile(2)
         empty_c(1)
         quantise_c(0)
-        widen_vector(3)
         quantise_b(3)
+        widen_vector(3)
         widen_x_scalar(3)
         multiply_c(0)
         multiply_x(0, 2, 4)
@@ -405,13 +432,15 @@ def tile_relative_offset_scores_d9_kernel(tc, X_bytes, X_scale, B, Q, v, R_bytes
             if s + 1 < NT:
                 widen_vector(s + 1)
             quantise_tile(s - 1)
-            finish(s - 3)
+            if s > 3:
+                finish(s - 4)
+        finish(NT - 3)
 
         last = NT - 1
         passes = [("c_mx", c) for c in range(DP)] + [("x_mx", c) for c in range(KP)]
         totals = []
         for lo, hi in LAST_PIECES:
-            total = flat(psum.tile([P, 2, 2, P], F32, name="bank", tag="turn"))[:, 0 : hi - lo]
+            total = flat(new_bank(("piece", lo)))[:, 0 : hi - lo]
             totals.append(total)
             for number, (product, c) in enumerate(passes):
                 one_pass(total, held[product, last], c, slice(lo, hi), number)

@@ -39,7 +39,7 @@ COPY = mybir.ActivationFunctionType.Copy
 
 
 def scalar_passes(i):
-    return [2,2,2,2,1,2,1,2,1,2,1,1][i]
+    return [2,2,2,2,1,2,1,1,1,1,1,1][i]
 
 
 def tile_relative_offset_scores_d9_kernel(tc, X_bytes, X_scale, B, Q, v, R_bytes, R_scale, g, out):
@@ -55,7 +55,6 @@ def tile_relative_offset_scores_d9_kernel(tc, X_bytes, X_scale, B, Q, v, R_bytes
         r_column = keep.tile([P, 1], F32, align_bytes=64)
         nc.vector.memset(r_column[:], 0.0)
         nc.vector.memset(one[:], 1.0)
-        nc.scalar.activation(out=ones[:], in_=one[:].to_broadcast([P, P]), func=COPY)
         v_row = keep.tile([P, D], BF16, align_bytes=64)
         nc.vector.memset(v_row[:], 0.0)
         ident = keep.tile([P, P], F32, align_bytes=64)
@@ -97,13 +96,14 @@ def tile_relative_offset_scores_d9_kernel(tc, X_bytes, X_scale, B, Q, v, R_bytes
                 for j in range(4):
                     nc.sync.dma_start(out=b_raw[c][j:P:4].rearrange("h (u e) n -> h u (e n)", u=2), in_=B_runs[c, j])
 
-        nc.sync.dma_start(out=x0_scales[:], in_=X_scale_rows[:, 0:NB])
+        nc.scalar.dma_start(out=x0_scales[:], in_=X_scale_rows[:, 0:NB])
         nc.sync.dma_start(out=x0_raw[1][:], in_=X_tiles[:, 0, K // 2 :])
-        nc.sync.dma_start(out=r_column[0 : RT * RB, :], in_=R_scale.rearrange("a (b o) -> (a b) o", o=1))
         load_r(0)
+        nc.scalar.dma_start(out=r_column[0 : RT * RB, :], in_=R_scale.rearrange("a (b o) -> (a b) o", o=1))
+        nc.scalar.activation(out=ones[:], in_=one[:].to_broadcast([P, P]), func=COPY)
+        nc.sync.dma_start(out=v_row[0:1, 0:D], in_=v.rearrange("(o k) -> o k", o=1))
         nc.sync.dma_start(out=x0_raw[0][:], in_=X_tiles[:, 0, 0 : K // 2])
         load_r(1)
-        nc.sync.dma_start(out=v_row[0:1, 0:D], in_=v.rearrange("(o k) -> o k", o=1))
         load_r(2)
         load_b(0)
         load_r(3)
@@ -117,9 +117,9 @@ def tile_relative_offset_scores_d9_kernel(tc, X_bytes, X_scale, B, Q, v, R_bytes
         load_b(3)
         load_q(2)
         load_x(4)
-        nc.sync.dma_start(out=g_all[:], in_=g.partition_broadcast(P))
         load_q(4)
         load_x(6)
+        nc.sync.dma_start(out=g_all[:], in_=g.partition_broadcast(P))
         load_x(8)
         load_q(8)
         load_x(10)
@@ -206,9 +206,11 @@ def tile_relative_offset_scores_d9_kernel(tc, X_bytes, X_scale, B, Q, v, R_bytes
         b_codes = keep.tile([P, KP, N], U32, align_bytes=MX_ALIGN)
         b_exps = keep.tile([P, KP, N], U8, align_bytes=MX_ALIGN)
 
-        def group_b(c):
+        def group_b(c, half=None):
             dst = b_grouped[c][:].rearrange("p (m i) t -> p m t i", i=4)
             src = b_raw[c][:].rearrange("p t (m i) -> p m t i", i=4)
+            if half is not None:
+                dst, src = (a[:, N // 8 * half : N // 8 * half + N // 8] for a in (dst, src))
             if c % 2 == 0:
                 nc.vector.tensor_scalar(out=dst, in0=src, scalar1=ROOT_D, scalar2=None, op0=MULT)
             else:
@@ -361,25 +363,26 @@ def tile_relative_offset_scores_d9_kernel(tc, X_bytes, X_scale, B, Q, v, R_bytes
             multiply_x(i, 0, KP)
 
         spread_r_scales()
+        spread_v()
         widen_x_vector(0)
         widen_x_scalar(0)
         turn_x(0, 1)
-        spread_v()
         turn_x(0, 0)
         widen_r(0)
         widen_r(1)
         widen_r(2)
-        group_b(0)
-        empty_x(0, 1)
+        group_b(0, 0)
         empty_v()
+        empty_x(0, 1)
         empty_x(0, 0)
         turn_r(0)
+        weave_b(0, 1)
         turn_r(1)
         turn_r(2)
         widen_r(3)
         widen_x_vector(1)
-        quantise_b(0)
         empty_r(0)
+        empty_b(0, 1)
         widen_x_scalar(1)
         turn_r(3)
         turn_x(1, 1)
@@ -389,14 +392,15 @@ def tile_relative_offset_scores_d9_kernel(tc, X_bytes, X_scale, B, Q, v, R_bytes
         empty_r(2)
         empty_r(3)
         turn_x(1, 0)
-        add_v(0)
         quantise_x(0)
-        add_v(1)
+        add_v(0)
+        quantise_b(0)
         empty_b(1, 0)
         empty_b(1, 1)
+        group_b(2)
+        add_v(1)
         turn_c(0)
         turn_c(1)
-        group_b(2)
         quantise_r(0)
         quantise_r(1)
         widen_x_vector(2)
@@ -415,8 +419,8 @@ def tile_relative_offset_scores_d9_kernel(tc, X_bytes, X_scale, B, Q, v, R_bytes
         turn_tile(2)
         empty_c(1)
         quantise_c(0)
-        quantise_b(3)
         widen_vector(3)
+        quantise_b(3)
         widen_x_scalar(3)
         multiply_c(0)
         multiply_x(0, 2, 4)

@@ -20,6 +20,7 @@ TURN_BANKS = 6
 SUM_BANKS = 2
 WIDE_BUFS = 4
 TURNED_BUFS = 4
+PLANE = 8
 MX_ALIGN = 256
 X_LOADS = [(1, 1)] + [(i, 2) for i in range(2, NT, 2)]
 Q_LOADS = [(0, 1), (1, 1), (2, 2)] + [(i, 4) for i in range(4, NT, 4)]
@@ -287,7 +288,7 @@ def tile_relative_offset_scores_d9_kernel(tc, X_bytes, X_scale, B, Q, v, R_bytes
             x_codes = work.tile([P, KP, P], U32, bufs=TURNED_BUFS, align_bytes=MX_ALIGN)
             x_exps = work.tile([P, KP, P], U8, bufs=TURNED_BUFS, align_bytes=MX_ALIGN)
             nc.vector.quantize_mx(out=x_codes[:].rearrange("p c r -> p (c r)").bitcast(FP8X4),
-                                  scales=x_exps[:].rearrange("p c r -> p (c r)"),
+                                  scales=x_exps[PLANE:].rearrange("p c r -> p (c r)"),
                                   in_=held.pop(("x_grouped", i))[:].rearrange("p c r t -> p (c r t)"))
             held["x_mx", i] = (x_codes, x_exps, b_codes, b_exps)
 
@@ -299,20 +300,20 @@ def tile_relative_offset_scores_d9_kernel(tc, X_bytes, X_scale, B, Q, v, R_bytes
             x_codes, x_exps = held["x_mx", i][0:2]
             two = slice(2 * half, 2 * half + 2)
             nc.vector.quantize_mx(out=x_codes[:, two].rearrange("p c r -> p (c r)").bitcast(FP8X4),
-                                  scales=x_exps[:, two].rearrange("p c r -> p (c r)"),
+                                  scales=x_exps[PLANE:, two].rearrange("p c r -> p (c r)"),
                                   in_=held["x_grouped", i][:, two].rearrange("p c r t -> p (c r t)"))
 
         def quantise_c(i):
             c_codes = work.tile([P, DP, P], U32, bufs=TURNED_BUFS, align_bytes=MX_ALIGN)
             c_exps = work.tile([P, DP, P], U8, bufs=TURNED_BUFS, align_bytes=MX_ALIGN)
             nc.vector.quantize_mx(out=c_codes[:].rearrange("p c r -> p (c r)").bitcast(FP8X4),
-                                  scales=c_exps[:].rearrange("p c r -> p (c r)"),
+                                  scales=c_exps[PLANE:].rearrange("p c r -> p (c r)"),
                                   in_=held.pop(("c_grouped", i))[:].rearrange("p c r t -> p (c r t)"))
             held["c_mx", i] = (c_codes, c_exps, r_codes, r_exps)
 
         def one_pass(total, operands, c, cols, number):
             codes, exps, other_codes, other_exps = operands
-            nc.tensor.matmul_mx(out=total, lhsT=codes[:, c, :].bitcast(FP8X4), lhsT_scale=exps[:, c, :],
+            nc.tensor.matmul_mx(out=total, lhsT=codes[:, c, :].bitcast(FP8X4), lhsT_scale=exps[PLANE:, c, :],
                                 rhs=other_codes[:, c, cols].bitcast(FP8X4), rhs_scale=other_exps[:, c, cols],
                                 start=(number == 0), stop=(number == KP + DP - 1))
 

@@ -54,14 +54,13 @@ def tile_relative_offset_scores_d9_kernel(tc, X_bytes, X_scale, B, Q, v, R_bytes
         ones = keep.tile([P, P], BF16, align_bytes=64)
         one = keep.tile([P, 1], F32, align_bytes=64)
         r_column = keep.tile([P, 1], F32, align_bytes=64)
-        nc.vector.memset(r_column[:], 0.0)
+        nc.gpsimd.memset(r_column[:], 0.0)
         nc.vector.memset(one[:], 1.0)
         v_row = keep.tile([P, D], BF16, align_bytes=64)
         nc.vector.memset(v_row[:], 0.0)
         ident = keep.tile([P, P], F32, align_bytes=64)
         make_identity(nc, ident[:])
         ident32 = keep.tile([P, P], BF16, align_bytes=64)
-        nc.vector.tensor_scalar(out=ident32[:], in0=ident[:], scalar1=ROOT_D, scalar2=None, op0=MULT)
 
         x_scales = keep.tile([P, (NT - 1) * NB], F32, align_bytes=64)
         r_scales = keep.tile([P, RT * RB], F32, align_bytes=64)
@@ -98,13 +97,14 @@ def tile_relative_offset_scores_d9_kernel(tc, X_bytes, X_scale, B, Q, v, R_bytes
                     nc.sync.dma_start(out=b_raw[c][j:P:4].rearrange("h (u e) n -> h u (e n)", u=2), in_=B_runs[c, j])
 
         nc.scalar.dma_start(out=x0_scales[:], in_=X_scale_rows[:, 0:NB])
+        nc.scalar.dma_start(out=r_column[0 : RT * RB, :], in_=R_scale.rearrange("a (b o) -> (a b) o", o=1))
         nc.sync.dma_start(out=x0_raw[1][:], in_=X_tiles[:, 0, K // 2 :])
         load_r(0)
-        nc.scalar.dma_start(out=r_column[0 : RT * RB, :], in_=R_scale.rearrange("a (b o) -> (a b) o", o=1))
         nc.scalar.activation(out=ones[:], in_=one[:].to_broadcast([P, P]), func=COPY)
-        nc.sync.dma_start(out=v_row[0:1, 0:D], in_=v.rearrange("(o k) -> o k", o=1))
+        nc.scalar.activation(out=ident32[:], in_=ident[:], func=COPY, scale=ROOT_D)
         nc.sync.dma_start(out=x0_raw[0][:], in_=X_tiles[:, 0, 0 : K // 2])
         load_r(1)
+        nc.sync.dma_start(out=v_row[0:1, 0:D], in_=v.rearrange("(o k) -> o k", o=1))
         load_r(2)
         load_b(0)
         load_r(3)
@@ -212,7 +212,7 @@ def tile_relative_offset_scores_d9_kernel(tc, X_bytes, X_scale, B, Q, v, R_bytes
             src = b_raw[c][:].rearrange("p t (m i) -> p m t i", i=4)
             if half is not None:
                 dst, src = (a[:, N // 8 * half : N // 8 * half + N // 8] for a in (dst, src))
-            if c % 2 == 0:
+            if True:
                 nc.vector.tensor_scalar(out=dst, in0=src, scalar1=ROOT_D, scalar2=None, op0=MULT)
             else:
                 nc.scalar.activation(out=dst, in_=src, func=COPY, scale=ROOT_D)
@@ -364,17 +364,17 @@ def tile_relative_offset_scores_d9_kernel(tc, X_bytes, X_scale, B, Q, v, R_bytes
             multiply_x(i, 0, KP)
 
         spread_r_scales()
-        spread_v()
         widen_x_vector(0)
         widen_x_scalar(0)
         turn_x(0, 1)
+        spread_v()
         turn_x(0, 0)
         widen_r(0)
         widen_r(1)
         widen_r(2)
         group_b(0, 0)
-        empty_v()
         empty_x(0, 1)
+        empty_v()
         empty_x(0, 0)
         turn_r(0)
         weave_b(0, 1)
@@ -436,8 +436,10 @@ def tile_relative_offset_scores_d9_kernel(tc, X_bytes, X_scale, B, Q, v, R_bytes
             multiply_tile(s - 2)
             if s + 1 < NT:
                 widen_vector(s + 1)
+            if s == NT:
+                finish(s - 4)
             quantise_tile(s - 1)
-            if s > 3:
+            if 3 < s < NT:
                 finish(s - 4)
         finish(NT - 3)
 

@@ -21,6 +21,7 @@ SUM_BANKS = 2
 WIDE_BUFS = 4
 TURNED_BUFS = 4
 PLANE = 8
+CAST_FROM = 6
 MX_ALIGN = 256
 X_LOADS = [(1, 1)] + [(i, 2) for i in range(2, NT, 2)]
 Q_LOADS = [(0, 1), (1, 1), (2, 2)] + [(i, 4) for i in range(4, NT, 4)]
@@ -246,6 +247,18 @@ def tile_relative_offset_scores_d9_kernel(tc, X_bytes, X_scale, B, Q, v, R_bytes
                 held["x_wide", i] = work.tile([P, K], BF16, name="x_wide", align_bytes=64)
             return held["x_wide", i][:]
 
+        def cast_x(i):
+            x_cast = work.tile([P, PASS], BF16, align_bytes=64)
+            held["x_cast", i] = x_cast
+            nc.scalar.copy(out=x_cast[:], in_=x_raw[i][:, 0:PASS].bitcast(FP8))
+
+        def scale_x(i):
+            x_cast = held.pop(("x_cast", i))
+            words = x_wide(i).rearrange("r (c u p e) -> r c p u e", u=2, p=P, e=2)
+            for blk in range(PASS_BLOCKS):
+                nc.scalar.activation(out=words[:, 0, 32 * blk : 32 * blk + 32], func=COPY, scale=x_block(i, blk)[1],
+                                     in_=x_cast[:, G * blk : G * blk + G].rearrange("r (p u e) -> r p u e", u=2, e=2))
+
         def widen_x_scalar(i):
             for blk in range(PASS_BLOCKS * scalar_passes(i)):
                 raw, scale = x_block(i, blk)
@@ -264,7 +277,7 @@ def tile_relative_offset_scores_d9_kernel(tc, X_bytes, X_scale, B, Q, v, R_bytes
                                     in1=v_all[:].rearrange("r (h u m) -> r h u m", u=2, m=8), op=ADD)
 
         def turn_x(i, half):
-            turn(new_bank(("x", i, half)), x_wide(i).bitcast(F32), 2 * half, scalar_passes(i))
+            turn(new_bank(("x", i, half)), x_wide(i).bitcast(F32), 2 * half, scalar_passes(i) if i < CAST_FROM else 0)
 
         def turn_c(i):
             bank = new_bank(("c", i))
@@ -428,8 +441,12 @@ def tile_relative_offset_scores_d9_kernel(tc, X_bytes, X_scale, B, Q, v, R_bytes
         quantise_tile(1)
         empty_tile(2)
         for s in range(3, NT + 1):
-            if s + 1 < NT:
+            if s + 1 < CAST_FROM:
                 widen_x_scalar(s + 1)
+            elif s + 1 < NT:
+                scale_x(s + 1)
+            if CAST_FROM <= s + 2 < NT:
+                cast_x(s + 2)
             if s < NT:
                 turn_tile(s)
                 empty_tile(s)

@@ -16,11 +16,10 @@ PASS_BLOCKS = PASS // G
 PLAIN_PASSES = 2
 ROOT_D = 32.0
 BANKS = 8
-TURN_BANKS = 6
-SUM_BANKS = 2
 WIDE_BUFS = 4
 TURNED_BUFS = 4
 PLANE = 8
+HEAD_TILES = 4
 CAST_FROM = 6
 MX_ALIGN = 256
 X_LOADS = [(1, 1)] + [(i, 2) for i in range(2, NT, 2)]
@@ -41,7 +40,11 @@ COPY = mybir.ActivationFunctionType.Copy
 
 
 def scalar_passes(i):
-    return [2,2,2,2,1,2,1,1,1,1,1,1][i]
+    return 2 if i < HEAD_TILES or (i % 3 == 2 and i < NT - 1) else 1
+
+
+def cast_first(i):
+    return CAST_FROM <= i < NT and scalar_passes(i) == 1
 
 
 def tile_relative_offset_scores_d9_kernel(tc, X_bytes, X_scale, B, Q, v, R_bytes, R_scale, g, out):
@@ -66,7 +69,8 @@ def tile_relative_offset_scores_d9_kernel(tc, X_bytes, X_scale, B, Q, v, R_bytes
         x_scales = keep.tile([P, (NT - 1) * NB], F32, align_bytes=64)
         r_scales = keep.tile([P, RT * RB], F32, align_bytes=64)
         g_all = keep.tile([P, N], BF16, align_bytes=64)
-        r_raw = [keep.tile([P, D], U8, name=f"r_raw{t}", align_bytes=64) for t in range(RT)]
+        r_lot = [keep.tile([P, 2, D], U8, name=f"r_raw{h}", align_bytes=64) for h in range(RT // 2)]
+        r_raw = [r_lot[t // 2][:, t % 2, :] for t in range(RT)]
         x_lot = {lo: keep.tile([P, n, K], U8, name=f"x_raw{lo}", align_bytes=64) for lo, n in X_LOADS}
         q_lot = {lo: keep.tile([P, n, D], BF16, name=f"q_raw{lo}", align_bytes=64) for lo, n in Q_LOADS}
         x_raw = {lo + j: x_lot[lo][:, j, :] for lo, n in X_LOADS for j in range(n)}
@@ -88,7 +92,7 @@ def tile_relative_offset_scores_d9_kernel(tc, X_bytes, X_scale, B, Q, v, R_bytes
             nc.sync.dma_start(out=q_lot[i][:], in_=Q_tiles[:, i : i + dict(Q_LOADS)[i], :])
 
         def load_r(t):
-            nc.sync.dma_start(out=r_raw[t][:], in_=R_bytes[P * t : P * t + P, :])
+            nc.sync.dma_start(out=r_lot[t // 2][:], in_=R_bytes.rearrange("(t p) k -> p t k", p=P)[:, t : t + 2, :])
 
         def load_b(c):
             if c < PLAIN_PASSES:
@@ -104,11 +108,9 @@ def tile_relative_offset_scores_d9_kernel(tc, X_bytes, X_scale, B, Q, v, R_bytes
         nc.scalar.activation(out=ones[:], in_=one[:].to_broadcast([P, P]), func=COPY)
         nc.scalar.activation(out=ident32[:], in_=ident[:], func=COPY, scale=ROOT_D)
         nc.sync.dma_start(out=x0_raw[0][:], in_=X_tiles[:, 0, 0 : K // 2])
-        load_r(1)
-        nc.sync.dma_start(out=v_row[0:1, 0:D], in_=v.rearrange("(o k) -> o k", o=1))
-        load_r(2)
+        nc.sync.dma_start(out=v_row[0:1, :], in_=v.rearrange("(o k) -> o k", o=1))
         load_b(0)
-        load_r(3)
+        load_r(2)
         nc.sync.dma_start(out=x_scales[:], in_=X_scale_rows[:, NB:])
         load_x(1)
         load_b(1)
@@ -127,7 +129,6 @@ def tile_relative_offset_scores_d9_kernel(tc, X_bytes, X_scale, B, Q, v, R_bytes
         load_x(10)
 
         held = {}
-
         free_banks = list(range(BANKS))
 
         def new_bank(key):
@@ -151,8 +152,8 @@ def tile_relative_offset_scores_d9_kernel(tc, X_bytes, X_scale, B, Q, v, R_bytes
                     src = words[:, w + u : w + 2 * P : 2] if first + c < stepped else words[:, w + P * u : w + P * u + P]
                     nc.tensor.transpose(bank[:, c, u, :], src, ident[:])
 
-        def empty(key, words, copy=nc.scalar.copy):
-            copy(out=words, in_=full_bank(key)[:].rearrange("p c u r -> p c r u"))
+        def empty(key, words):
+            nc.scalar.copy(out=words, in_=full_bank(key)[:].rearrange("p c u r -> p c r u"))
 
         def as_words(grouped):
             return grouped.rearrange("p c r t -> p (c r t)").bitcast(F32).rearrange("p (c r u) -> p c r u", c=grouped.shape[1], u=2)
@@ -197,8 +198,8 @@ def tile_relative_offset_scores_d9_kernel(tc, X_bytes, X_scale, B, Q, v, R_bytes
         def turn_r(t):
             turn(new_bank(("r", t)), r_wide[t][:].bitcast(F32), 0, 0)
 
-        def empty_r(t, copy=nc.scalar.copy):
-            empty(("r", t), as_words(r_grouped[:])[:, :, P * t : P * t + P, :], copy)
+        def empty_r(t):
+            empty(("r", t), as_words(r_grouped[:])[:, :, P * t : P * t + P, :])
 
         def quantise_r(c):
             nc.vector.quantize_mx(out=r_codes[:, c, :].bitcast(FP8X4), scales=r_exps[:, c, :],
@@ -208,15 +209,10 @@ def tile_relative_offset_scores_d9_kernel(tc, X_bytes, X_scale, B, Q, v, R_bytes
         b_codes = keep.tile([P, KP, N], U32, align_bytes=MX_ALIGN)
         b_exps = keep.tile([P, KP, N], U8, align_bytes=MX_ALIGN)
 
-        def group_b(c, half=None):
+        def group_b(c, end):
             dst = b_grouped[c][:].rearrange("p (m i) t -> p m t i", i=4)
             src = b_raw[c][:].rearrange("p t (m i) -> p m t i", i=4)
-            if half is not None:
-                dst, src = (a[:, N // 8 * half : N // 8 * half + N // 8] for a in (dst, src))
-            if True:
-                nc.vector.tensor_scalar(out=dst, in0=src, scalar1=ROOT_D, scalar2=None, op0=MULT)
-            else:
-                nc.scalar.activation(out=dst, in_=src, func=COPY, scale=ROOT_D)
+            nc.vector.tensor_scalar(out=dst[:, 0 : end // 4], in0=src[:, 0 : end // 4], scalar1=ROOT_D, scalar2=None, op0=MULT)
 
         def weave_b(c, half):
             slots = flat(new_bank(("b", c, half))).bitcast(BF16).rearrange("p (n u e) -> p u e n", u=2, e=2)
@@ -224,12 +220,9 @@ def tile_relative_offset_scores_d9_kernel(tc, X_bytes, X_scale, B, Q, v, R_bytes
             for u in range(2):
                 nc.tensor.matmul(slots[:, u], lhsT=ident32[:], rhs=b_raw[c][:, 2 * u : 2 * u + 2, cols], start=True, stop=True)
 
-        def empty_b(c, half, vector=False):
+        def empty_b(c, half):
             words = b_grouped[c][:].rearrange("p n t -> p (n t)").bitcast(F32)[:, N * half : N * half + N]
-            if vector:
-                nc.vector.tensor_copy(out=words, in_=flat(full_bank(("b", c, half))))
-            else:
-                nc.scalar.copy(out=words, in_=flat(full_bank(("b", c, half))))
+            nc.scalar.copy(out=words, in_=flat(full_bank(("b", c, half))))
 
         def quantise_b(c):
             nc.vector.quantize_mx(out=b_codes[:, c, :].bitcast(FP8X4), scales=b_exps[:, c, :],
@@ -277,7 +270,7 @@ def tile_relative_offset_scores_d9_kernel(tc, X_bytes, X_scale, B, Q, v, R_bytes
                                     in1=v_all[:].rearrange("r (h u m) -> r h u m", u=2, m=8), op=ADD)
 
         def turn_x(i, half):
-            turn(new_bank(("x", i, half)), x_wide(i).bitcast(F32), 2 * half, scalar_passes(i) if i < CAST_FROM else 0)
+            turn(new_bank(("x", i, half)), x_wide(i).bitcast(F32), 2 * half, 0 if cast_first(i) else scalar_passes(i))
 
         def turn_c(i):
             bank = new_bank(("c", i))
@@ -287,15 +280,15 @@ def tile_relative_offset_scores_d9_kernel(tc, X_bytes, X_scale, B, Q, v, R_bytes
                     w = P * (DP * u + c)
                     nc.tensor.transpose(bank[:, c, u, :], words[:, w : w + P], ident[:])
 
-        def empty_x(i, half, copy=nc.scalar.copy):
+        def empty_x(i, half):
             if ("x_grouped", i) not in held:
                 held["x_grouped", i] = work.tile([P, KP, P, 4], BF16, name="x_grouped", bufs=TURNED_BUFS, align_bytes=64)
-            empty(("x", i, half), as_words(held["x_grouped", i][:])[:, 2 * half : 2 * half + 2], copy)
+            empty(("x", i, half), as_words(held["x_grouped", i][:])[:, 2 * half : 2 * half + 2])
 
-        def empty_c(i, copy=nc.scalar.copy):
+        def empty_c(i):
             c_grouped = work.tile([P, DP, P, 4], BF16, bufs=TURNED_BUFS, align_bytes=64)
             held["c_grouped", i] = c_grouped
-            empty(("c", i), as_words(c_grouped[:]), copy)
+            empty(("c", i), as_words(c_grouped[:]))
 
         def quantise_x(i):
             x_codes = work.tile([P, KP, P], U32, bufs=TURNED_BUFS, align_bytes=MX_ALIGN)
@@ -304,17 +297,6 @@ def tile_relative_offset_scores_d9_kernel(tc, X_bytes, X_scale, B, Q, v, R_bytes
                                   scales=x_exps[PLANE:].rearrange("p c r -> p (c r)"),
                                   in_=held.pop(("x_grouped", i))[:].rearrange("p c r t -> p (c r t)"))
             held["x_mx", i] = (x_codes, x_exps, b_codes, b_exps)
-
-        def quantise_x_half(i, half):
-            if ("x_mx", i) not in held:
-                x_codes = work.tile([P, KP, P], U32, bufs=TURNED_BUFS, align_bytes=MX_ALIGN)
-                x_exps = work.tile([P, KP, P], U8, bufs=TURNED_BUFS, align_bytes=MX_ALIGN)
-                held["x_mx", i] = (x_codes, x_exps, b_codes, b_exps)
-            x_codes, x_exps = held["x_mx", i][0:2]
-            two = slice(2 * half, 2 * half + 2)
-            nc.vector.quantize_mx(out=x_codes[:, two].rearrange("p c r -> p (c r)").bitcast(FP8X4),
-                                  scales=x_exps[PLANE:, two].rearrange("p c r -> p (c r)"),
-                                  in_=held["x_grouped", i][:, two].rearrange("p c r t -> p (c r t)"))
 
         def quantise_c(i):
             c_codes = work.tile([P, DP, P], U32, bufs=TURNED_BUFS, align_bytes=MX_ALIGN)
@@ -353,7 +335,6 @@ def tile_relative_offset_scores_d9_kernel(tc, X_bytes, X_scale, B, Q, v, R_bytes
             result = work.tile([P, N], F32, bufs=NT, align_bytes=64)
             scale_and_store(result, flat(full_bank(("sum", i))), i, slice(0, N))
 
-
         def turn_tile(i):
             turn_c(i)
             turn_x(i, 1)
@@ -384,8 +365,8 @@ def tile_relative_offset_scores_d9_kernel(tc, X_bytes, X_scale, B, Q, v, R_bytes
         turn_x(0, 0)
         widen_r(0)
         widen_r(1)
+        group_b(0, N // 2)
         widen_r(2)
-        group_b(0, 0)
         empty_x(0, 1)
         empty_v()
         empty_x(0, 0)
@@ -411,7 +392,7 @@ def tile_relative_offset_scores_d9_kernel(tc, X_bytes, X_scale, B, Q, v, R_bytes
         quantise_b(0)
         empty_b(1, 0)
         empty_b(1, 1)
-        group_b(2)
+        group_b(2, N)
         add_v(1)
         turn_c(0)
         turn_c(1)
@@ -440,27 +421,28 @@ def tile_relative_offset_scores_d9_kernel(tc, X_bytes, X_scale, B, Q, v, R_bytes
         multiply_x(0, 2, 4)
         quantise_tile(1)
         empty_tile(2)
-        for s in range(3, NT + 1):
-            if s + 1 < CAST_FROM:
-                widen_x_scalar(s + 1)
-            elif s + 1 < NT:
+
+        for s in range(HEAD_TILES - 1, NT):
+            if cast_first(s + 1):
                 scale_x(s + 1)
-            if CAST_FROM <= s + 2 < NT:
+            elif s + 1 < NT:
+                widen_x_scalar(s + 1)
+            if cast_first(s + 2):
                 cast_x(s + 2)
-            if s < NT:
-                turn_tile(s)
-                empty_tile(s)
+            turn_tile(s)
+            empty_tile(s)
             multiply_tile(s - 2)
             if s + 1 < NT:
                 widen_vector(s + 1)
-            if s == NT:
-                finish(s - 4)
             quantise_tile(s - 1)
-            if 3 < s < NT:
+            if s >= 4:
                 finish(s - 4)
-        finish(NT - 3)
-
         last = NT - 1
+        multiply_tile(last - 1)
+        finish(last - 3)
+        quantise_tile(last)
+        finish(last - 2)
+
         passes = [("c_mx", c) for c in range(DP)] + [("x_mx", c) for c in range(KP)]
         totals = []
         for lo, hi in LAST_PIECES:

@@ -20,7 +20,9 @@ WIDE_BUFS = 4
 TURNED_BUFS = 4
 PLANE = 8
 HEAD_TILES = 4
-CAST_FROM = 6
+SORT_FROM = 5
+SCALAR_PASSES = [2, 2, 2, 2, 1, 1, 2, 2, 1, 2, 2, 1]
+FINISH_LAG = 4
 MX_ALIGN = 256
 X_LOADS = [(1, 1)] + [(i, 2) for i in range(2, NT, 2)]
 Q_LOADS = [(0, 1), (1, 1), (2, 2)] + [(i, 4) for i in range(4, NT, 4)]
@@ -40,11 +42,11 @@ COPY = mybir.ActivationFunctionType.Copy
 
 
 def scalar_passes(i):
-    return 2 if i < HEAD_TILES or (i % 3 == 2 and i < NT - 1) else 1
+    return SCALAR_PASSES[i]
 
 
-def cast_first(i):
-    return CAST_FROM <= i < NT and scalar_passes(i) == 1
+def is_sorted(i):
+    return SORT_FROM <= i < NT
 
 
 def tile_relative_offset_scores_d9_kernel(tc, X_bytes, X_scale, B, Q, v, R_bytes, R_scale, g, out):
@@ -108,7 +110,7 @@ def tile_relative_offset_scores_d9_kernel(tc, X_bytes, X_scale, B, Q, v, R_bytes
         nc.scalar.activation(out=ones[:], in_=one[:].to_broadcast([P, P]), func=COPY)
         nc.scalar.activation(out=ident32[:], in_=ident[:], func=COPY, scale=ROOT_D)
         nc.sync.dma_start(out=x0_raw[0][:], in_=X_tiles[:, 0, 0 : K // 2])
-        nc.sync.dma_start(out=v_row[0:1, :], in_=v.rearrange("(o k) -> o k", o=1))
+        nc.sync.dma_start(out=v_row[0:1, 0:D], in_=v.rearrange("(o k) -> o k", o=1))
         load_b(0)
         load_r(2)
         nc.sync.dma_start(out=x_scales[:], in_=X_scale_rows[:, NB:])
@@ -165,22 +167,10 @@ def tile_relative_offset_scores_d9_kernel(tc, X_bytes, X_scale, B, Q, v, R_bytes
                                     in0=raw.bitcast(FP8).rearrange("r (h u m) -> r h u m", u=2, m=8),
                                     scalar1=scale, scalar2=None, op0=MULT)
 
-        def widen_words(wide, raw, scale, blk):
-            c, q = divmod(blk, PASS_BLOCKS)
-            words = wide.rearrange("r (c u p e) -> r c p u e", u=2, p=P, e=2)
-            nc.vector.tensor_scalar(out=words[:, c, 32 * q : 32 * q + 32],
-                                    in0=raw.bitcast(FP8).rearrange("r (p u e) -> r p u e", u=2, e=2),
-                                    scalar1=scale, scalar2=None, op0=MULT)
-
-        v_all = keep.tile([P, D], BF16, align_bytes=64)
-
         def spread_v():
             wide = flat(new_bank("v")).bitcast(BF16)
             for h in range(D // N):
                 nc.tensor.matmul(wide[:, N * h : N * h + N], lhsT=ones[:], rhs=v_row[:, N * h : N * h + N], start=True, stop=True)
-
-        def empty_v():
-            nc.scalar.copy(out=v_all[:].bitcast(F32), in_=flat(full_bank("v")))
 
         def spread_r_scales():
             nc.tensor.transpose(new_bank("r_scales")[:, 0, 0, :], r_column[:].to_broadcast([P, P]), ident[:])
@@ -240,37 +230,45 @@ def tile_relative_offset_scores_d9_kernel(tc, X_bytes, X_scale, B, Q, v, R_bytes
                 held["x_wide", i] = work.tile([P, K], BF16, name="x_wide", align_bytes=64)
             return held["x_wide", i][:]
 
-        def cast_x(i):
-            x_cast = work.tile([P, PASS], BF16, align_bytes=64)
-            held["x_cast", i] = x_cast
-            nc.scalar.copy(out=x_cast[:], in_=x_raw[i][:, 0:PASS].bitcast(FP8))
-
-        def scale_x(i):
-            x_cast = held.pop(("x_cast", i))
-            words = x_wide(i).rearrange("r (c u p e) -> r c p u e", u=2, p=P, e=2)
-            for blk in range(PASS_BLOCKS):
-                nc.scalar.activation(out=words[:, 0, 32 * blk : 32 * blk + 32], func=COPY, scale=x_block(i, blk)[1],
-                                     in_=x_cast[:, G * blk : G * blk + G].rearrange("r (p u e) -> r p u e", u=2, e=2))
+        def x_plain(i):
+            if not is_sorted(i):
+                return x_wide(i)
+            if ("x_plain", i) not in held:
+                held["x_plain", i] = work.tile([P, PASS * PLAIN_PASSES], BF16, name="x_plain", bufs=2, align_bytes=64)
+            return held["x_plain", i][:]
 
         def widen_x_scalar(i):
             for blk in range(PASS_BLOCKS * scalar_passes(i)):
                 raw, scale = x_block(i, blk)
-                nc.scalar.activation(out=x_wide(i)[:, G * blk : G * blk + G], in_=raw.bitcast(FP8), func=COPY, scale=scale)
+                nc.scalar.activation(out=x_plain(i)[:, G * blk : G * blk + G], in_=raw.bitcast(FP8), func=COPY, scale=scale)
+
+        def sort_x(i):
+            x_sorted = work.tile([P, PLAIN_PASSES, 2, P], F32, name=f"turned{i % 2}", bufs=1, align_bytes=64)
+            held["x_sorted", i] = x_sorted
+            nc.gpsimd.tensor_copy(out=x_sorted[:], in_=held.pop(("x_plain", i))[:].bitcast(F32).rearrange("r (c p u) -> r c u p", u=2, p=P))
 
         def widen_x_vector(i):
             for blk in range(PASS_BLOCKS * scalar_passes(i), NB):
-                widen = widen_words if blk < PASS_BLOCKS * PLAIN_PASSES else widen_runs
-                widen(x_wide(i), *x_block(i, blk), blk)
+                raw, scale = x_block(i, blk)
+                if blk < PASS_BLOCKS * PLAIN_PASSES:
+                    nc.vector.tensor_scalar(out=x_plain(i)[:, G * blk : G * blk + G], in0=raw.bitcast(FP8),
+                                            scalar1=scale, scalar2=None, op0=MULT)
+                else:
+                    widen_runs(x_wide(i), raw, scale, blk)
 
         def add_v(i):
             c_wide = work.tile([P, D], BF16, align_bytes=64)
             held["c_wide", i] = c_wide
             nc.vector.tensor_tensor(out=c_wide[:].rearrange("r (u h m) -> r h u m", u=2, m=8),
                                     in0=q_raw[i].rearrange("r (h u m) -> r h u m", u=2, m=8),
-                                    in1=v_all[:].rearrange("r (h u m) -> r h u m", u=2, m=8), op=ADD)
+                                    in1=flat(held["v"][0]).bitcast(BF16).rearrange("r (h u m) -> r h u m", u=2, m=8), op=ADD)
 
         def turn_x(i, half):
-            turn(new_bank(("x", i, half)), x_wide(i).bitcast(F32), 2 * half, 0 if cast_first(i) else scalar_passes(i))
+            bank = new_bank(("x", i, half))
+            if half == 0 and is_sorted(i):
+                turn(bank, held["x_sorted", i][:].rearrange("r c u p -> r (c u p)"), 0, 0)
+            else:
+                turn(bank, x_wide(i).bitcast(F32), 2 * half, PLAIN_PASSES)
 
         def turn_c(i):
             bank = new_bank(("c", i))
@@ -282,7 +280,7 @@ def tile_relative_offset_scores_d9_kernel(tc, X_bytes, X_scale, B, Q, v, R_bytes
 
         def empty_x(i, half):
             if ("x_grouped", i) not in held:
-                held["x_grouped", i] = work.tile([P, KP, P, 4], BF16, name="x_grouped", bufs=TURNED_BUFS, align_bytes=64)
+                held["x_grouped", i] = work.tile([P, KP, P, 4], BF16, name=f"turned{i % 2}", bufs=1, align_bytes=64)
             empty(("x", i, half), as_words(held["x_grouped", i][:])[:, 2 * half : 2 * half + 2])
 
         def empty_c(i):
@@ -297,6 +295,17 @@ def tile_relative_offset_scores_d9_kernel(tc, X_bytes, X_scale, B, Q, v, R_bytes
                                   scales=x_exps[PLANE:].rearrange("p c r -> p (c r)"),
                                   in_=held.pop(("x_grouped", i))[:].rearrange("p c r t -> p (c r t)"))
             held["x_mx", i] = (x_codes, x_exps, b_codes, b_exps)
+
+        def quantise_x_half(i, half):
+            if ("x_mx", i) not in held:
+                x_codes = work.tile([P, KP, P], U32, bufs=TURNED_BUFS, align_bytes=MX_ALIGN)
+                x_exps = work.tile([P, KP, P], U8, bufs=TURNED_BUFS, align_bytes=MX_ALIGN)
+                held["x_mx", i] = (x_codes, x_exps, b_codes, b_exps)
+            x_codes, x_exps = held["x_mx", i][:2]
+            two = slice(2 * half, 2 * half + 2)
+            nc.vector.quantize_mx(out=x_codes[:, two].rearrange("p c r -> p (c r)").bitcast(FP8X4),
+                                  scales=x_exps[PLANE:, two].rearrange("p c r -> p (c r)"),
+                                  in_=held["x_grouped", i][:, two].rearrange("p c r t -> p (c r t)"))
 
         def quantise_c(i):
             c_codes = work.tile([P, DP, P], U32, bufs=TURNED_BUFS, align_bytes=MX_ALIGN)
@@ -336,8 +345,8 @@ def tile_relative_offset_scores_d9_kernel(tc, X_bytes, X_scale, B, Q, v, R_bytes
             scale_and_store(result, flat(full_bank(("sum", i))), i, slice(0, N))
 
         def turn_tile(i):
-            turn_c(i)
             turn_x(i, 1)
+            turn_c(i)
             turn_x(i, 0)
 
         def empty_tile(i):
@@ -368,7 +377,6 @@ def tile_relative_offset_scores_d9_kernel(tc, X_bytes, X_scale, B, Q, v, R_bytes
         group_b(0, N // 2)
         widen_r(2)
         empty_x(0, 1)
-        empty_v()
         empty_x(0, 0)
         turn_r(0)
         weave_b(0, 1)
@@ -423,27 +431,33 @@ def tile_relative_offset_scores_d9_kernel(tc, X_bytes, X_scale, B, Q, v, R_bytes
         empty_tile(2)
 
         for s in range(HEAD_TILES - 1, NT):
-            if cast_first(s + 1):
-                scale_x(s + 1)
-            elif s + 1 < NT:
+            if s + 1 < NT:
                 widen_x_scalar(s + 1)
-            if cast_first(s + 2):
-                cast_x(s + 2)
             turn_tile(s)
             empty_tile(s)
             multiply_tile(s - 2)
             if s + 1 < NT:
-                widen_vector(s + 1)
-            quantise_tile(s - 1)
-            if s >= 4:
-                finish(s - 4)
+                widen_x_vector(s + 1)
+                if not is_sorted(s + 1):
+                    add_v(s + 1)
+            quantise_x(s - 1)
+            if is_sorted(s + 1):
+                sort_x(s + 1)
+            quantise_c(s - 1)
+            if is_sorted(s + 1):
+                add_v(s + 1)
+            if s >= FINISH_LAG:
+                finish(s - FINISH_LAG)
         last = NT - 1
         multiply_tile(last - 1)
-        finish(last - 3)
-        quantise_tile(last)
+        for i in range(NT - FINISH_LAG, last - 2):
+            finish(i)
+        quantise_x_half(last, 1)
+        quantise_c(last)
+        quantise_x_half(last, 0)
         finish(last - 2)
 
-        passes = [("c_mx", c) for c in range(DP)] + [("x_mx", c) for c in range(KP)]
+        passes = [("c_mx", c) for c in range(DP)] + [("x_mx", c) for c in reversed(range(KP))]
         totals = []
         for lo, hi in LAST_PIECES:
             total = flat(new_bank(("piece", lo)))[:, 0 : hi - lo]

@@ -20,9 +20,9 @@ WIDE_BUFS = 4
 TURNED_BUFS = 4
 PLANE = 8
 HEAD_TILES = 4
-SORT_FROM = 5
-SCALAR_PASSES = [2, 2, 2, 2, 1, 1, 2, 2, 1, 2, 2, 1]
-FINISH_LAG = 4
+SORT_FROM = 4
+SCALAR_PASSES = [2, 2, 2, 2, 0, 2, 2, 2, 1, 2, 2, 2]
+FINISH_LAG = 3
 MX_ALIGN = 256
 X_LOADS = [(1, 1)] + [(i, 2) for i in range(2, NT, 2)]
 Q_LOADS = [(0, 1), (1, 1), (2, 2)] + [(i, 4) for i in range(4, NT, 4)]
@@ -243,12 +243,13 @@ def tile_relative_offset_scores_d9_kernel(tc, X_bytes, X_scale, B, Q, v, R_bytes
                 nc.scalar.activation(out=x_plain(i)[:, G * blk : G * blk + G], in_=raw.bitcast(FP8), func=COPY, scale=scale)
 
         def sort_x(i):
-            x_sorted = work.tile([P, PLAIN_PASSES, 2, P], F32, name=f"turned{i % 2}", bufs=1, align_bytes=64)
+            x_sorted = work.tile([P, PLAIN_PASSES, 2, P], F32, name=f"turned{i % 2}" if i > SORT_FROM else "first_sorted", bufs=1, align_bytes=64)
             held["x_sorted", i] = x_sorted
             nc.gpsimd.tensor_copy(out=x_sorted[:], in_=held.pop(("x_plain", i))[:].bitcast(F32).rearrange("r (c p u) -> r c u p", u=2, p=P))
 
         def widen_x_vector(i):
-            for blk in range(PASS_BLOCKS * scalar_passes(i), NB):
+            first = PASS_BLOCKS * PLAIN_PASSES
+            for blk in [*range(first, NB), *range(PASS_BLOCKS * scalar_passes(i), first)]:
                 raw, scale = x_block(i, blk)
                 if blk < PASS_BLOCKS * PLAIN_PASSES:
                     nc.vector.tensor_scalar(out=x_plain(i)[:, G * blk : G * blk + G], in0=raw.bitcast(FP8),
@@ -260,8 +261,8 @@ def tile_relative_offset_scores_d9_kernel(tc, X_bytes, X_scale, B, Q, v, R_bytes
             c_wide = work.tile([P, D], BF16, align_bytes=64)
             held["c_wide", i] = c_wide
             nc.vector.tensor_tensor(out=c_wide[:].rearrange("r (u h m) -> r h u m", u=2, m=8),
-                                    in0=q_raw[i].rearrange("r (h u m) -> r h u m", u=2, m=8),
-                                    in1=flat(held["v"][0]).bitcast(BF16).rearrange("r (h u m) -> r h u m", u=2, m=8), op=ADD)
+                                    in0=flat(held["v"][0]).bitcast(BF16).rearrange("r (h u m) -> r h u m", u=2, m=8),
+                                    in1=q_raw[i].rearrange("r (h u m) -> r h u m", u=2, m=8), op=ADD)
 
         def turn_x(i, half):
             bank = new_bank(("x", i, half))
@@ -408,6 +409,7 @@ def tile_relative_offset_scores_d9_kernel(tc, X_bytes, X_scale, B, Q, v, R_bytes
         quantise_r(1)
         widen_x_vector(2)
         quantise_b(1)
+        multiply_x(0, 0, 1)
         weave_b(3, 0)
         empty_x(1, 1)
         weave_b(3, 1)
@@ -415,7 +417,7 @@ def tile_relative_offset_scores_d9_kernel(tc, X_bytes, X_scale, B, Q, v, R_bytes
         empty_c(0)
         add_v(2)
         widen_x_scalar(2)
-        multiply_x(0, 0, 2)
+        multiply_x(0, 1, 2)
         empty_b(3, 0)
         empty_b(3, 1)
         quantise_b(2)
@@ -427,10 +429,20 @@ def tile_relative_offset_scores_d9_kernel(tc, X_bytes, X_scale, B, Q, v, R_bytes
         widen_x_scalar(3)
         multiply_c(0)
         multiply_x(0, 2, 4)
-        quantise_tile(1)
+        quantise_x(1)
         empty_tile(2)
+        turn_tile(3)
+        empty_tile(3)
+        widen_x_vector(4)
+        sort_x(4)
+        quantise_c(1)
+        multiply_x(1, 0, KP)
+        multiply_c(1)
+        add_v(4)
+        add_v(5)
+        quantise_tile(2)
 
-        for s in range(HEAD_TILES - 1, NT):
+        for s in range(4, NT):
             if s + 1 < NT:
                 widen_x_scalar(s + 1)
             turn_tile(s)
@@ -438,20 +450,19 @@ def tile_relative_offset_scores_d9_kernel(tc, X_bytes, X_scale, B, Q, v, R_bytes
             multiply_tile(s - 2)
             if s + 1 < NT:
                 widen_x_vector(s + 1)
-                if not is_sorted(s + 1):
-                    add_v(s + 1)
             quantise_x(s - 1)
-            if is_sorted(s + 1):
+            if s + 1 < NT:
                 sort_x(s + 1)
             quantise_c(s - 1)
-            if is_sorted(s + 1):
-                add_v(s + 1)
-            if s >= FINISH_LAG:
-                finish(s - FINISH_LAG)
+            if s + 2 < NT:
+                add_v(s + 2)
+                finish(s - 4)
+            elif s + 1 < NT:
+                finish(s - 4)
+                finish(s - 3)
         last = NT - 1
         multiply_tile(last - 1)
-        for i in range(NT - FINISH_LAG, last - 2):
-            finish(i)
+        finish(last - 3)
         quantise_x_half(last, 1)
         quantise_c(last)
         quantise_x_half(last, 0)

@@ -21,10 +21,10 @@ TURNED_BUFS = 4
 PLANE = 8
 HEAD_TILES = 4
 SORT_FROM = 4
-SCALAR_PASSES = [2, 2, 2, 2, 0, 2, 2, 2, 1, 2, 2, 2]
+SCALAR_PASSES = [1, 2, 2, 2, 1, 2, 2, 2, 1, 2, 2, 2]
 FINISH_LAG = 3
 MX_ALIGN = 256
-X_LOADS = [(1, 1)] + [(i, 2) for i in range(2, NT, 2)]
+X_LOADS = [(1, 1), (2, 1), (3, 1)] + [(i, 2) for i in range(4, NT, 2)]
 Q_LOADS = [(0, 1), (1, 1), (2, 2)] + [(i, 4) for i in range(4, NT, 4)]
 LAST_PIECES = [(0, N // 2), (N // 2, 3 * N // 4), (3 * N // 4, N)]
 
@@ -106,21 +106,22 @@ def tile_relative_offset_scores_d9_kernel(tc, X_bytes, X_scale, B, Q, v, R_bytes
         nc.scalar.dma_start(out=x0_scales[:], in_=X_scale_rows[:, 0:NB])
         nc.scalar.dma_start(out=r_column[0 : RT * RB, :], in_=R_scale.rearrange("a (b o) -> (a b) o", o=1))
         nc.sync.dma_start(out=x0_raw[1][:], in_=X_tiles[:, 0, K // 2 :])
-        load_r(0)
+        nc.sync.dma_start(out=x0_raw[0][:], in_=X_tiles[:, 0, 0 : K // 2])
         nc.scalar.activation(out=ones[:], in_=one[:].to_broadcast([P, P]), func=COPY)
         nc.scalar.activation(out=ident32[:], in_=ident[:], func=COPY, scale=ROOT_D)
-        nc.sync.dma_start(out=x0_raw[0][:], in_=X_tiles[:, 0, 0 : K // 2])
+        load_r(0)
         nc.sync.dma_start(out=v_row[0:1, 0:D], in_=v.rearrange("(o k) -> o k", o=1))
-        load_b(0)
-        load_r(2)
         nc.sync.dma_start(out=x_scales[:], in_=X_scale_rows[:, NB:])
         load_x(1)
-        load_b(1)
+        load_r(2)
+        load_b(0)
         load_q(0)
+        load_b(1)
+        load_x(2)
         load_b(2)
         load_q(1)
-        load_x(2)
         load_b(3)
+        load_x(3)
         load_q(2)
         load_x(4)
         load_q(4)
@@ -375,74 +376,101 @@ def tile_relative_offset_scores_d9_kernel(tc, X_bytes, X_scale, B, Q, v, R_bytes
         turn_x(0, 0)
         widen_r(0)
         widen_r(1)
-        group_b(0, N // 2)
+        widen_x_vector(1)
         widen_r(2)
+        widen_r(3)
         empty_x(0, 1)
+        widen_x_scalar(1)
         empty_x(0, 0)
         turn_r(0)
-        weave_b(0, 1)
         turn_r(1)
+        weave_b(0, 1)
         turn_r(2)
-        widen_r(3)
-        widen_x_vector(1)
-        empty_r(0)
-        empty_b(0, 1)
-        widen_x_scalar(1)
         turn_r(3)
-        turn_x(1, 1)
-        weave_b(1, 0)
-        weave_b(1, 1)
+        empty_r(0)
         empty_r(1)
+        empty_b(0, 1)
         empty_r(2)
         empty_r(3)
         turn_x(1, 0)
+        turn_x(1, 1)
+        weave_b(1, 0)
+        weave_b(1, 1)
         quantise_x(0)
+        group_b(0, N // 2)
         add_v(0)
+        widen_x_vector(2)
         quantise_b(0)
+        turn_c(0)
+        turn_x(2, 1)
+        empty_x(1, 0)
+        empty_x(1, 1)
         empty_b(1, 0)
+        widen_x_scalar(2)
         empty_b(1, 1)
+        empty_c(0)
         group_b(2, N)
         add_v(1)
-        turn_c(0)
-        turn_c(1)
         quantise_r(0)
         quantise_r(1)
-        widen_x_vector(2)
-        quantise_b(1)
-        multiply_x(0, 0, 1)
         weave_b(3, 0)
-        empty_x(1, 1)
+        turn_c(1)
         weave_b(3, 1)
-        empty_x(1, 0)
-        empty_c(0)
-        add_v(2)
-        widen_x_scalar(2)
-        multiply_x(0, 1, 2)
-        empty_b(3, 0)
-        empty_b(3, 1)
-        quantise_b(2)
-        turn_tile(2)
-        empty_c(1)
-        quantise_c(0)
-        widen_vector(3)
-        quantise_b(3)
-        widen_x_scalar(3)
-        multiply_c(0)
-        multiply_x(0, 2, 4)
         quantise_x(1)
-        empty_tile(2)
-        turn_tile(3)
-        empty_tile(3)
+        quantise_b(1)
+        add_v(2)
+        quantise_b(2)
+        multiply_x(0, 0, 2)
+        multiply_x(1, 0, 2)
+        widen_x_vector(3)
+        empty_x(2, 1)
+        empty_b(3, 0)
+        empty_c(1)
+        empty_b(3, 1)
+        turn_c(2)
+        turn_x(2, 0)
+        turn_x(3, 1)
+        quantise_c(0)
+        quantise_c(1)
+        quantise_b(3)
+        add_v(3)
+        widen_x_scalar(3)
+        widen_x_scalar(4)
+        multiply_c(0)
+        multiply_c(1)
+        multiply_x(0, 2, 3)
+        multiply_x(1, 2, 3)
+        multiply_x(0, 3, 4)
+        multiply_x(1, 3, 4)
+        empty_c(2)
+        empty_x(2, 0)
         widen_x_vector(4)
         sort_x(4)
-        quantise_c(1)
-        multiply_x(1, 0, KP)
-        multiply_c(1)
+        quantise_c(2)
         add_v(4)
         add_v(5)
-        quantise_tile(2)
-
-        for s in range(4, NT):
+        quantise_x(2)
+        empty_x(3, 1)
+        turn_c(3)
+        turn_x(3, 0)
+        turn_x(4, 1)
+        turn_c(4)
+        turn_x(4, 0)
+        widen_x_scalar(5)
+        empty_x(3, 0)
+        empty_c(3)
+        multiply_c(2)
+        multiply_x(2, 0, 4)
+        empty_x(4, 1)
+        empty_c(4)
+        empty_x(4, 0)
+        widen_x_vector(5)
+        quantise_x(3)
+        sort_x(5)
+        quantise_c(3)
+        add_v(6)
+        finish(0)
+        for s in range(5, NT):
             if s + 1 < NT:
                 widen_x_scalar(s + 1)
             turn_tile(s)

@@ -20,12 +20,10 @@ WIDE_BUFS = 4
 TURNED_BUFS = 4
 PLANE = 8
 HEAD_TILES = 4
-SORT_FROM = 4
-SCALAR_PASSES = [1, 2, 2, 2, 1, 2, 2, 2, 1, 2, 2, 2]
-FINISH_LAG = 3
+C_BUFS = 3
+RESULT_BUFS = 8
 MX_ALIGN = 256
 X_LOADS = [(1, 1), (2, 1), (3, 1)] + [(i, 2) for i in range(4, NT, 2)]
-Q_LOADS = [(0, 1), (1, 1), (2, 2)] + [(i, 4) for i in range(4, NT, 4)]
 LAST_PIECES = [(0, N // 2), (N // 2, 3 * N // 4), (3 * N // 4, N)]
 
 FLOPS = 2 * T * N * (K + D)
@@ -41,14 +39,6 @@ ADD = mybir.AluOpType.add
 COPY = mybir.ActivationFunctionType.Copy
 
 
-def scalar_passes(i):
-    return SCALAR_PASSES[i]
-
-
-def is_sorted(i):
-    return SORT_FROM <= i < NT
-
-
 def tile_relative_offset_scores_d9_kernel(tc, X_bytes, X_scale, B, Q, v, R_bytes, R_scale, g, out):
     nc = tc.nc
     with ExitStack() as ctx:
@@ -57,13 +47,11 @@ def tile_relative_offset_scores_d9_kernel(tc, X_bytes, X_scale, B, Q, v, R_bytes
         psum = ctx.enter_context(tc.psum_pool(name="psum", bufs=1))
         ctx.enter_context(tc.manual_schedule())
 
-        ones = keep.tile([P, P], BF16, align_bytes=64)
-        one = keep.tile([P, 1], F32, align_bytes=64)
         r_column = keep.tile([P, 1], F32, align_bytes=64)
         nc.gpsimd.memset(r_column[:], 0.0)
-        nc.vector.memset(one[:], 1.0)
-        v_row = keep.tile([P, D], BF16, align_bytes=64)
-        nc.vector.memset(v_row[:], 0.0)
+        v_rows = keep.tile([P, PASS], BF16, align_bytes=64)
+        nc.vector.memset(v_rows[:], 0.0)
+        v_turned = keep.tile([P, DP, P, 4], BF16, align_bytes=64)
         ident = keep.tile([P, P], F32, align_bytes=64)
         make_identity(nc, ident[:])
         ident32 = keep.tile([P, P], BF16, align_bytes=64)
@@ -74,9 +62,8 @@ def tile_relative_offset_scores_d9_kernel(tc, X_bytes, X_scale, B, Q, v, R_bytes
         r_lot = [keep.tile([P, 2, D], U8, name=f"r_raw{h}", align_bytes=64) for h in range(RT // 2)]
         r_raw = [r_lot[t // 2][:, t % 2, :] for t in range(RT)]
         x_lot = {lo: keep.tile([P, n, K], U8, name=f"x_raw{lo}", align_bytes=64) for lo, n in X_LOADS}
-        q_lot = {lo: keep.tile([P, n, D], BF16, name=f"q_raw{lo}", align_bytes=64) for lo, n in Q_LOADS}
+        plain = [keep.tile([P, PLAIN_PASSES * PASS + D], BF16, name=f"plain{i}", align_bytes=64) for i in range(NT)]
         x_raw = {lo + j: x_lot[lo][:, j, :] for lo, n in X_LOADS for j in range(n)}
-        q_raw = {lo + j: q_lot[lo][:, j, :] for lo, n in Q_LOADS for j in range(n)}
         b_raw = [keep.tile([P, 4, N], BF16, name=f"b_raw{c}", align_bytes=64) for c in range(KP)]
         x0_scales = keep.tile([P, NB], F32, align_bytes=64)
         x0_raw = [keep.tile([P, K // 2], U8, name=f"x0_raw{h}", align_bytes=64) for h in range(2)]
@@ -91,7 +78,7 @@ def tile_relative_offset_scores_d9_kernel(tc, X_bytes, X_scale, B, Q, v, R_bytes
             nc.sync.dma_start(out=x_lot[i][:], in_=X_tiles[:, i : i + dict(X_LOADS)[i], :])
 
         def load_q(i):
-            nc.sync.dma_start(out=q_lot[i][:], in_=Q_tiles[:, i : i + dict(Q_LOADS)[i], :])
+            nc.sync.dma_start(out=plain[i][:, PLAIN_PASSES * PASS :], in_=Q_tiles[:, i, :])
 
         def load_r(t):
             nc.sync.dma_start(out=r_lot[t // 2][:], in_=R_bytes.rearrange("(t p) k -> p t k", p=P)[:, t : t + 2, :])
@@ -107,10 +94,9 @@ def tile_relative_offset_scores_d9_kernel(tc, X_bytes, X_scale, B, Q, v, R_bytes
         nc.scalar.dma_start(out=r_column[0 : RT * RB, :], in_=R_scale.rearrange("a (b o) -> (a b) o", o=1))
         nc.sync.dma_start(out=x0_raw[1][:], in_=X_tiles[:, 0, K // 2 :])
         nc.sync.dma_start(out=x0_raw[0][:], in_=X_tiles[:, 0, 0 : K // 2])
-        nc.scalar.activation(out=ones[:], in_=one[:].to_broadcast([P, P]), func=COPY)
         nc.scalar.activation(out=ident32[:], in_=ident[:], func=COPY, scale=ROOT_D)
         load_r(0)
-        nc.sync.dma_start(out=v_row[0:1, 0:D], in_=v.rearrange("(o k) -> o k", o=1))
+        nc.sync.dma_start(out=v_rows[0:DP, :], in_=v.rearrange("(c k) -> c k", c=DP))
         nc.sync.dma_start(out=x_scales[:], in_=X_scale_rows[:, NB:])
         load_x(1)
         load_r(2)
@@ -123,13 +109,17 @@ def tile_relative_offset_scores_d9_kernel(tc, X_bytes, X_scale, B, Q, v, R_bytes
         load_b(3)
         load_x(3)
         load_q(2)
+        load_q(3)
         load_x(4)
         load_q(4)
+        load_q(5)
         load_x(6)
         nc.sync.dma_start(out=g_all[:], in_=g.partition_broadcast(P))
-        load_x(8)
-        load_q(8)
-        load_x(10)
+        for i in range(6, NT, 2):
+            load_q(i)
+            load_q(i + 1)
+            if i + 2 < NT:
+                load_x(i + 2)
 
         held = {}
         free_banks = list(range(BANKS))
@@ -148,18 +138,30 @@ def tile_relative_offset_scores_d9_kernel(tc, X_bytes, X_scale, B, Q, v, R_bytes
         def flat(bank):
             return bank[:].rearrange("p c u r -> p (c u r)")
 
-        def turn(bank, words, first, stepped):
-            for c in range(2):
-                for u in range(2):
-                    w = 2 * P * (first + c)
-                    src = words[:, w + u : w + 2 * P : 2] if first + c < stepped else words[:, w + P * u : w + P * u + P]
-                    nc.tensor.transpose(bank[:, c, u, :], src, ident[:])
+        def turn(key, words, u_first=False):
+            def one(c, u):
+                bank = held[key][0] if key in held else new_bank(key)
+                nc.tensor.transpose(bank[:, u, c, :] if u_first else bank[:, c, u, :], words(c, u), ident[:])
+            return [lambda c=c, u=u: one(c, u) for c in range(2) for u in range(2)]
+
+        def run(calls):
+            for call in calls:
+                call()
+
+        def stepped(words, c, u):
+            return words[:, 2 * P * c + u : 2 * P * c + 2 * P : 2]
 
         def empty(key, words):
             nc.scalar.copy(out=words, in_=full_bank(key)[:].rearrange("p c u r -> p c r u"))
 
         def as_words(grouped):
             return grouped.rearrange("p c r t -> p (c r t)").bitcast(F32).rearrange("p (c r u) -> p c r u", c=grouped.shape[1], u=2)
+
+        def widen_plain(wide, raw, scale, on_scalar):
+            if on_scalar:
+                nc.scalar.activation(out=wide, in_=raw.bitcast(FP8), func=COPY, scale=scale)
+            else:
+                nc.vector.tensor_scalar(out=wide, in0=raw.bitcast(FP8), scalar1=scale, scalar2=None, op0=MULT)
 
         def widen_runs(wide, raw, scale, blk):
             c, q = divmod(blk, PASS_BLOCKS)
@@ -168,10 +170,14 @@ def tile_relative_offset_scores_d9_kernel(tc, X_bytes, X_scale, B, Q, v, R_bytes
                                     in0=raw.bitcast(FP8).rearrange("r (h u m) -> r h u m", u=2, m=8),
                                     scalar1=scale, scalar2=None, op0=MULT)
 
-        def spread_v():
-            wide = flat(new_bank("v")).bitcast(BF16)
-            for h in range(D // N):
-                nc.tensor.matmul(wide[:, N * h : N * h + N], lhsT=ones[:], rhs=v_row[:, N * h : N * h + N], start=True, stop=True)
+        def turn_v():
+            bank = new_bank("v")
+            for u in range(2):
+                nc.tensor.transpose(bank[:, u, 0, :], v_rows[:].bitcast(F32)[:, u::2], ident[:])
+
+        def repeat_v():
+            column = full_bank("v")[:, :, 0, 0:DP].rearrange("p u (c o) -> p c o u", o=1)
+            nc.scalar.copy(out=as_words(v_turned[:]), in_=column.to_broadcast([P, DP, P, 2]))
 
         def spread_r_scales():
             nc.tensor.transpose(new_bank("r_scales")[:, 0, 0, :], r_column[:].to_broadcast([P, P]), ident[:])
@@ -182,12 +188,13 @@ def tile_relative_offset_scores_d9_kernel(tc, X_bytes, X_scale, B, Q, v, R_bytes
         r_codes = keep.tile([P, DP, N], U32, align_bytes=MX_ALIGN)
         r_exps = keep.tile([P, DP, N], U8, align_bytes=MX_ALIGN)
 
-        def widen_r(t):
+        def widen_r(t, on_scalar=False):
             for blk in range(RB):
-                widen_runs(r_wide[t][:], r_raw[t][:, G * blk : G * blk + G], r_scales[:, RB * t + blk : RB * t + blk + 1], blk)
+                widen_plain(r_wide[t][:, G * blk : G * blk + G], r_raw[t][:, G * blk : G * blk + G],
+                            r_scales[:, RB * t + blk : RB * t + blk + 1], on_scalar)
 
         def turn_r(t):
-            turn(new_bank(("r", t)), r_wide[t][:].bitcast(F32), 0, 0)
+            return turn(("r", t), lambda c, u: stepped(r_wide[t][:].bitcast(F32), c, u))
 
         def empty_r(t):
             empty(("r", t), as_words(r_grouped[:])[:, :, P * t : P * t + P, :])
@@ -205,11 +212,20 @@ def tile_relative_offset_scores_d9_kernel(tc, X_bytes, X_scale, B, Q, v, R_bytes
             src = b_raw[c][:].rearrange("p t (m i) -> p m t i", i=4)
             nc.vector.tensor_scalar(out=dst[:, 0 : end // 4], in0=src[:, 0 : end // 4], scalar1=ROOT_D, scalar2=None, op0=MULT)
 
-        def weave_b(c, half):
+        def group_b_scalar(c, half):
+            cols = slice(N // 8 * half, N // 8 * half + N // 8)
+            dst = b_grouped[c][:].rearrange("p (m i) t -> p m t i", i=4)
+            src = b_raw[c][:].rearrange("p t (m i) -> p m t i", i=4)
+            nc.scalar.activation(out=dst[:, cols], in_=src[:, cols], func=COPY, scale=ROOT_D)
+
+        def weave_b(c, half, beside):
             slots = flat(new_bank(("b", c, half))).bitcast(BF16).rearrange("p (n u e) -> p u e n", u=2, e=2)
-            cols = slice(N // 2 * half, N // 2 * half + N // 2)
-            for u in range(2):
-                nc.tensor.matmul(slots[:, u], lhsT=ident32[:], rhs=b_raw[c][:, 2 * u : 2 * u + 2, cols], start=True, stop=True)
+            for step, transpose in enumerate(beside):
+                u, quarter = divmod(step, 2)
+                lo = N // 4 * quarter
+                nc.tensor.matmul(slots[:, u, :, lo : lo + N // 4], lhsT=ident32[:],
+                                 rhs=b_raw[c][:, 2 * u : 2 * u + 2, N // 2 * half + lo : N // 2 * half + lo + N // 4], start=True, stop=True)
+                transpose()
 
         def empty_b(c, half):
             words = b_grouped[c][:].rearrange("p n t -> p (n t)").bitcast(F32)[:, N * half : N * half + N]
@@ -226,69 +242,78 @@ def tile_relative_offset_scores_d9_kernel(tc, X_bytes, X_scale, B, Q, v, R_bytes
             col = NB * (i - 1) + blk
             return x_raw[i][:, G * blk : G * blk + G], x_scales[:, col : col + 1]
 
-        def x_wide(i):
-            if ("x_wide", i) not in held:
-                held["x_wide", i] = work.tile([P, K], BF16, name="x_wide", align_bytes=64)
-            return held["x_wide", i][:]
-
-        def x_plain(i):
-            if not is_sorted(i):
-                return x_wide(i)
-            if ("x_plain", i) not in held:
-                held["x_plain", i] = work.tile([P, PASS * PLAIN_PASSES], BF16, name="x_plain", bufs=2, align_bytes=64)
-            return held["x_plain", i][:]
+        def widen_x_plain(i, c, on_scalar):
+            for blk in range(PASS_BLOCKS * c, PASS_BLOCKS * c + PASS_BLOCKS):
+                raw, scale = x_block(i, blk)
+                widen_plain(plain[i][:, G * blk : G * blk + G], raw, scale, on_scalar)
 
         def widen_x_scalar(i):
-            for blk in range(PASS_BLOCKS * scalar_passes(i)):
-                raw, scale = x_block(i, blk)
-                nc.scalar.activation(out=x_plain(i)[:, G * blk : G * blk + G], in_=raw.bitcast(FP8), func=COPY, scale=scale)
+            for c in range(PLAIN_PASSES):
+                widen_x_plain(i, c, True)
 
-        def sort_x(i):
-            x_sorted = work.tile([P, PLAIN_PASSES, 2, P], F32, name=f"turned{i % 2}" if i > SORT_FROM else "first_sorted", bufs=1, align_bytes=64)
-            held["x_sorted", i] = x_sorted
-            nc.gpsimd.tensor_copy(out=x_sorted[:], in_=held.pop(("x_plain", i))[:].bitcast(F32).rearrange("r (c p u) -> r c u p", u=2, p=P))
+        def x_runs(i):
+            if ("x_runs", i) not in held:
+                held["x_runs", i] = work.tile([P, K - PLAIN_PASSES * PASS], BF16, name="x_runs", align_bytes=64)
+            return held["x_runs", i][:]
+
+        def widen_x_runs(i, c):
+            for blk in range(PASS_BLOCKS * c, PASS_BLOCKS * c + PASS_BLOCKS):
+                raw, scale = x_block(i, blk)
+                widen_runs(x_runs(i), raw, scale, blk - PASS_BLOCKS * PLAIN_PASSES)
+
+        def widen_x_runs_scalar(i, c):
+            lying = work.tile([P, PASS], BF16, bufs=1, align_bytes=64)
+            for q in range(PASS_BLOCKS):
+                raw, scale = x_block(i, PASS_BLOCKS * c + q)
+                widen_plain(lying[:, G * q : G * q + G], raw, scale, True)
+            runs = x_runs(i)[:, PASS * (c - PLAIN_PASSES) : PASS * (c - PLAIN_PASSES + 1)]
+            nc.scalar.copy(out=runs.rearrange("r (u h m) -> r u h m", u=2, m=8), in_=lying[:].rearrange("r (h u m) -> r u h m", u=2, m=8))
 
         def widen_x_vector(i):
-            first = PASS_BLOCKS * PLAIN_PASSES
-            for blk in [*range(first, NB), *range(PASS_BLOCKS * scalar_passes(i), first)]:
-                raw, scale = x_block(i, blk)
-                if blk < PASS_BLOCKS * PLAIN_PASSES:
-                    nc.vector.tensor_scalar(out=x_plain(i)[:, G * blk : G * blk + G], in0=raw.bitcast(FP8),
-                                            scalar1=scale, scalar2=None, op0=MULT)
-                else:
-                    widen_runs(x_wide(i), raw, scale, blk)
+            for c in range(PLAIN_PASSES, KP):
+                widen_x_runs(i, c)
 
-        def add_v(i):
-            c_wide = work.tile([P, D], BF16, align_bytes=64)
-            held["c_wide", i] = c_wide
-            nc.vector.tensor_tensor(out=c_wide[:].rearrange("r (u h m) -> r h u m", u=2, m=8),
-                                    in0=flat(held["v"][0]).bitcast(BF16).rearrange("r (h u m) -> r h u m", u=2, m=8),
-                                    in1=q_raw[i].rearrange("r (h u m) -> r h u m", u=2, m=8), op=ADD)
+        def sort_words(i, first, end, name):
+            ordered = work.tile([P, end - first, 2, P], F32, name=name, bufs=1, align_bytes=64)
+            words = plain[i][:].bitcast(F32)[:, 2 * P * first : 2 * P * end]
+            nc.gpsimd.tensor_copy(out=ordered[:], in_=words.rearrange("r (c p u) -> r c u p", u=2, p=P))
+            for c in range(first, end):
+                held["sorted", i, c] = ordered[:, c - first]
+
+        def sort_tile(i):
+            sort_words(i, 0, PLAIN_PASSES + DP, f"turned{i % 2}")
+
+        def sort_q(i, name):
+            sort_words(i, PLAIN_PASSES, PLAIN_PASSES + DP, name)
+
+        def sort_x(i, name):
+            sort_words(i, 0, PLAIN_PASSES, name)
+
+        def plain_words(i, c, u):
+            if ("sorted", i, c) in held:
+                return held["sorted", i, c][:, u, :]
+            return stepped(plain[i][:].bitcast(F32), c, u)
 
         def turn_x(i, half):
-            bank = new_bank(("x", i, half))
-            if half == 0 and is_sorted(i):
-                turn(bank, held["x_sorted", i][:].rearrange("r c u p -> r (c u p)"), 0, 0)
-            else:
-                turn(bank, x_wide(i).bitcast(F32), 2 * half, PLAIN_PASSES)
+            if half == 0:
+                return turn(("x", i, 0), lambda c, u: plain_words(i, c, u))
+            return turn(("x", i, 1), lambda c, u: x_runs(i).bitcast(F32)[:, P * (2 * c + u) : P * (2 * c + u + 1)])
 
         def turn_c(i):
-            bank = new_bank(("c", i))
-            words = held.pop(("c_wide", i))[:].bitcast(F32)
-            for c in range(DP):
-                for u in range(2):
-                    w = P * (DP * u + c)
-                    nc.tensor.transpose(bank[:, c, u, :], words[:, w : w + P], ident[:])
+            return turn(("c", i), lambda c, u: plain_words(i, PLAIN_PASSES + c, u), u_first=True)
 
         def empty_x(i, half):
             if ("x_grouped", i) not in held:
                 held["x_grouped", i] = work.tile([P, KP, P, 4], BF16, name=f"turned{i % 2}", bufs=1, align_bytes=64)
             empty(("x", i, half), as_words(held["x_grouped", i][:])[:, 2 * half : 2 * half + 2])
 
-        def empty_c(i):
-            c_grouped = work.tile([P, DP, P, 4], BF16, bufs=TURNED_BUFS, align_bytes=64)
+        def add_v(i):
+            c_grouped = work.tile([P, DP, P, 4], BF16, name=f"c_grouped{i % C_BUFS}", bufs=1, align_bytes=64)
             held["c_grouped", i] = c_grouped
-            empty(("c", i), as_words(c_grouped[:]))
+            pairs = "p c r (u e) -> p (c r) u e"
+            nc.vector.tensor_tensor(out=c_grouped[:].rearrange(pairs, e=2),
+                                    in0=flat(full_bank(("c", i))).bitcast(BF16).rearrange("p (u x e) -> p x u e", u=2, e=2),
+                                    in1=v_turned[:].rearrange(pairs, e=2), op=ADD)
 
         def quantise_x(i):
             x_codes = work.tile([P, KP, P], U32, bufs=TURNED_BUFS, align_bytes=MX_ALIGN)
@@ -343,37 +368,27 @@ def tile_relative_offset_scores_d9_kernel(tc, X_bytes, X_scale, B, Q, v, R_bytes
             nc.sync.dma_start(out=out_tiles[:, i, cols], in_=result[:])
 
         def finish(i):
-            result = work.tile([P, N], F32, bufs=NT, align_bytes=64)
+            result = work.tile([P, N], F32, bufs=RESULT_BUFS, align_bytes=64)
             scale_and_store(result, flat(full_bank(("sum", i))), i, slice(0, N))
 
         def turn_tile(i):
-            turn_x(i, 1)
-            turn_c(i)
-            turn_x(i, 0)
+            run(turn_c(i) + turn_x(i, 0) + turn_x(i, 1))
 
         def empty_tile(i):
-            empty_x(i, 1)
-            empty_c(i)
             empty_x(i, 0)
-
-        def widen_vector(i):
-            widen_x_vector(i)
-            add_v(i)
-
-        def quantise_tile(i):
-            quantise_x(i)
-            quantise_c(i)
+            empty_x(i, 1)
 
         def multiply_tile(i):
-            multiply_c(i)
             multiply_x(i, 0, KP)
+            multiply_c(i)
 
         spread_r_scales()
         widen_x_vector(0)
-        widen_x_scalar(0)
-        turn_x(0, 1)
-        spread_v()
-        turn_x(0, 0)
+        widen_x_plain(0, 1, False)
+        widen_x_plain(0, 0, True)
+        run(turn_x(0, 1))
+        turn_v()
+        run(turn_x(0, 0))
         widen_r(0)
         widen_r(1)
         widen_x_vector(1)
@@ -382,121 +397,87 @@ def tile_relative_offset_scores_d9_kernel(tc, X_bytes, X_scale, B, Q, v, R_bytes
         empty_x(0, 1)
         widen_x_scalar(1)
         empty_x(0, 0)
-        turn_r(0)
-        turn_r(1)
-        weave_b(0, 1)
-        turn_r(2)
-        turn_r(3)
+        run(turn_r(0))
+        run(turn_r(1))
+        repeat_v()
+        run(turn_x(1, 1))
+        weave_b(0, 1, turn_r(2))
+        run(turn_c(0))
         empty_r(0)
         empty_r(1)
         empty_b(0, 1)
-        empty_r(2)
-        empty_r(3)
-        turn_x(1, 0)
-        turn_x(1, 1)
-        weave_b(1, 0)
-        weave_b(1, 1)
+        widen_x_scalar(2)
         quantise_x(0)
+        sort_x(1, "turned0")
         group_b(0, N // 2)
         add_v(0)
         widen_x_vector(2)
         quantise_b(0)
-        turn_c(0)
-        turn_x(2, 1)
-        empty_x(1, 0)
+        weave_b(1, 0, turn_r(3))
+        run(turn_x(1, 0))
+        empty_r(2)
+        empty_r(3)
         empty_x(1, 1)
+        empty_x(1, 0)
         empty_b(1, 0)
-        widen_x_scalar(2)
-        empty_b(1, 1)
-        empty_c(0)
+        weave_b(1, 1, turn_c(1))
+        run(turn_x(2, 1))
         group_b(2, N)
-        add_v(1)
+        quantise_c(0)
+        sort_q(2, "c_grouped0")
         quantise_r(0)
+        add_v(1)
+        empty_b(1, 1)
+        weave_b(3, 0, turn_x(2, 0))
+        weave_b(3, 1, turn_c(2))
         quantise_r(1)
-        weave_b(3, 0)
-        turn_c(1)
-        weave_b(3, 1)
         quantise_x(1)
         quantise_b(1)
-        add_v(2)
-        quantise_b(2)
-        multiply_x(0, 0, 2)
-        multiply_x(1, 0, 2)
-        widen_x_vector(3)
+        multiply_x(0, 0, 1)
+        multiply_c(0)
+        multiply_x(1, 0, 1)
         empty_x(2, 1)
         empty_b(3, 0)
-        empty_c(1)
-        empty_b(3, 1)
-        turn_c(2)
-        turn_x(2, 0)
-        turn_x(3, 1)
-        quantise_c(0)
-        quantise_c(1)
-        quantise_b(3)
-        add_v(3)
         widen_x_scalar(3)
-        widen_x_scalar(4)
-        multiply_c(0)
+        empty_b(3, 1)
+        empty_x(2, 0)
+        quantise_b(2)
+        widen_x_vector(3)
+        quantise_c(1)
+        sort_q(3, "c_grouped1")
+        quantise_b(3)
+        add_v(2)
+        multiply_x(0, 1, 3)
+        multiply_x(1, 1, 3)
         multiply_c(1)
-        multiply_x(0, 2, 3)
-        multiply_x(1, 2, 3)
         multiply_x(0, 3, 4)
         multiply_x(1, 3, 4)
-        empty_c(2)
-        empty_x(2, 0)
-        widen_x_vector(4)
-        sort_x(4)
-        quantise_c(2)
-        add_v(4)
-        add_v(5)
-        quantise_x(2)
-        empty_x(3, 1)
-        turn_c(3)
-        turn_x(3, 0)
-        turn_x(4, 1)
-        turn_c(4)
-        turn_x(4, 0)
-        widen_x_scalar(5)
-        empty_x(3, 0)
-        empty_c(3)
-        multiply_c(2)
-        multiply_x(2, 0, 4)
-        empty_x(4, 1)
-        empty_c(4)
-        empty_x(4, 0)
-        widen_x_vector(5)
-        quantise_x(3)
-        sort_x(5)
-        quantise_c(3)
-        add_v(6)
-        finish(0)
-        for s in range(5, NT):
-            if s + 1 < NT:
-                widen_x_scalar(s + 1)
+        widen_x_scalar(4)
+        for s in range(3, NT):
+            if s + 2 < NT:
+                widen_x_scalar(s + 2)
             turn_tile(s)
             empty_tile(s)
-            multiply_tile(s - 2)
+            if s + 2 in ():
+                widen_x_runs_scalar(s + 2, 2)
             if s + 1 < NT:
-                widen_x_vector(s + 1)
+                if s + 1 not in ():
+                    widen_x_runs(s + 1, 2)
+                widen_x_runs(s + 1, 3)
             quantise_x(s - 1)
             if s + 1 < NT:
-                sort_x(s + 1)
+                sort_tile(s + 1)
             quantise_c(s - 1)
-            if s + 2 < NT:
-                add_v(s + 2)
-                finish(s - 4)
-            elif s + 1 < NT:
-                finish(s - 4)
-                finish(s - 3)
+            multiply_tile(s - 1)
+            add_v(s)
+            finish(s - 3)
         last = NT - 1
-        multiply_tile(last - 1)
-        finish(last - 3)
-        quantise_x_half(last, 1)
         quantise_c(last)
         quantise_x_half(last, 0)
+        quantise_x_half(last, 1)
         finish(last - 2)
 
-        passes = [("c_mx", c) for c in range(DP)] + [("x_mx", c) for c in reversed(range(KP))]
+        passes = [("c_mx", c) for c in range(DP)] + [("x_mx", c) for c in range(KP)]
         totals = []
         for lo, hi in LAST_PIECES:
             total = flat(new_bank(("piece", lo)))[:, 0 : hi - lo]

@@ -21,6 +21,7 @@ TURNED_BUFS = 4
 PLANE = 8
 HEAD_TILES = 4
 C_BUFS = 3
+SORT_FIRST = 1
 RESULT_BUFS = 8
 MX_ALIGN = 256
 X_LOADS = [(1, 1), (2, 1), (3, 1)] + [(i, 2) for i in range(4, NT, 2)]
@@ -281,7 +282,14 @@ def tile_relative_offset_scores_d9_kernel(tc, X_bytes, X_scale, B, Q, v, R_bytes
                 held["sorted", i, c] = ordered[:, c - first]
 
         def sort_tile(i):
-            sort_words(i, 0, PLAIN_PASSES + DP, f"turned{i % 2}")
+            sort_words(i, SORT_FIRST, PLAIN_PASSES + DP, f"c_grouped{(i - 2) % C_BUFS}")
+
+        def sort_scalar(i):
+            for c in range(SORT_FIRST):
+                ordered = work.tile([P, 2, P], F32, name="sorted_scalar", bufs=3, align_bytes=64)
+                words = plain[i][:].bitcast(F32)[:, 2 * P * c : 2 * P * c + 2 * P]
+                nc.scalar.copy(out=ordered[:], in_=words.rearrange("r (p u) -> r u p", u=2))
+                held["sorted", i, c] = ordered[:]
 
         def sort_q(i, name):
             sort_words(i, PLAIN_PASSES, PLAIN_PASSES + DP, name)
@@ -379,8 +387,8 @@ def tile_relative_offset_scores_d9_kernel(tc, X_bytes, X_scale, B, Q, v, R_bytes
             empty_x(i, 1)
 
         def multiply_tile(i):
-            multiply_x(i, 0, KP)
             multiply_c(i)
+            multiply_x(i, 0, KP)
 
         spread_r_scales()
         widen_x_vector(0)
@@ -408,7 +416,6 @@ def tile_relative_offset_scores_d9_kernel(tc, X_bytes, X_scale, B, Q, v, R_bytes
         empty_b(0, 1)
         widen_x_scalar(2)
         quantise_x(0)
-        sort_x(1, "turned0")
         group_b(0, N // 2)
         add_v(0)
         widen_x_vector(2)
@@ -424,7 +431,6 @@ def tile_relative_offset_scores_d9_kernel(tc, X_bytes, X_scale, B, Q, v, R_bytes
         run(turn_x(2, 1))
         group_b(2, N)
         quantise_c(0)
-        sort_q(2, "c_grouped0")
         quantise_r(0)
         add_v(1)
         empty_b(1, 1)
@@ -444,7 +450,6 @@ def tile_relative_offset_scores_d9_kernel(tc, X_bytes, X_scale, B, Q, v, R_bytes
         quantise_b(2)
         widen_x_vector(3)
         quantise_c(1)
-        sort_q(3, "c_grouped1")
         quantise_b(3)
         add_v(2)
         multiply_x(0, 1, 3)
@@ -453,21 +458,21 @@ def tile_relative_offset_scores_d9_kernel(tc, X_bytes, X_scale, B, Q, v, R_bytes
         multiply_x(0, 3, 4)
         multiply_x(1, 3, 4)
         widen_x_scalar(4)
+        sort_scalar(4)
         for s in range(3, NT):
             if s + 2 < NT:
                 widen_x_scalar(s + 2)
             turn_tile(s)
-            empty_tile(s)
-            if s + 2 in ():
-                widen_x_runs_scalar(s + 2, 2)
+            empty_x(s, 0)
+            if s + 2 < NT:
+                sort_scalar(s + 2)
+            empty_x(s, 1)
             if s + 1 < NT:
-                if s + 1 not in ():
-                    widen_x_runs(s + 1, 2)
-                widen_x_runs(s + 1, 3)
-            quantise_x(s - 1)
+                widen_x_vector(s + 1)
+            quantise_c(s - 1)
             if s + 1 < NT:
                 sort_tile(s + 1)
-            quantise_c(s - 1)
+            quantise_x(s - 1)
             multiply_tile(s - 1)
             add_v(s)
             finish(s - 3)

@@ -99,9 +99,9 @@ def tile_relative_offset_scores_d9_kernel(tc, X_bytes, X_scale, B, Q, v, R_bytes
         load_r(0)
         nc.sync.dma_start(out=v_rows[0:DP, :], in_=v.rearrange("(c k) -> c k", c=DP))
         nc.sync.dma_start(out=x_scales[:], in_=X_scale_rows[:, NB:])
+        load_b(0)
         load_x(1)
         load_r(2)
-        load_b(0)
         load_q(0)
         load_b(1)
         load_x(2)
@@ -399,59 +399,62 @@ def tile_relative_offset_scores_d9_kernel(tc, X_bytes, X_scale, B, Q, v, R_bytes
         run(turn_x(0, 0))
         widen_r(0)
         widen_r(1)
+        group_b(0, N // 2)
         widen_x_vector(1)
         widen_r(2)
         widen_r(3)
         empty_x(0, 1)
-        widen_x_scalar(1)
+        repeat_v()
         empty_x(0, 0)
         run(turn_r(0))
-        run(turn_r(1))
-        repeat_v()
+        weave_b(0, 1, turn_r(1))
+        widen_x_scalar(1)
         run(turn_x(1, 1))
-        weave_b(0, 1, turn_r(2))
+        run(turn_r(2))
         run(turn_c(0))
+        empty_b(0, 1)
         empty_r(0)
         empty_r(1)
-        empty_b(0, 1)
-        widen_x_scalar(2)
         quantise_x(0)
-        group_b(0, N // 2)
+        quantise_b(0)
         add_v(0)
         widen_x_vector(2)
-        quantise_b(0)
-        weave_b(1, 0, turn_r(3))
-        run(turn_x(1, 0))
+        weave_b(1, 0, turn_x(1, 0))
+        weave_b(1, 1, turn_r(3))
         empty_r(2)
-        empty_r(3)
+        widen_x_scalar(2)
         empty_x(1, 1)
         empty_x(1, 0)
+        empty_r(3)
         empty_b(1, 0)
-        weave_b(1, 1, turn_c(1))
         run(turn_x(2, 1))
+        run(turn_c(1))
         group_b(2, N)
         quantise_c(0)
-        quantise_r(0)
         add_v(1)
+        quantise_r(0)
         empty_b(1, 1)
+        empty_x(2, 1)
         weave_b(3, 0, turn_x(2, 0))
-        weave_b(3, 1, turn_c(2))
+        run(turn_c(2))
         quantise_r(1)
+        widen_x_vector(3)
         quantise_x(1)
         quantise_b(1)
-        multiply_x(0, 0, 1)
-        multiply_c(0)
-        multiply_x(1, 0, 1)
-        empty_x(2, 1)
         empty_b(3, 0)
         widen_x_scalar(3)
-        empty_b(3, 1)
+        run(turn_c(3))
+        multiply_x(0, 0, 1)
+        multiply_c(0)
+        run(turn_x(3, 1))
+        run(turn_x(3, 0))
+        group_b_scalar(3, 1)
         empty_x(2, 0)
         quantise_b(2)
-        widen_x_vector(3)
         quantise_c(1)
-        quantise_b(3)
         add_v(2)
+        quantise_b(3)
+        multiply_x(1, 0, 1)
         multiply_x(0, 1, 3)
         multiply_x(1, 1, 3)
         multiply_c(1)
@@ -459,16 +462,28 @@ def tile_relative_offset_scores_d9_kernel(tc, X_bytes, X_scale, B, Q, v, R_bytes
         multiply_x(1, 3, 4)
         widen_x_scalar(4)
         sort_scalar(4)
-        for s in range(3, NT):
+        empty_tile(3)
+        widen_x_scalar(5)
+        sort_scalar(5)
+        widen_x_vector(4)
+        quantise_c(2)
+        sort_tile(4)
+        quantise_x(2)
+        multiply_tile(2)
+        add_v(3)
+        finish(0)
+        for s in range(4, NT):
+            turn_tile(s)
+            empty_tile(s)
             if s + 2 < NT:
                 widen_x_scalar(s + 2)
-            turn_tile(s)
-            empty_x(s, 0)
-            if s + 2 < NT:
                 sort_scalar(s + 2)
-            empty_x(s, 1)
+            if s + 1 == NT - 1:
+                widen_x_runs_scalar(s + 1, 2)
+            else:
+                widen_x_runs(s + 1, 2) if s + 1 < NT else None
             if s + 1 < NT:
-                widen_x_vector(s + 1)
+                widen_x_runs(s + 1, 3)
             quantise_c(s - 1)
             if s + 1 < NT:
                 sort_tile(s + 1)

@@ -20,7 +20,7 @@ WIDE_BUFS = 4
 TURNED_BUFS = 4
 PLANE = 8
 HEAD_TILES = 4
-C_BUFS = 3
+C_BUFS = 4
 SORT_FIRST = 1
 RESULT_BUFS = 8
 MX_ALIGN = 256
@@ -51,7 +51,8 @@ def tile_relative_offset_scores_d9_kernel(tc, X_bytes, X_scale, B, Q, v, R_bytes
         r_column = keep.tile([P, 1], F32, align_bytes=64)
         nc.gpsimd.memset(r_column[:], 0.0)
         v_rows = keep.tile([P, PASS], BF16, align_bytes=64)
-        nc.vector.memset(v_rows[:], 0.0)
+        zero = keep.tile([P, 1], F32, align_bytes=64)
+        nc.vector.memset(zero[:], 0.0)
         v_turned = keep.tile([P, DP, P, 4], BF16, align_bytes=64)
         ident = keep.tile([P, P], F32, align_bytes=64)
         make_identity(nc, ident[:])
@@ -63,7 +64,9 @@ def tile_relative_offset_scores_d9_kernel(tc, X_bytes, X_scale, B, Q, v, R_bytes
         r_lot = [keep.tile([P, 2, D], U8, name=f"r_raw{h}", align_bytes=64) for h in range(RT // 2)]
         r_raw = [r_lot[t // 2][:, t % 2, :] for t in range(RT)]
         x_lot = {lo: keep.tile([P, n, K], U8, name=f"x_raw{lo}", align_bytes=64) for lo, n in X_LOADS}
-        plain = [keep.tile([P, PLAIN_PASSES * PASS + D], BF16, name=f"plain{i}", align_bytes=64) for i in range(NT)]
+        plain = [keep.tile([P, PLAIN_PASSES * PASS + (D if i + 1 < NT else 0)], BF16, name=f"plain{i}", align_bytes=64) for i in range(NT)]
+        q_first = keep.tile([P, D], BF16, align_bytes=64)
+        q_raw = [q_first[:]] + [plain[i][:, PLAIN_PASSES * PASS :] for i in range(NT - 1)]
         x_raw = {lo + j: x_lot[lo][:, j, :] for lo, n in X_LOADS for j in range(n)}
         b_raw = [keep.tile([P, 4, N], BF16, name=f"b_raw{c}", align_bytes=64) for c in range(KP)]
         x0_scales = keep.tile([P, NB], F32, align_bytes=64)
@@ -79,7 +82,7 @@ def tile_relative_offset_scores_d9_kernel(tc, X_bytes, X_scale, B, Q, v, R_bytes
             nc.sync.dma_start(out=x_lot[i][:], in_=X_tiles[:, i : i + dict(X_LOADS)[i], :])
 
         def load_q(i):
-            nc.sync.dma_start(out=plain[i][:, PLAIN_PASSES * PASS :], in_=Q_tiles[:, i, :])
+            nc.sync.dma_start(out=q_raw[i], in_=Q_tiles[:, i, :])
 
         def load_r(t):
             nc.sync.dma_start(out=r_lot[t // 2][:], in_=R_bytes.rearrange("(t p) k -> p t k", p=P)[:, t : t + 2, :])
@@ -95,13 +98,14 @@ def tile_relative_offset_scores_d9_kernel(tc, X_bytes, X_scale, B, Q, v, R_bytes
         nc.scalar.dma_start(out=r_column[0 : RT * RB, :], in_=R_scale.rearrange("a (b o) -> (a b) o", o=1))
         nc.sync.dma_start(out=x0_raw[1][:], in_=X_tiles[:, 0, K // 2 :])
         nc.sync.dma_start(out=x0_raw[0][:], in_=X_tiles[:, 0, 0 : K // 2])
+        nc.scalar.activation(out=v_rows[:].bitcast(F32), in_=zero[:].to_broadcast([P, PASS // 2]), func=COPY)
         nc.scalar.activation(out=ident32[:], in_=ident[:], func=COPY, scale=ROOT_D)
         load_r(0)
-        nc.sync.dma_start(out=v_rows[0:DP, :], in_=v.rearrange("(c k) -> c k", c=DP))
         nc.sync.dma_start(out=x_scales[:], in_=X_scale_rows[:, NB:])
         load_b(0)
         load_x(1)
         load_r(2)
+        nc.sync.dma_start(out=v_rows[0:DP, :], in_=v.rearrange("(c k) -> c k", c=DP))
         load_q(0)
         load_b(1)
         load_x(2)
@@ -139,11 +143,11 @@ def tile_relative_offset_scores_d9_kernel(tc, X_bytes, X_scale, B, Q, v, R_bytes
         def flat(bank):
             return bank[:].rearrange("p c u r -> p (c u r)")
 
-        def turn(key, words, u_first=False):
+        def turn(key, words, u_first=False, order=(0, 1)):
             def one(c, u):
                 bank = held[key][0] if key in held else new_bank(key)
                 nc.tensor.transpose(bank[:, u, c, :] if u_first else bank[:, c, u, :], words(c, u), ident[:])
-            return [lambda c=c, u=u: one(c, u) for c in range(2) for u in range(2)]
+            return [lambda c=c, u=u: one(c, u) for c in order for u in range(2)]
 
         def run(calls):
             for call in calls:
@@ -219,14 +223,11 @@ def tile_relative_offset_scores_d9_kernel(tc, X_bytes, X_scale, B, Q, v, R_bytes
             src = b_raw[c][:].rearrange("p t (m i) -> p m t i", i=4)
             nc.scalar.activation(out=dst[:, cols], in_=src[:, cols], func=COPY, scale=ROOT_D)
 
-        def weave_b(c, half, beside):
+        def weave_b(c, half):
             slots = flat(new_bank(("b", c, half))).bitcast(BF16).rearrange("p (n u e) -> p u e n", u=2, e=2)
-            for step, transpose in enumerate(beside):
-                u, quarter = divmod(step, 2)
-                lo = N // 4 * quarter
-                nc.tensor.matmul(slots[:, u, :, lo : lo + N // 4], lhsT=ident32[:],
-                                 rhs=b_raw[c][:, 2 * u : 2 * u + 2, N // 2 * half + lo : N // 2 * half + lo + N // 4], start=True, stop=True)
-                transpose()
+            cols = slice(N // 2 * half, N // 2 * half + N // 2)
+            for u in range(2):
+                nc.tensor.matmul(slots[:, u], lhsT=ident32[:], rhs=b_raw[c][:, 2 * u : 2 * u + 2, cols], start=True, stop=True)
 
         def empty_b(c, half):
             words = b_grouped[c][:].rearrange("p n t -> p (n t)").bitcast(F32)[:, N * half : N * half + N]
@@ -282,11 +283,11 @@ def tile_relative_offset_scores_d9_kernel(tc, X_bytes, X_scale, B, Q, v, R_bytes
                 held["sorted", i, c] = ordered[:, c - first]
 
         def sort_tile(i):
-            sort_words(i, SORT_FIRST, PLAIN_PASSES + DP, f"c_grouped{(i - 2) % C_BUFS}")
+            sort_words(i, SORT_FIRST, PLAIN_PASSES + (DP if i + 1 < NT else 0), f"c_grouped{(i - 2) % C_BUFS}")
 
-        def sort_scalar(i):
-            for c in range(SORT_FIRST):
-                ordered = work.tile([P, 2, P], F32, name="sorted_scalar", bufs=3, align_bytes=64)
+        def sort_scalar(i, passes=range(SORT_FIRST)):
+            for c in passes:
+                ordered = work.tile([P, 2, P], F32, name="sorted_scalar", bufs=4, align_bytes=64)
                 words = plain[i][:].bitcast(F32)[:, 2 * P * c : 2 * P * c + 2 * P]
                 nc.scalar.copy(out=ordered[:], in_=words.rearrange("r (p u) -> r u p", u=2))
                 held["sorted", i, c] = ordered[:]
@@ -302,13 +303,18 @@ def tile_relative_offset_scores_d9_kernel(tc, X_bytes, X_scale, B, Q, v, R_bytes
                 return held["sorted", i, c][:, u, :]
             return stepped(plain[i][:].bitcast(F32), c, u)
 
+        def q_words(i, c, u):
+            if ("sorted", i - 1, PLAIN_PASSES + c) in held:
+                return held["sorted", i - 1, PLAIN_PASSES + c][:, u, :]
+            return stepped(q_raw[i].bitcast(F32), c, u)
+
         def turn_x(i, half):
             if half == 0:
                 return turn(("x", i, 0), lambda c, u: plain_words(i, c, u))
-            return turn(("x", i, 1), lambda c, u: x_runs(i).bitcast(F32)[:, P * (2 * c + u) : P * (2 * c + u + 1)])
+            return turn(("x", i, 1), lambda c, u: x_runs(i).bitcast(F32)[:, P * (2 * c + u) : P * (2 * c + u + 1)], order=(1, 0) if i else (0, 1))
 
         def turn_c(i):
-            return turn(("c", i), lambda c, u: plain_words(i, PLAIN_PASSES + c, u), u_first=True)
+            return turn(("c", i), lambda c, u: q_words(i, c, u), u_first=True)
 
         def empty_x(i, half):
             if ("x_grouped", i) not in held:
@@ -380,11 +386,11 @@ def tile_relative_offset_scores_d9_kernel(tc, X_bytes, X_scale, B, Q, v, R_bytes
             scale_and_store(result, flat(full_bank(("sum", i))), i, slice(0, N))
 
         def turn_tile(i):
-            run(turn_c(i) + turn_x(i, 0) + turn_x(i, 1))
+            run(turn_c(i) + turn_x(i, 1) + turn_x(i, 0))
 
         def empty_tile(i):
-            empty_x(i, 0)
             empty_x(i, 1)
+            empty_x(i, 0)
 
         def multiply_tile(i):
             multiply_c(i)
@@ -395,7 +401,6 @@ def tile_relative_offset_scores_d9_kernel(tc, X_bytes, X_scale, B, Q, v, R_bytes
         widen_x_plain(0, 1, False)
         widen_x_plain(0, 0, True)
         run(turn_x(0, 1))
-        turn_v()
         run(turn_x(0, 0))
         widen_r(0)
         widen_r(1)
@@ -404,29 +409,32 @@ def tile_relative_offset_scores_d9_kernel(tc, X_bytes, X_scale, B, Q, v, R_bytes
         widen_r(2)
         widen_r(3)
         empty_x(0, 1)
-        repeat_v()
         empty_x(0, 0)
         run(turn_r(0))
-        weave_b(0, 1, turn_r(1))
+        weave_b(0, 1)
+        run(turn_r(1))
         widen_x_scalar(1)
         run(turn_x(1, 1))
+        turn_v()
         run(turn_r(2))
         run(turn_c(0))
         empty_b(0, 1)
+        repeat_v()
         empty_r(0)
         empty_r(1)
         quantise_x(0)
         quantise_b(0)
+        group_b(1, N // 2)
         add_v(0)
         widen_x_vector(2)
-        weave_b(1, 0, turn_x(1, 0))
-        weave_b(1, 1, turn_r(3))
+        run(turn_x(1, 0))
+        weave_b(1, 1)
+        run(turn_r(3))
         empty_r(2)
         widen_x_scalar(2)
         empty_x(1, 1)
         empty_x(1, 0)
         empty_r(3)
-        empty_b(1, 0)
         run(turn_x(2, 1))
         run(turn_c(1))
         group_b(2, N)
@@ -435,7 +443,8 @@ def tile_relative_offset_scores_d9_kernel(tc, X_bytes, X_scale, B, Q, v, R_bytes
         quantise_r(0)
         empty_b(1, 1)
         empty_x(2, 1)
-        weave_b(3, 0, turn_x(2, 0))
+        weave_b(3, 0)
+        run(turn_x(2, 0))
         run(turn_c(2))
         quantise_r(1)
         widen_x_vector(3)
@@ -460,11 +469,13 @@ def tile_relative_offset_scores_d9_kernel(tc, X_bytes, X_scale, B, Q, v, R_bytes
         multiply_c(1)
         multiply_x(0, 3, 4)
         multiply_x(1, 3, 4)
-        widen_x_scalar(4)
+        widen_x_plain(4, 1, True)
+        widen_x_plain(4, 0, True)
+        sort_scalar(3, range(PLAIN_PASSES, PLAIN_PASSES + DP))
         sort_scalar(4)
         empty_tile(3)
-        widen_x_scalar(5)
-        sort_scalar(5)
+        widen_x_plain(5, 1, True)
+        widen_x_plain(5, 0, True)
         widen_x_vector(4)
         quantise_c(2)
         sort_tile(4)
@@ -474,16 +485,15 @@ def tile_relative_offset_scores_d9_kernel(tc, X_bytes, X_scale, B, Q, v, R_bytes
         finish(0)
         for s in range(4, NT):
             turn_tile(s)
-            empty_tile(s)
-            if s + 2 < NT:
-                widen_x_scalar(s + 2)
-                sort_scalar(s + 2)
-            if s + 1 == NT - 1:
-                widen_x_runs_scalar(s + 1, 2)
-            else:
-                widen_x_runs(s + 1, 2) if s + 1 < NT else None
+            empty_x(s, 1)
             if s + 1 < NT:
-                widen_x_runs(s + 1, 3)
+                sort_scalar(s + 1)
+            empty_x(s, 0)
+            if s + 2 < NT:
+                widen_x_plain(s + 2, 1, True)
+                widen_x_plain(s + 2, 0, True)
+            if s + 1 < NT:
+                widen_x_vector(s + 1)
             quantise_c(s - 1)
             if s + 1 < NT:
                 sort_tile(s + 1)
@@ -493,11 +503,11 @@ def tile_relative_offset_scores_d9_kernel(tc, X_bytes, X_scale, B, Q, v, R_bytes
             finish(s - 3)
         last = NT - 1
         quantise_c(last)
-        quantise_x_half(last, 0)
         quantise_x_half(last, 1)
+        quantise_x_half(last, 0)
         finish(last - 2)
 
-        passes = [("c_mx", c) for c in range(DP)] + [("x_mx", c) for c in range(KP)]
+        passes = [("c_mx", c) for c in range(DP)] + [("x_mx", c) for c in reversed(range(KP))]
         totals = []
         for lo, hi in LAST_PIECES:
             total = flat(new_bank(("piece", lo)))[:, 0 : hi - lo]

@@ -102,13 +102,13 @@ def tile_relative_offset_scores_d9_kernel(tc, X_bytes, X_scale, B, Q, v, R_bytes
         nc.scalar.activation(out=ident32[:], in_=ident[:], func=COPY, scale=ROOT_D)
         load_r(0)
         nc.sync.dma_start(out=x_scales[:], in_=X_scale_rows[:, NB:])
-        load_b(0)
         load_x(1)
         load_r(2)
         nc.sync.dma_start(out=v_rows[0:DP, :], in_=v.rearrange("(c k) -> c k", c=DP))
+        load_b(0)
         load_q(0)
-        load_b(1)
         load_x(2)
+        load_b(1)
         load_b(2)
         load_q(1)
         load_b(3)
@@ -398,49 +398,48 @@ def tile_relative_offset_scores_d9_kernel(tc, X_bytes, X_scale, B, Q, v, R_bytes
 
         spread_r_scales()
         widen_x_vector(0)
-        widen_x_plain(0, 1, False)
-        widen_x_plain(0, 0, True)
+        widen_x_scalar(0)
         run(turn_x(0, 1))
-        run(turn_x(0, 0))
         widen_r(0)
         widen_r(1)
-        group_b(0, N // 2)
         widen_x_vector(1)
         widen_r(2)
         widen_r(3)
-        empty_x(0, 1)
-        empty_x(0, 0)
+        group_b(0, N // 2)
         run(turn_r(0))
-        weave_b(0, 1)
-        run(turn_r(1))
+        run(turn_x(0, 0))
+        empty_x(0, 1)
         widen_x_scalar(1)
+        run(turn_r(1))
         run(turn_x(1, 1))
+        empty_x(0, 0)
         turn_v()
+        weave_b(0, 1)
         run(turn_r(2))
         run(turn_c(0))
-        empty_b(0, 1)
-        repeat_v()
         empty_r(0)
+        repeat_v()
+        empty_b(0, 1)
         empty_r(1)
         quantise_x(0)
-        quantise_b(0)
+        widen_x_vector(2)
         group_b(1, N // 2)
         add_v(0)
-        widen_x_vector(2)
-        run(turn_x(1, 0))
-        weave_b(1, 1)
+        quantise_b(0)
         run(turn_r(3))
+        weave_b(1, 1)
+        run(turn_x(1, 0))
         empty_r(2)
+        empty_r(3)
         widen_x_scalar(2)
         empty_x(1, 1)
         empty_x(1, 0)
-        empty_r(3)
         run(turn_x(2, 1))
         run(turn_c(1))
         group_b(2, N)
         quantise_c(0)
-        add_v(1)
         quantise_r(0)
+        add_v(1)
         empty_b(1, 1)
         empty_x(2, 1)
         weave_b(3, 0)

@@ -105,6 +105,7 @@ def tile_relative_offset_scores_d9_kernel(tc, X_bytes, X_scale, B, Q, v, R_bytes
         load_x(1)
         load_r(2)
         nc.sync.dma_start(out=v_rows[0:DP, :], in_=v.rearrange("(c k) -> c k", c=DP))
+        nc.sync.dma_start(out=v_rows[DP : DP + 1, :], in_=g.rearrange("(o n) -> o n", o=1))
         load_b(0)
         load_q(0)
         load_x(2)
@@ -119,7 +120,6 @@ def tile_relative_offset_scores_d9_kernel(tc, X_bytes, X_scale, B, Q, v, R_bytes
         load_q(4)
         load_q(5)
         load_x(6)
-        nc.sync.dma_start(out=g_all[:], in_=g.partition_broadcast(P))
         for i in range(6, NT, 2):
             load_q(i)
             load_q(i + 1)
@@ -183,6 +183,13 @@ def tile_relative_offset_scores_d9_kernel(tc, X_bytes, X_scale, B, Q, v, R_bytes
         def repeat_v():
             column = full_bank("v")[:, :, 0, 0:DP].rearrange("p u (c o) -> p c o u", o=1)
             nc.scalar.copy(out=as_words(v_turned[:]), in_=column.to_broadcast([P, DP, P, 2]))
+
+        def spread_g():
+            wide = flat(new_bank("g")).bitcast(BF16)[:, 0:N]
+            nc.tensor.matmul(wide, lhsT=ident32[:, DP : DP + 1].to_broadcast([P, P]), rhs=v_rows[:], start=True, stop=True)
+
+        def empty_g():
+            nc.scalar.copy(out=g_all[:], in_=flat(full_bank("g")).bitcast(BF16)[:, 0:N])
 
         def spread_r_scales():
             nc.tensor.transpose(new_bank("r_scales")[:, 0, 0, :], r_column[:].to_broadcast([P, P]), ident[:])
@@ -378,7 +385,7 @@ def tile_relative_offset_scores_d9_kernel(tc, X_bytes, X_scale, B, Q, v, R_bytes
             multiply(i, "x_mx", range(first, end))
 
         def scale_and_store(result, total, i, cols):
-            nc.vector.scalar_tensor_tensor(out=result[:], in0=total, scalar=1.0 / ROOT_D, in1=g_all[:, cols], op0=MULT, op1=MULT)
+            nc.vector.scalar_tensor_tensor(out=result[:], in0=total, scalar=1.0 / D, in1=g_all[:, cols], op0=MULT, op1=MULT)
             nc.sync.dma_start(out=out_tiles[:, i, cols], in_=result[:])
 
         def finish(i):
@@ -451,12 +458,14 @@ def tile_relative_offset_scores_d9_kernel(tc, X_bytes, X_scale, B, Q, v, R_bytes
         quantise_b(1)
         empty_b(3, 0)
         widen_x_scalar(3)
+        spread_g()
         run(turn_c(3))
         multiply_x(0, 0, 1)
         multiply_c(0)
         run(turn_x(3, 1))
         run(turn_x(3, 0))
         group_b_scalar(3, 1)
+        empty_g()
         empty_x(2, 0)
         quantise_b(2)
         quantise_c(1)

from contextlib import ExitStack

import concourse.mybir as mybir
from concourse.masks import make_identity

T, K, D, N, G = 1536, 2048, 1024, 512, 128
P = 128
PASS = 512
NT = T // P
KP = K // PASS
DP = D // PASS
NB = K // G
RB = D // G
RT = N // P
PASS_BLOCKS = PASS // G
PLAIN_PASSES = 2
ROOT_D = 32.0
BANKS = 8
WIDE_BUFS = 4
TURNED_BUFS = 4
PLANE = 8
HEAD_TILES = 4
C_BUFS = 4
SORT_FIRST = 1
RESULT_BUFS = 8
MX_ALIGN = 256
X_LOADS = [(1, 1), (2, 1), (3, 1)] + [(i, 2) for i in range(4, NT, 2)]
LAST_PIECES = [(0, N // 2), (N // 2, 3 * N // 4), (3 * N // 4, N)]

FLOPS = 2 * T * N * (K + D)

F32 = mybir.dt.float32
BF16 = mybir.dt.bfloat16
U32 = mybir.dt.uint32
U8 = mybir.dt.uint8
FP8 = mybir.dt.float8_e4m3fn
FP8X4 = mybir.dt.float8_e4m3fn_x4
MULT = mybir.AluOpType.mult
ADD = mybir.AluOpType.add
COPY = mybir.ActivationFunctionType.Copy


def tile_relative_offset_scores_d9_kernel(tc, X_bytes, X_scale, B, Q, v, R_bytes, R_scale, g, out):
    nc = tc.nc
    with ExitStack() as ctx:
        keep = ctx.enter_context(tc.tile_pool(name="keep", bufs=1))
        work = ctx.enter_context(tc.tile_pool(name="work", bufs=WIDE_BUFS))
        psum = ctx.enter_context(tc.psum_pool(name="psum", bufs=1))
        ctx.enter_context(tc.manual_schedule())

        r_column = keep.tile([P, 1], F32, align_bytes=64)
        nc.gpsimd.memset(r_column[:], 0.0)
        v_rows = keep.tile([P, PASS], BF16, align_bytes=64)
        zero = keep.tile([P, 1], F32, align_bytes=64)
        nc.vector.memset(zero[:], 0.0)
        v_turned = keep.tile([P, DP, P, 4], BF16, align_bytes=64)
        ident = keep.tile([P, P], F32, align_bytes=64)
        make_identity(nc, ident[:])
        ident32 = keep.tile([P, P], BF16, align_bytes=64)

        x_scales = keep.tile([P, (NT - 1) * NB], F32, align_bytes=64)
        r_scales = keep.tile([P, RT * RB], F32, align_bytes=64)
        g_all = keep.tile([P, N], BF16, align_bytes=64)
        r_lot = [keep.tile([P, 2, D], U8, name=f"r_raw{h}", align_bytes=64) for h in range(RT // 2)]
        r_raw = [r_lot[t // 2][:, t % 2, :] for t in range(RT)]
        x_lot = {lo: keep.tile([P, n, K], U8, name=f"x_raw{lo}", align_bytes=64) for lo, n in X_LOADS}
        plain = [keep.tile([P, PLAIN_PASSES * PASS + (D if i + 1 < NT else 0)], BF16, name=f"plain{i}", align_bytes=64) for i in range(NT)]
        q_first = keep.tile([P, D], BF16, align_bytes=64)
        q_raw = [q_first[:]] + [plain[i][:, PLAIN_PASSES * PASS :] for i in range(NT - 1)]
        x_raw = {lo + j: x_lot[lo][:, j, :] for lo, n in X_LOADS for j in range(n)}
        b_raw = [keep.tile([P, 4, N], BF16, name=f"b_raw{c}", align_bytes=64) for c in range(KP)]
        x0_scales = keep.tile([P, NB], F32, align_bytes=64)
        x0_raw = [keep.tile([P, K // 2], U8, name=f"x0_raw{h}", align_bytes=64) for h in range(2)]
        X_tiles = X_bytes.rearrange("(p i) k -> p i k", i=NT)
        Q_tiles = Q.rearrange("(p i) k -> p i k", i=NT)
        out_tiles = out.rearrange("(p i) n -> p i n", i=NT)
        X_scale_rows = X_scale.rearrange("(p i) j -> p (i j)", i=NT)
        B_plain = B.rearrange("(c p t) n -> c p t n", p=P, t=4)
        B_runs = B.rearrange("(c h u j e) n -> c j h u (e n)", h=32, u=2, j=4, e=2)

        def load_x(i):
            nc.sync.dma_start(out=x_lot[i][:], in_=X_tiles[:, i : i + dict(X_LOADS)[i], :])

        def load_q(i):
            nc.sync.dma_start(out=q_raw[i], in_=Q_tiles[:, i, :])

        def load_r(t):
            nc.sync.dma_start(out=r_lot[t // 2][:], in_=R_bytes.rearrange("(t p) k -> p t k", p=P)[:, t : t + 2, :])

        def load_b(c):
            if c < PLAIN_PASSES:
                nc.sync.dma_start(out=b_raw[c][:], in_=B_plain[c])
            else:
                for j in range(4):
                    nc.sync.dma_start(out=b_raw[c][j:P:4].rearrange("h (u e) n -> h u (e n)", u=2), in_=B_runs[c, j])

        nc.scalar.dma_start(out=x0_scales[:], in_=X_scale_rows[:, 0:NB])
        nc.scalar.dma_start(out=r_column[0 : RT * RB, :], in_=R_scale.rearrange("a (b o) -> (a b) o", o=1))
        nc.sync.dma_start(out=x0_raw[1][:], in_=X_tiles[:, 0, K // 2 :])
        nc.sync.dma_start(out=x0_raw[0][:], in_=X_tiles[:, 0, 0 : K // 2])
        nc.scalar.activation(out=v_rows[:].bitcast(F32), in_=zero[:].to_broadcast([P, PASS // 2]), func=COPY)
        nc.scalar.activation(out=ident32[:], in_=ident[:], func=COPY, scale=ROOT_D)
        load_r(0)
        nc.sync.dma_start(out=x_scales[:], in_=X_scale_rows[:, NB:])
        load_x(1)
        load_r(2)
        nc.sync.dma_start(out=v_rows[0:DP, :], in_=v.rearrange("(c k) -> c k", c=DP))
        nc.sync.dma_start(out=v_rows[DP : DP + 1, :], in_=g.rearrange("(o n) -> o n", o=1))
        load_b(0)
        load_q(0)
        load_x(2)
        load_b(1)
        load_b(2)
        load_q(1)
        load_b(3)
        load_x(3)
        load_q(2)
        load_q(3)
        load_x(4)
        load_q(4)
        load_q(5)
        load_x(6)
        for i in range(6, NT, 2):
            load_q(i)
            load_q(i + 1)
            if i + 2 < NT:
                load_x(i + 2)

        held = {}
        free_banks = list(range(BANKS))

        def new_bank(key):
            number = free_banks.pop(0)
            bank = psum.tile([P, 2, 2, P], F32, name=f"bank{number}")
            held[key] = (bank, number)
            return bank

        def full_bank(key):
            bank, number = held.pop(key)
            free_banks.append(number)
            return bank

        def flat(bank):
            return bank[:].rearrange("p c u r -> p (c u r)")

        def turn(key, words, u_first=False, order=(0, 1)):
            def one(c, u):
                bank = held[key][0] if key in held else new_bank(key)
                nc.tensor.transpose(bank[:, u, c, :] if u_first else bank[:, c, u, :], words(c, u), ident[:])
            return [lambda c=c, u=u: one(c, u) for c in order for u in range(2)]

        def run(calls):
            for call in calls:
                call()

        def stepped(words, c, u):
            return words[:, 2 * P * c + u : 2 * P * c + 2 * P : 2]

        def empty(key, words):
            nc.scalar.copy(out=words, in_=full_bank(key)[:].rearrange("p c u r -> p c r u"))

        def as_words(grouped):
            return grouped.rearrange("p c r t -> p (c r t)").bitcast(F32).rearrange("p (c r u) -> p c r u", c=grouped.shape[1], u=2)

        def widen_plain(wide, raw, scale, on_scalar):
            if on_scalar:
                nc.scalar.activation(out=wide, in_=raw.bitcast(FP8), func=COPY, scale=scale)
            else:
                nc.vector.tensor_scalar(out=wide, in0=raw.bitcast(FP8), scalar1=scale, scalar2=None, op0=MULT)

        def widen_runs(wide, raw, scale, blk):
            c, q = divmod(blk, PASS_BLOCKS)
            runs = wide.rearrange("r (c u h m) -> r c h u m", u=2, h=32, m=8)
            nc.vector.tensor_scalar(out=runs[:, c, 8 * q : 8 * q + 8],
                                    in0=raw.bitcast(FP8).rearrange("r (h u m) -> r h u m", u=2, m=8),
                                    scalar1=scale, scalar2=None, op0=MULT)

        def turn_v():
            bank = new_bank("v")
            for u in range(2):
                nc.tensor.transpose(bank[:, u, 0, :], v_rows[:].bitcast(F32)[:, u::2], ident[:])

        def repeat_v():
            column = full_bank("v")[:, :, 0, 0:DP].rearrange("p u (c o) -> p c o u", o=1)
            nc.scalar.copy(out=as_words(v_turned[:]), in_=column.to_broadcast([P, DP, P, 2]))

        def spread_g():
            wide = flat(new_bank("g")).bitcast(BF16)[:, 0:N]
            nc.tensor.matmul(wide, lhsT=ident32[:, DP : DP + 1].to_broadcast([P, P]), rhs=v_rows[:], start=True, stop=True)

        def empty_g():
            nc.scalar.copy(out=g_all[:], in_=flat(full_bank("g")).bitcast(BF16)[:, 0:N])

        def spread_r_scales():
            nc.tensor.transpose(new_bank("r_scales")[:, 0, 0, :], r_column[:].to_broadcast([P, P]), ident[:])
            nc.scalar.copy(out=r_scales[:], in_=full_bank("r_scales")[:, 0, 0, 0 : RT * RB])

        r_wide = [keep.tile([P, D], BF16, name=f"r_wide{t}", align_bytes=64) for t in range(RT)]
        r_grouped = keep.tile([P, DP, N, 4], BF16, align_bytes=64)
        r_codes = keep.tile([P, DP, N], U32, align_bytes=MX_ALIGN)
        r_exps = keep.tile([P, DP, N], U8, align_bytes=MX_ALIGN)

        def widen_r(t, on_scalar=False):
            for blk in range(RB):
                widen_plain(r_wide[t][:, G * blk : G * blk + G], r_raw[t][:, G * blk : G * blk + G],
                            r_scales[:, RB * t + blk : RB * t + blk + 1], on_scalar)

        def turn_r(t):
            return turn(("r", t), lambda c, u: stepped(r_wide[t][:].bitcast(F32), c, u))

        def empty_r(t):
            empty(("r", t), as_words(r_grouped[:])[:, :, P * t : P * t + P, :])

        def quantise_r(c):
            nc.vector.quantize_mx(out=r_codes[:, c, :].bitcast(FP8X4), scales=r_exps[:, c, :],
                                  in_=r_grouped[:, c].rearrange("p n t -> p (n t)"))

        b_grouped = [keep.tile([P, N, 4], BF16, name=f"b_grouped{c}", align_bytes=64) for c in range(KP)]
        b_codes = keep.tile([P, KP, N], U32, align_bytes=MX_ALIGN)
        b_exps = keep.tile([P, KP, N], U8, align_bytes=MX_ALIGN)

        def group_b(c, end):
            dst = b_grouped[c][:].rearrange("p (m i) t -> p m t i", i=4)
            src = b_raw[c][:].rearrange("p t (m i) -> p m t i", i=4)
            nc.vector.tensor_scalar(out=dst[:, 0 : end // 4], in0=src[:, 0 : end // 4], scalar1=ROOT_D, scalar2=None, op0=MULT)

        def group_b_scalar(c, half):
            cols = slice(N // 8 * half, N // 8 * half + N // 8)
            dst = b_grouped[c][:].rearrange("p (m i) t -> p m t i", i=4)
            src = b_raw[c][:].rearrange("p t (m i) -> p m t i", i=4)
            nc.scalar.activation(out=dst[:, cols], in_=src[:, cols], func=COPY, scale=ROOT_D)

        def weave_b(c, half):
            slots = flat(new_bank(("b", c, half))).bitcast(BF16).rearrange("p (n u e) -> p u e n", u=2, e=2)
            cols = slice(N // 2 * half, N // 2 * half + N // 2)
            for u in range(2):
                nc.tensor.matmul(slots[:, u], lhsT=ident32[:], rhs=b_raw[c][:, 2 * u : 2 * u + 2, cols], start=True, stop=True)

        def empty_b(c, half):
            words = b_grouped[c][:].rearrange("p n t -> p (n t)").bitcast(F32)[:, N * half : N * half + N]
            nc.scalar.copy(out=words, in_=flat(full_bank(("b", c, half))))

        def quantise_b(c):
            nc.vector.quantize_mx(out=b_codes[:, c, :].bitcast(FP8X4), scales=b_exps[:, c, :],
                                  in_=b_grouped[c][:].rearrange("p n t -> p (n t)"))

        def x_block(i, blk):
            if i == 0:
                h, b = divmod(blk, NB // 2)
                return x0_raw[h][:, G * b : G * b + G], x0_scales[:, blk : blk + 1]
            col = NB * (i - 1) + blk
            return x_raw[i][:, G * blk : G * blk + G], x_scales[:, col : col + 1]

        def widen_x_plain(i, c, on_scalar):
            for blk in range(PASS_BLOCKS * c, PASS_BLOCKS * c + PASS_BLOCKS):
                raw, scale = x_block(i, blk)
                widen_plain(plain[i][:, G * blk : G * blk + G], raw, scale, on_scalar)

        def widen_x_scalar(i):
            for c in range(PLAIN_PASSES):
                widen_x_plain(i, c, True)

        def x_runs(i):
            if ("x_runs", i) not in held:
                held["x_runs", i] = work.tile([P, K - PLAIN_PASSES * PASS], BF16, name="x_runs", align_bytes=64)
            return held["x_runs", i][:]

        def widen_x_runs(i, c):
            for blk in range(PASS_BLOCKS * c, PASS_BLOCKS * c + PASS_BLOCKS):
                raw, scale = x_block(i, blk)
                widen_runs(x_runs(i), raw, scale, blk - PASS_BLOCKS * PLAIN_PASSES)

        def widen_x_runs_scalar(i, c):
            lying = work.tile([P, PASS], BF16, bufs=1, align_bytes=64)
            for q in range(PASS_BLOCKS):
                raw, scale = x_block(i, PASS_BLOCKS * c + q)
                widen_plain(lying[:, G * q : G * q + G], raw, scale, True)
            runs = x_runs(i)[:, PASS * (c - PLAIN_PASSES) : PASS * (c - PLAIN_PASSES + 1)]
            nc.scalar.copy(out=runs.rearrange("r (u h m) -> r u h m", u=2, m=8), in_=lying[:].rearrange("r (h u m) -> r u h m", u=2, m=8))

        def widen_x_vector(i):
            for c in range(PLAIN_PASSES, KP):
                widen_x_runs(i, c)

        def sort_words(i, first, end, name):
            ordered = work.tile([P, end - first, 2, P], F32, name=name, bufs=1, align_bytes=64)
            words = plain[i][:].bitcast(F32)[:, 2 * P * first : 2 * P * end]
            nc.gpsimd.tensor_copy(out=ordered[:], in_=words.rearrange("r (c p u) -> r c u p", u=2, p=P))
            for c in range(first, end):
                held["sorted", i, c] = ordered[:, c - first]

        def sort_tile(i):
            sort_words(i, SORT_FIRST, PLAIN_PASSES + (DP if i + 1 < NT else 0), f"c_grouped{(i - 2) % C_BUFS}")

        def sort_scalar(i, passes=range(SORT_FIRST)):
            for c in passes:
                ordered = work.tile([P, 2, P], F32, name="sorted_scalar", bufs=4, align_bytes=64)
                words = plain[i][:].bitcast(F32)[:, 2 * P * c : 2 * P * c + 2 * P]
                nc.scalar.copy(out=ordered[:], in_=words.rearrange("r (p u) -> r u p", u=2))
                held["sorted", i, c] = ordered[:]

        def sort_q(i, name):
            sort_words(i, PLAIN_PASSES, PLAIN_PASSES + DP, name)

        def sort_x(i, name):
            sort_words(i, 0, PLAIN_PASSES, name)

        def plain_words(i, c, u):
            if ("sorted", i, c) in held:
                return held["sorted", i, c][:, u, :]
            return stepped(plain[i][:].bitcast(F32), c, u)

        def q_words(i, c, u):
            if ("sorted", i - 1, PLAIN_PASSES + c) in held:
                return held["sorted", i - 1, PLAIN_PASSES + c][:, u, :]
            return stepped(q_raw[i].bitcast(F32), c, u)

        def turn_x(i, half):
            if half == 0:
                return turn(("x", i, 0), lambda c, u: plain_words(i, c, u))
            return turn(("x", i, 1), lambda c, u: x_runs(i).bitcast(F32)[:, P * (2 * c + u) : P * (2 * c + u + 1)], order=(1, 0) if i else (0, 1))

        def turn_c(i):
            return turn(("c", i), lambda c, u: q_words(i, c, u), u_first=True)

        def empty_x(i, half):
            if ("x_grouped", i) not in held:
                held["x_grouped", i] = work.tile([P, KP, P, 4], BF16, name=f"turned{i % 2}", bufs=1, align_bytes=64)
            empty(("x", i, half), as_words(held["x_grouped", i][:])[:, 2 * half : 2 * half + 2])

        def add_v(i):
            c_grouped = work.tile([P, DP, P, 4], BF16, name=f"c_grouped{i % C_BUFS}", bufs=1, align_bytes=64)
            held["c_grouped", i] = c_grouped
            pairs = "p c r (u e) -> p (c r) u e"
            nc.vector.tensor_tensor(out=c_grouped[:].rearrange(pairs, e=2),
                                    in0=flat(full_bank(("c", i))).bitcast(BF16).rearrange("p (u x e) -> p x u e", u=2, e=2),
                                    in1=v_turned[:].rearrange(pairs, e=2), op=ADD)

        def quantise_x(i):
            x_codes = work.tile([P, KP, P], U32, bufs=TURNED_BUFS, align_bytes=MX_ALIGN)
            x_exps = work.tile([P, KP, P], U8, bufs=TURNED_BUFS, align_bytes=MX_ALIGN)
            nc.vector.quantize_mx(out=x_codes[:].rearrange("p c r -> p (c r)").bitcast(FP8X4),
                                  scales=x_exps[PLANE:].rearrange("p c r -> p (c r)"),
                                  in_=held.pop(("x_grouped", i))[:].rearrange("p c r t -> p (c r t)"))
            held["x_mx", i] = (x_codes, x_exps, b_codes, b_exps)

        def quantise_x_half(i, half):
            if ("x_mx", i) not in held:
                x_codes = work.tile([P, KP, P], U32, bufs=TURNED_BUFS, align_bytes=MX_ALIGN)
                x_exps = work.tile([P, KP, P], U8, bufs=TURNED_BUFS, align_bytes=MX_ALIGN)
                held["x_mx", i] = (x_codes, x_exps, b_codes, b_exps)
            x_codes, x_exps = held["x_mx", i][:2]
            two = slice(2 * half, 2 * half + 2)
            nc.vector.quantize_mx(out=x_codes[:, two].rearrange("p c r -> p (c r)").bitcast(FP8X4),
                                  scales=x_exps[PLANE:, two].rearrange("p c r -> p (c r)"),
                                  in_=held["x_grouped", i][:, two].rearrange("p c r t -> p (c r t)"))

        def quantise_c(i):
            c_codes = work.tile([P, DP, P], U32, bufs=TURNED_BUFS, align_bytes=MX_ALIGN)
            c_exps = work.tile([P, DP, P], U8, bufs=TURNED_BUFS, align_bytes=MX_ALIGN)
            nc.vector.quantize_mx(out=c_codes[:].rearrange("p c r -> p (c r)").bitcast(FP8X4),
                                  scales=c_exps[PLANE:].rearrange("p c r -> p (c r)"),
                                  in_=held.pop(("c_grouped", i))[:].rearrange("p c r t -> p (c r t)"))
            held["c_mx", i] = (c_codes, c_exps, r_codes, r_exps)

        def one_pass(total, operands, c, cols, number):
            codes, exps, other_codes, other_exps = operands
            nc.tensor.matmul_mx(out=total, lhsT=codes[:, c, :].bitcast(FP8X4), lhsT_scale=exps[PLANE:, c, :],
                                rhs=other_codes[:, c, cols].bitcast(FP8X4), rhs_scale=other_exps[:, c, cols],
                                start=(number == 0), stop=(number == KP + DP - 1))

        added = [0] * NT

        def multiply(i, product, passes):
            for c in passes:
                if added[i] == 0:
                    new_bank(("sum", i))
                one_pass(flat(held["sum", i][0]), held[product, i], c, slice(0, N), added[i])
                added[i] = added[i] + 1

        def multiply_c(i):
            multiply(i, "c_mx", range(DP))

        def multiply_x(i, first, end):
            multiply(i, "x_mx", range(first, end))

        def scale_and_store(result, total, i, cols):
            nc.vector.scalar_tensor_tensor(out=result[:], in0=total, scalar=1.0 / D, in1=g_all[:, cols], op0=MULT, op1=MULT)
            nc.sync.dma_start(out=out_tiles[:, i, cols], in_=result[:])

        def finish(i):
            result = work.tile([P, N], F32, bufs=RESULT_BUFS, align_bytes=64)
            scale_and_store(result, flat(full_bank(("sum", i))), i, slice(0, N))

        def turn_tile(i):
            run(turn_c(i) + turn_x(i, 1) + turn_x(i, 0))

        def empty_tile(i):
            empty_x(i, 1)
            empty_x(i, 0)

        def multiply_tile(i):
            multiply_c(i)
            multiply_x(i, 0, KP)

        spread_r_scales()
        widen_x_vector(0)
        widen_x_scalar(0)
        run(turn_x(0, 1))
        widen_r(0)
        widen_r(1)
        widen_x_vector(1)
        widen_r(2)
        widen_r(3)
        group_b(0, N // 2)
        run(turn_r(0))
        run(turn_x(0, 0))
        empty_x(0, 1)
        widen_x_scalar(1)
        run(turn_r(1))
        run(turn_x(1, 1))
        empty_x(0, 0)
        turn_v()
        weave_b(0, 1)
        run(turn_r(2))
        run(turn_c(0))
        empty_r(0)
        repeat_v()
        empty_b(0, 1)
        empty_r(1)
        quantise_x(0)
        widen_x_vector(2)
        group_b(1, N // 2)
        add_v(0)
        quantise_b(0)
        run(turn_r(3))
        weave_b(1, 1)
        run(turn_x(1, 0))
        empty_r(2)
        empty_r(3)
        widen_x_scalar(2)
        empty_x(1, 1)
        empty_x(1, 0)
        run(turn_x(2, 1))
        run(turn_c(1))
        group_b(2, N)
        quantise_c(0)
        quantise_r(0)
        add_v(1)
        empty_b(1, 1)
        empty_x(2, 1)
        weave_b(3, 0)
        run(turn_x(2, 0))
        run(turn_c(2))
        quantise_r(1)
        widen_x_vector(3)
        quantise_x(1)
        quantise_b(1)
        empty_b(3, 0)
        widen_x_scalar(3)
        spread_g()
        run(turn_c(3))
        multiply_x(0, 0, 1)
        multiply_c(0)
        run(turn_x(3, 1))
        run(turn_x(3, 0))
        group_b_scalar(3, 1)
        empty_g()
        empty_x(2, 0)
        quantise_b(2)
        quantise_c(1)
        add_v(2)
        quantise_b(3)
        multiply_x(1, 0, 1)
        multiply_x(0, 1, 3)
        multiply_x(1, 1, 3)
        multiply_c(1)
        multiply_x(0, 3, 4)
        multiply_x(1, 3, 4)
        widen_x_plain(4, 1, True)
        widen_x_plain(4, 0, True)
        sort_scalar(3, range(PLAIN_PASSES, PLAIN_PASSES + DP))
        sort_scalar(4)
        empty_tile(3)
        widen_x_plain(5, 1, True)
        widen_x_plain(5, 0, True)
        widen_x_vector(4)
        quantise_c(2)
        sort_tile(4)
        quantise_x(2)
        multiply_tile(2)
        add_v(3)
        finish(0)
        for s in range(4, NT):
            turn_tile(s)
            empty_x(s, 1)
            if s + 1 < NT:
                sort_scalar(s + 1)
            empty_x(s, 0)
            if s + 2 < NT:
                widen_x_plain(s + 2, 1, True)
                widen_x_plain(s + 2, 0, True)
            if s + 1 < NT:
                widen_x_vector(s + 1)
            quantise_c(s - 1)
            if s + 1 < NT:
                sort_tile(s + 1)
            quantise_x(s - 1)
            multiply_tile(s - 1)
            add_v(s)
            finish(s - 3)
        last = NT - 1
        quantise_c(last)
        quantise_x_half(last, 1)
        quantise_x_half(last, 0)
        finish(last - 2)

        passes = [("c_mx", c) for c in range(DP)] + [("x_mx", c) for c in reversed(range(KP))]
        totals = []
        for lo, hi in LAST_PIECES:
            total = flat(new_bank(("piece", lo)))[:, 0 : hi - lo]
            totals.append(total)
            for number, (product, c) in enumerate(passes):
                one_pass(total, held[product, last], c, slice(lo, hi), number)
        finish(last - 1)
        for (lo, hi), total in zip(LAST_PIECES, totals):
            piece = work.tile([P, hi - lo], F32, align_bytes=64)
            scale_and_store(piece, total, last, slice(lo, hi))
